import numpy as np, ml_dtypes
CORES = [40,41,42,43,44,45,46,47]
N = 8
BF = ml_dtypes.bfloat16
T0, L, M, RO, KILL, HOPS, TILE = 1536, 512, 3, 3, 200, [1, 3], [0, 1, 1]
NS, GB, W = L * M, T0 + L * RO, T0 + L * (2 * RO - 1)
LAST = NS - M + max(TILE)
R4 = np.arange(N).reshape(N, 1, 1, 1); G4 = np.arange(8).reshape(1, 8, 1, 1); R3 = R4[..., 0]; G3 = G4[..., 0]
def members(rng, of, cl, k):
    tab = np.argsort(of, axis=-1, kind="stable").reshape(N, 8, 32, -1)
    return tab[R4, G4, cl[:, :, None, :], rng.integers(0, tab.shape[3], (N, 8, k, cl.shape[2]))]
def around(rng, cen, cl):
    n = cl.shape[2]; w = rng.choice(np.array([2, 6, 10]), (N, 8, n, 1))
    p = cen[R3, G3, cl] + np.rint(w * (2 * rng.random((N, 8, n, 16)) - 1)).astype(np.int64)
    return np.ascontiguousarray(np.clip(p, 0, 63).transpose(0, 1, 3, 2))
def parts(rng):
    cen = np.where(rng.random((N, 8, 32, 1)) < 0.7, rng.integers(0, 64, (1, 8, 32, 16)), rng.integers(0, 64, (N, 8, 32, 16)))
    cv = np.argsort(rng.random((N, 8, T0)), axis=-1) % 32; cz = np.argsort(rng.random((N, 8, NS)), axis=-1) % 32
    two = rng.permutation(8)[:2]; cz[:, two] = np.repeat(np.argsort(rng.random((2, L)), axis=-1) % 32, M, axis=1)
    V = around(rng, cen, cv); Z = around(rng, cen, cz)
    stray = rng.choice(np.array([0.0, 0.1, 0.1, 0.5, 0.5]), (N, 8, 1, NS))
    S = np.where(rng.random((N, 8, 16, NS)) < stray, rng.integers(0, T0, (N, 8, 16, NS)), members(rng, cv, cz, 16))
    Q = np.where(rng.random((N, 8, 16, T0)) < 0.4, rng.integers(0, NS, (N, 8, 16, T0)), members(rng, cz, cv, 16))
    Q[R4, G4, np.arange(5).reshape(1, 1, 5, 1), S[:, :, :5]] = np.arange(NS)
    u = rng.random((N, 8, T0))
    kid = np.where(u < 0.15, np.arange(T0), np.where(u < 0.4, rng.integers(0, T0, (N, 8, T0)), members(rng, cv, cv, 1)[:, :, 0]))
    u = rng.random((N, 8, NS)); best = np.take_along_axis(S, rng.integers(0, 16, (N, 8, 1, NS)), 2)[:, :, 0]
    best = np.where(u < 0.07, -1, np.where(u < 0.2, rng.integers(0, T0, (N, 8, NS)), best))
    return V, Z, S, Q, kid, best
def pack(V, Z, S, Q, kid, best):
    def p(x): return np.ascontiguousarray(x).reshape(N, 128, -1)
    return {"vn": p(V).astype(np.float32).astype(BF), "zs": p(Z).astype(np.float32).astype(BF), "sn": p(S).astype(np.int32), "nq": p(Q).astype(np.int32),
            "kid": np.ascontiguousarray(kid).astype(np.int32), "bst": np.ascontiguousarray(best).astype(np.int32)}
def setup_inputs(rng):
    return pack(*parts(rng))
def setup_inputs_spread(rng):
    def pts(n):
        x = np.minimum((np.exp2(6 * rng.random((N, 8, 1, n))) * rng.random((N, 8, 16, n))).astype(np.int64), 63)
        return np.where(rng.random((N, 8, 1, n)) < 0.5, x, 63 - x)
    def lst(n, k, hi):
        return np.minimum((hi * rng.random((N, 8, k, n)) ** rng.choice(np.array([1.0, 2.0, 6.0]), (N, 8, 1, n))).astype(np.int64), hi - 1)
    return pack(pts(T0), pts(NS), lst(NS, 16, T0), lst(T0, 16, NS), lst(T0, 1, T0)[:, :, 0], lst(NS, 1, T0 + 1)[:, :, 0] - 1)
def edge(rng, shape, lo, hi, by):
    m = rng.choice(np.array([0.0, 0.5, 0.5, 1.0]), shape[:-2] + (1, shape[-1]))
    return np.where(rng.random(by) < 0.2, rng.integers(lo, hi + 1, shape), np.where(rng.random(shape) < m, hi, lo))
def setup_inputs_ends(rng):
    V = edge(rng, (N, 8, 16, T0), 0, 63, (N, 8, 1, T0)); Z = edge(rng, (N, 8, 16, NS), 0, 63, (N, 8, 1, NS))
    S = edge(rng, (N, 8, 16, NS), 0, T0 - 1, (N, 8, 16, NS)); Q = edge(rng, (N, 8, 16, T0), 0, NS - 1, (N, 8, 16, T0))
    kid = edge(rng, (N, 8, 1, T0), 0, T0 - 1, (N, 8, 1, T0))[:, :, 0]; best = edge(rng, (N, 8, 1, NS), -1, T0 - 1, (N, 8, 1, NS))[:, :, 0]
    for q in range(N):
        for g in range(8):
            hi = 63 if g % 2 == 0 else 0; own = (g // 2) % 2 == 1
            V[q, g, :, 0] = 63 - hi; V[q, g, :, [3, 8, T0 - 1]] = hi
            kid[q, g, 0] = 0 if own else T0 - 1; kid[q, g, T0 - 1] = T0 - 1 if own else 0; kid[q, g, 3] = 3; kid[q, g, 8] = 8
            Z[q, g, :, LAST] = hi; S[q, g, :, LAST] = 0; S[q, g, 4, LAST] = 3; S[q, g, 9, LAST] = 8; S[q, g, 15, LAST] = T0 - 1
            Z[q, g, :, LAST - 1] = 63 - hi; S[q, g, :, LAST - 1] = T0 - 1; Z[q, g, :, 0] = hi; S[q, g, :, 0] = 0
            Q[q, g, :, 3] = LAST; Q[q, g, :, T0 - 1] = LAST - 1
    return pack(V, Z, S, Q, kid, best)
def setup_inputs_corners(rng):
    V, Z, S, Q, kid, best = parts(rng); sh = int(rng.integers(0, 8))
    for q in range(N):
        for g in range(8):
            c = (g + q + sh) % 8
            if c == 0:
                kid[q, g] = np.arange(T0); best[q, g] = -1
            elif c == 1:
                kid[q, g] = 0; best[q, g] = 0; S[q, g, :, ::3] = 0
            elif c == 2:
                kid[q, g] = T0 - 1; best[q, g] = T0 - 1; S[q, g, :, 1::3] = T0 - 1
            elif c == 3:
                kid[q, g] = (np.arange(T0) + 1) % T0
            elif c == 4:
                o = rng.permutation(T0)[:6]; kid[q, g, o] = o; Z[q, g] = 0
                for j in range(6):
                    s = KILL - 1 + j // 2; x = np.full(16, s // 16); x[rng.permutation(16)[:s % 16]] += 1; V[q, g, :, o[j]] = x
                typ = rng.integers(0, 5, NS); s = o[rng.integers(0, 2, (16, NS))]
                s = np.where((np.arange(16)[:, None] == rng.integers(0, 16, NS)) & (typ == 1), o[2], s); s = np.where(typ == 2, o[3], s)
                s = np.where(typ == 3, o[rng.integers(0, 6, (16, NS))], s); S[q, g] = np.where(typ == 4, S[q, g], s)
            elif c == 5:
                S[q, g] = np.arange(NS); Q[q, g] = np.arange(T0) % NS; kid[q, g, ::2] = np.arange(0, T0, 2)
            elif c == 6:
                V[q, g] = rng.choice(np.array([0, 1, 62, 63]), (16, T0)); Z[q, g] = rng.choice(np.array([0, 63]), (16, NS))
                S[q, g, :, ::2] = rng.choice(np.array([0, T0 - 1]), (16, (NS + 1) // 2))
                o = rng.permutation(T0)[:10]; kid[q, g, o] = o; kid[q, g, o[8]] = o[7]; flip = (q + g) % 2 == 1
                for j in range(10):
                    x = 63 - (rng.permutation(16) < 8 - j); V[q, g, :, o[j]] = 63 - x if flip else x
                far = (np.arange(NS) // M) % 2 == 1; least = (np.arange(NS) // (2 * M)) % 10
                Z[q, g] = np.where(far, 63 if flip else 0, Z[q, g]); S[q, g] = np.where(far, o[rng.integers(least, 10, (16, NS))], S[q, g])
            else:
                Q[q, g] = rng.choice(np.array([0, NS - 1]), (16, T0)); best[q, g] = rng.choice(np.array([-1, 0, T0 - 1]), NS)
    return pack(V, Z, S, Q, kid, best)
def setup_inputs_crowd(rng):
    V, Z, S, Q, kid, best = parts(rng); sh = int(rng.integers(0, 8)); e = NS - M
    for q in range(N):
        for g in range(8):
            c = (g + sh) % 8; p = T0 - 1 if (q + g) % 2 else int(rng.integers(1, T0 - 1)); o = (p + 1) % T0
            kid[q, g, p] = p; kid[q, g, o] = o; V[q, g, :, p] = 0
            if c in (0, 1, 5):
                Z[q, g] = np.maximum(Z[q, g], 20); S[q, g] = p
            if c == 1: S[q, g, :, e:] = o
            if c in (2, 3):
                Z[q, g] = rng.integers(0, 4, (16, NS)); S[q, g] = p
            if c == 2: Z[q, g, :, e:] = 63
            if c == 4: S[q, g] = rng.choice(np.array([p, o, (p + 2) % T0]), (16, NS))
            if c == 5:
                Q[q, g, :, p] = NS - 1; best[q, g, NS - 1] = p
            if c >= 6:
                V[q, g, :, p] = 31; S[q, g] = p
                Z[q, g] = np.where(rng.random((1, NS)) < 0.5, rng.integers(50, 64, (16, NS)), rng.integers(0, 13, (16, NS))); Z[q, g, :, NS - 1] = 63; Z[q, g, :, 0] = 0
                best[q, g, 0] = p; best[q, g, NS - 1] = p; Q[q, g, :, p] = NS - 1; Q[q, g, (15 if c == 6 else 8):, p] = 0
            if c == 7:
                Z[q, g, :, 1] = 31
                if q % 4 == 3: Q[q, g, 0, p] = 1
                else: Q[q, g, 16 - q % 4:, p] = 1
    return pack(V, Z, S, Q, kid, best)
def setup_inputs_ties(rng):
    V, Z, S, Q, kid, best = parts(rng)
    pts = rng.integers(0, 64, (8, 48, 16)); pts[1::2] = 20 + 25 * (pts[1::2] % 2)
    few = rng.choice(np.array([3, 6, 16, 48]), (N, 8, 1))
    V = pts[G3, rng.integers(0, 48, (N, 8, T0)) % few].transpose(0, 1, 3, 2); Z = pts[G3, rng.integers(0, 48, (N, 8, NS))].transpose(0, 1, 3, 2)
    return pack(V, Z, S, Q, kid, best)
def check_inputs(d):
    bad = []
    for k, lo, hi in (("vn", 0, 63), ("zs", 0, 63), ("sn", 0, T0 - 1), ("nq", 0, NS - 1), ("kid", 0, T0 - 1), ("bst", -1, T0 - 1)):
        x = np.asarray(d[k]).astype(np.float64)
        if not (np.min(x) >= lo and np.max(x) <= hi and np.all(x == np.floor(x))): bad.append("range of " + k)
    return bad
def columns(x):
    return np.ascontiguousarray(x.astype(np.float32).astype(np.int32).reshape(N, 8, 16, -1).transpose(0, 1, 3, 2))
def rows(x):
    return np.ascontiguousarray(x.transpose(0, 1, 3, 2)).reshape(N, 128, -1)
def dist(a, b):
    return np.add.reduce(np.abs(a - b), axis=-1)
def reference(vn, zs, sn, nq, kid, bst):
    V = np.zeros((N, 8, W, 16), np.int32); V[:, :, :T0] = columns(vn); Z = columns(zs); S = columns(sn)
    Q = np.zeros((N, 8, W, 16), np.int32); Q[:, :, :T0] = columns(nq)
    child = np.tile(np.arange(W), (N, 8, 1)); child[:, :, :T0] = kid
    best = bst.astype(np.int64); lane = np.arange(L)
    for t in range(RO):
        v = M * lane + TILE[t]; z = Z[:, :, v]; z1 = z[:, :, :, None, :]; s = S[:, :, v].astype(np.int64)
        e = child[R4, G4, s]
        ds = dist(V[R4, G4, s], z1); de = dist(V[R4, G4, e], z1)
        s = np.where(de < ds, e, s); d = np.minimum(ds, de)
        if t > 0:
            m = GB + L * (t - 1) + lane; dm = dist(V[:, :, m], z)
            put = (np.arange(16) == np.argmax(d, axis=3)[..., None]) & (dm < np.max(d, axis=3))[..., None]
            s = np.where(put, m[:, None], s); d = np.where(put, dm[..., None], d)
        S[:, :, v] = s
        b = np.argmin(d, axis=3); a = np.take_along_axis(s, b[..., None], 3)[..., 0]
        live = np.max(d, axis=3) >= KILL
        best[:, :, v] = np.where(live, a, -1)
        va = V[R3, G3, a]; va1 = va[:, :, :, None, :]; qa = Q[R3, G3, a]
        bq = best[R4, G4, qa]; zq = Z[R4, G4, qa]
        att = (bq >= 0) & ((bq == a[..., None]) | (dist(V[R4, G4, np.maximum(bq, 0)], va1) >= dist(zq, va1)))
        pull = np.add.reduce(np.where(att[..., None], np.clip(zq - va1, -1, 1), 0), axis=3)
        new = np.clip(va + np.clip(pull, -2, 2), 0, 63); n = T0 + L * t + lane
        V[:, :, n] = new
        low = np.full((N, 8, W), L); np.minimum.at(low, (R3, G3, a), np.where(live, lane, L))
        child = np.where(low < L, T0 + L * t + low, child)
        if t < RO - 1:
            Q[:, :, n] = qa; m = GB + L * t + lane
            V[:, :, m] = np.roll(new, HOPS[t], axis=0); Q[:, :, m] = np.roll(qa, HOPS[t], axis=0)
    h = NS // 2
    return {"yv": rows(V[:, :, T0:GB]).astype(np.float32).astype(BF), "ys": rows(S[:, :, :h] + 4096 * S[:, :, h:]).astype(np.float32), "yk": child.astype(np.float32), "yb": best.astype(np.float32)}

@@ -1,0 +1,838 @@
+from concourse.mybir import dt, AluOpType, AxisListType, ActivationFunctionType
+
+A = AluOpType
+F = ActivationFunctionType
+BF, F32, I32, U16 = "bfloat16", "float32", "int32", "uint16"
+HOPS, TILE = [1, 3], [0, 1, 1]
+K14 = 16384.0
+FAR = 1009.0
+
+SCRATCH = {}
+
+
+def _sb(name, shape, dtype):
+    SCRATCH[name] = ("sbuf", [128] + list(shape), dtype)
+
+
+for _n, _w, _d in [("Vb", 4112, BF), ("IO", 4112, F32), ("CH", 4112, F32), ("Qt", 4096, F32), ("VB", 1536, F32),
+                   ("Bt", 1536, F32), ("Zb", 1536, BF), ("sni", 1536, I32), ("nqi", 768, I32), ("SC", 512, F32),
+                   ("YS", 768, F32), ("Wb", 2048, BF), ("Wt", 2048, BF), ("XS", 4096, BF),
+                   ("xi", 160, F32), ("xl", 16, F32), ("U", 144, BF), ("Ua", 144, BF), ("U2", 144, BF), ("Un", 144, BF),
+                   ("IW0", 160, F32), ("IW1", 160, F32), ("idb", 128, BF), ("nid", 128, BF), ("idf", 128, F32),
+                   ("SL", 144, F32), ("ci", 8, I32), ("cf", 16, F32),
+                   ("OB", 16, U16), ("OE", 16, U16), ("OP", 16, U16), ("OL", 16, U16), ("gid", 64, F32),
+                   ("kidc", 96, I32), ("bsc", 96, I32), ("iu", 64, U16), ("it2", 512, F32),
+                   ("qn0", 512, F32), ("qn1", 512, F32), ("GQ0", 512, F32), ("GQ1", 512, F32), ("GV0", 512, BF), ("GV1", 512, BF),
+                   ("zr", 4096, BF)]:
+    _sb(_n, [_w], _d)
+_sb("pY", [8, 2, 16], F32)
+for _c in "ab":
+    for _n, _s, _d in [("XE", [4096], BF), ("XZ", [4096], BF), ("XA", [4096], BF),
+                       ("sg", [256, 16], BF), ("f1", [256], F32), ("f2", [256], F32), ("Ks", [256], F32),
+                       ("ef", [256], F32), ("sf", [256], F32), ("su", [512], U16), ("eu", [256], U16), ("qu", [256], U16),
+                       ("M", [256], I32), ("M2", [256], I32), ("Mc", [16, 16], I32), ("A1", [16, 16], F32), ("L1", [8, 16], F32),
+                       ("L2", [4, 16], I32), ("L3", [8, 16], F32), ("tr", [256], F32), ("ti", [32], I32), ("tf", [128], F32),
+                       ("au", [64], U16), ("va", [1024], BF), ("vf", [1024], F32), ("t1", [256], F32),
+                       ("lo", [512], BF), ("nt", [768], BF)]:
+        _sb(_n + _c, _s, _d)
+for _n in ["PXa", "PXb", "PE0", "PE1", "PM", "PK"]:
+    SCRATCH[_n] = ("psum", [128, 512], F32)
+for _n in ["PYa", "PYb"]:
+    SCRATCH[_n] = ("psum", [128, 16, 2, 16], F32)
+
+NDMA = 40
+SEMAPHORES = ["v", "a", "p", "g", "sent"] + ["d%d" % _i for _i in range(NDMA)] + ["arr%d" % _i for _i in range(4)]
+
+COST = {"cyc": 1.0, "gat": 1.56, "sca": 3.8, "pe": 0.55, "lat": 90.0, "dma": 2000.0, "alt": 500.0, "turns": 1}
+KS = [(0, 8), (8, 12), (12, 16)]
+BIAS = {'z2ba':-2,'z2bp':-2,'z2bv':-1,'i1ba':10,'i1bp':10,'i1bv':10,'k4096aa':-1,'k4096ap':19,'k4096av':-1,'i0aa':10,'i0ap':10,'i0av':10,'b0aa':-1,'b0av':9,'q2ba':-1,'k1536ap':-20,'e2bv':-5,'o0v':5,'b1aa':1,'b1av':1,'g1aa':1,'q1aa':20,'q1ap':20,'q1av':20,'l2ba':-1,'l2bp':-1,'x1v':20,'c1aa':10,'c1ap':10,'c1av':10,'h1aa':4,'e2ba':-1,'i0ba':1,'i0bp':1,'i0bv':1,'z1ba':-1,'z1bp':-1,'z1bv':-1,'l1ba':1,'loadv':-1,'h1ap':10,'h1av':5,'d2ap':10,'d2av':10,'e1aa':1,'e1ap':1,'d1ap':2,'d1av':3,'b0ba':-5,'c0aa':1,'c0ap':1,'c0av':1,'h2aa':5,'h2ap':5,'h2as':5,'h2av':5,'e2aa':20,'b2ba':-1,'b2bv':-1,'c1ba':5,'c1bp':5,'c1bv':5,'i1ap':5,'d0av':-2,'q1bv':-2,'s0bv':-20,'d1bv':5,'h0aa':9,'x0g':-1,'x0s':-1,'x0v':-1,'e2av':1,'l0ap':5,'h0ap':10,'h0av':10,'k2048aa':-5,'q0bv':1,'s1ba':-2,'s1bp':-2,'s1bv':-2,'h0ba':2,'h0bg':2,'h0bp':2,'h0bs':2,'h0bv':2}
+WIDE = {}
+KS4 = [(0, 8), (8, 12), (12, 16)]
+ONACT = {"s0a": [], "s0b": [], "s1a": [], "s1b": [], "e0a": [], "e0b": [], "e1a": [], "e1b": [], "e2a": [], "e2b": [],
+         "z0a": [], "z0b": [], "z1a": [], "z1b": [], "z2a": [], "z2b": [],
+         "E0a": [], "E0b": [], "E1a": [], "E1b": [], "E2a": [], "E2b": [],
+         "Z0a": [], "Z0b": [], "Z1a": [], "Z1b": [], "Z2a": [], "Z2b": []}
+ONACT.update({'s0a':[1],'s0b':[2],'s1a':[2,4,5],'s1b':[0,2,4,6],'e0b':[0],'e1a':[4,5],'e1b':[5,7],'e2a':[0,1,6],'e2b':[0],'z0a':[0,3],'z1a':[1],'z1b':[2],'z2a':[1],'z2b':[0]})
+BIAS = {'c1av':32,'c2av':8,'q1av':-12,'q2av':2,'q1aa':5,'q2aa':2,'x0v':22,'d1bv':22,'d0av':5,'d0bv':10,'loada':10,'loadg':13,'loads':18,'loadv':10,'q1ap':-20,'g1ba':83,'g1bp':95,'q2ba':22,'q2bp':22,'q2bv':22,'x1g':-5,'x1s':10,'q2ap':-13,'s1ap':-2,'s0ba':20,'s0bp':10,'s0bv':10,'q1bv':-2,'z2bv':8,'x0g':-8,'s0ap':-5,'e2aa':2,'e2ap':2,'e2av':-14,'i0aa':17,'i0ag':9,'i0ap':-9,'i0av':3,'i1ba':-20,'z0bv':-3,'h1ba':3,'h1bg':-2,'h1bp':3,'h1bs':3,'h1bv':3,'s1aa':11,'s1av':30,'d1bp':9,'e1ap':1,'h0av':54,'g2bp':-25,'z2ba':3,'z2bp':-12,'h2bp':34,'o0p':52,'e1bp':42,'l2aa':2,'c1bv':42,'e1aa':-1,'c0ba':2,'c0bp':-5,'d1ap':-30,'h1aa':19,'b2av':9,'l1bg':1,'i1bg':10,'z0ba':-5,'z0bp':-33,'l2ba':-11,'l2bg':-6,'l2bp':-6,'g2aa':2,'g2ap':8,'i1bv':-12,'h2ba':67,'h2bs':42,'h2bv':24,'q0ba':-11,'b1bv':45,'z1aa':-5,'z1ap':-7,'z1av':15,'x2g':-12,'x2s':-2,'x2v':-17,'c2ba':-52,'e0bv':10,'s1bv':10,'x0s':-3,'q0aa':1,'q0ap':1,'z1ba':13,'d2ap':20,'i0ba':9,'i0bg':-3,'i0bp':-2,'i0bv':4,'e2bp':-10,'d0ap':-5,'o1a':33,'c2bp':-12,'c2bv':-35,'k2048ba':9,'k2048bp':-3,'k2048bv':-11,'c0av':17,'e0ap':-21,'z1bp':-4,'z1bv':-14,'g1ap':17,'k1536aa':-5,'k1536ap':-5,'k1536av':5,'z2ap':5,'k1536ba':-1,'k1536bv':-2,'c1aa':20,'c1ap':22,'h2av':35,'q0bp':-11,'q0bv':-1,'o0a':20,'o0v':24,'e0aa':-1,'e0av':-1,'i1aa':-5,'i1ag':-2,'h0bv':21,'h2aa':38,'h2ap':65,'h2as':38,'l1ba':-2,'l1bp':-2,'l0ag':-5,'c1ba':32,'o1v':63,'o1s':18,'k4096aa':-2,'c1bp':22,'b0ba':-14,'h0ba':51,'c0aa':-2,'c0ap':5,'q1bp':-3,'h0aa':-3,'h0ap':-6,'k4096ba':-1,'e2bv':5,'k4096bp':-1,'k4096bv':-1,'h0bs':16,'h0bg':-4,'h0bp':-4,'constg':2,'k2048aa':30,'k2048ap':10,'k2048av':12,'h1ap':23,'s0av':9,'s0aa':-1,'h1av':40,'o1p':40,'g2ba':-20,'b2ba':20,'consta':-1,'d2bp':-12,'b1aa':20,'l0aa':-1,'e0bp':-10}
+
+WIDE = {'e2b':[0,2],'b2a':[1,2]}
+ONACT.update({'s0a':[2],'s0b':[2],'s1a':[0,2,5],'s1b':[0,2,4,6],'e0b':[0],'e1a':[4,5],'e1b':[5,7],'e2a':[0,1,6],'e2b':[0],'z0a':[0,3],'z1a':[1],'z1b':[2],'z2a':[1],'z2b':[0]})
+BIAS = {'c1av':17,'c2av':-21,'q1av':-2,'q2av':6,'q1aa':5,'q2aa':6,'x0v':24,'d1bv':-5,'d0bv':19,'loada':14,'loadg':17,'loads':22,'loadv':14,'q1ap':-20,'g1ba':98,'g1bp':115,'q2ba':18,'q2bp':15,'q2bv':16,'x1g':5,'x1s':2,'q2ap':-31,'s1ap':3,'s0ba':20,'s0bp':20,'s0bv':15,'q1bv':-2,'z2bv':10,'x0g':-6,'s0ap':1,'e2aa':3,'e2ap':-6,'e2av':-12,'i0aa':14,'i0ag':6,'i0av':23,'i1ba':-20,'z0bv':-3,'h1ba':-4,'h1bg':-5,'h1bp':8,'h1bs':-2,'h1bv':-2,'s1aa':14,'s1av':35,'d1bp':4,'e1ap':26,'h0av':54,'g2bp':-7,'z2ba':5,'z2bp':-21,'h2bp':-21,'o0p':31,'e1bp':22,'l2aa':10,'c1bv':60,'e1aa':-2,'c0ba':16,'c0bp':-3,'d1ap':-46,'h1aa':19,'b2av':29,'l1bg':-2,'i1bg':10,'z0ba':-25,'z0bp':-33,'l2ba':7,'l2bg':-20,'l2bp':-10,'g2aa':7,'g2ap':3,'i1bv':-14,'h2ba':-26,'h2bs':-26,'h2bv':-26,'q0ba':-11,'b1bv':45,'z1aa':-5,'z1ap':-7,'z1av':3,'x2v':-10,'c2ba':-43,'e0bv':9,'s1bv':10,'x0s':-1,'q0aa':-6,'z1ba':13,'d2ap':40,'i0ba':9,'i0bp':-2,'i0bv':4,'e2bp':-5,'d0ap':5,'c2bp':-2,'c2bv':-25,'k2048ba':2,'k2048bp':-9,'k2048bv':2,'c0av':20,'e0ap':-19,'z1bv':-14,'g1ap':12,'k1536aa':-4,'k1536ap':-4,'k1536av':-4,'z2ap':26,'k1536ba':-1,'k1536bv':-3,'c1aa':3,'c1ap':27,'h2av':65,'q0bp':-11,'q0bv':-1,'o0a':19,'o0v':23,'e0aa':-1,'e0av':-1,'i1aa':-5,'i1ag':-2,'h0bv':45,'h2aa':63,'h2ap':95,'h2as':88,'l1ba':-7,'l1bp':-7,'l0ag':-5,'c1ba':50,'o1v':20,'k4096aa':-4,'c1bp':40,'b0ba':-19,'h0ba':65,'c0aa':20,'c0ap':20,'q1bp':-4,'h0aa':-3,'h0ap':-6,'k4096ba':-1,'e2bv':4,'k4096bp':-1,'k4096bv':-2,'h0bs':30,'h0bg':32,'h0bp':10,'constg':10,'k2048aa':30,'k2048ap':-2,'k2048av':10,'h1ap':43,'s0av':35,'s0aa':5,'h1av':40,'g2ba':-2,'b2ba':26,'d2bp':-38,'b1aa':10,'l0aa':-1,'e0bp':-13,'x1v':-8,'c2aa':-19,'c2ap':-3,'constp':-2,'i1ap':-2,'b2bv':16,'c0bv':24,'z0aa':4,'z0ap':5,'z0av':7,'e0ba':-1,'d2bv':-11,'z2aa':4,'z2av':3,'l1aa':-1,'b2aa':10,'d2av':-4,'s1ba':-10,'b1ba':-10,'l2ag':10,'l0bg':-1,'k1536bp':-10,'d0bp':-11,'l2ap':8,'q1ba':-5,'k4096ap':-1,'l0ap':10,'l0ba':-1,'l0bp':-1,'i1bp':2}
+if not any(_v for _k, _v in ONACT.items() if _k[0] in "EZ"):
+    SCRATCH.pop("U2")
+    SCRATCH.pop("Un")
+
+
+def ap(name, *idx):
+    return (name, idx)
+
+
+def cols(name, a, b, step=1):
+    return (name, (slice(None), slice(a, b, step)))
+
+
+def ind(win, off):
+    return ("*", win, off)
+
+
+_masks = {}
+
+
+def _mask(x):
+    name, idx = x
+    key = (name, repr(idx))
+    if key not in _masks:
+        shape = SCRATCH[name][1][1:]
+        idx = list(idx[1:]) + [slice(None)] * (len(shape) + 1 - max(len(idx), 1))
+        offs = [0]
+        for d, (n, i) in enumerate(zip(shape, idx)):
+            r = range(n)[i] if isinstance(i, slice) else [i]
+            offs = [o * n + j for o in offs for j in r]
+        m = 0
+        for o in offs:
+            m |= 1 << o
+        _masks[key] = (m, len(offs))
+    return _masks[key]
+
+
+def _size(x):
+    if x[0] == "*":
+        return 16 * _size(x[2])
+    return _mask(x)[1]
+
+
+def _two(x):
+    return SCRATCH[x[1][0] if x[0] == "*" else x[0]][2] in (BF, U16)
+
+
+def _psum(x):
+    return x[0] != "*" and x[0] in SCRATCH and SCRATCH[x[0]][0] == "psum"
+
+
+def build():
+    ops = []
+    tag = ["load"]
+
+    def enumerate(names):
+        return [(1, names[0]), (0, names[1])]
+
+    def add(kind, alts, reads, writes, **kw):
+        rd, wr = [], []
+        for x in reads:
+            if isinstance(x, tuple):
+                rd += [x[1], x[2]] if x[0] == "*" else [x]
+        for x in writes:
+            if x[0] == "*":
+                wr.append(x[1])
+                rd.append(x[2])
+            else:
+                wr.append(x)
+        o = dict(kind=kind, alts=alts, rd=[x for x in rd if x[0] in SCRATCH], wr=[x for x in wr if x[0] in SCRATCH], n=len(ops), tag=tag[0])
+        o.update(kw)
+        ops.append(o)
+        return o
+
+    def vcost(out, ins, tt=False):
+        if out[0] == "*":
+            return ("sca", _size(out))
+        if ins[0][0] == "*":
+            return ("gat", _size(ins[0]))
+        n = _size(out)
+        if tt:
+            return ("cyc", n if (_psum(ins[0]) or _psum(ins[1])) else 2 * n)
+        return ("cyc", n // 2 if all(_two(x) for x in [out] + ins) else n)
+
+    def tt(out, a, b, op):
+        return add("c", {"v": (("tt", out, a, b, op), vcost(out, [a, b], True))}, [a, b], [out])
+
+    def ts(out, a, s1, s2, op0, op1=None):
+        return add("c", {"v": (("ts", out, a, s1, s2, op0, op1), vcost(out, [a]))}, [a, s1, s2], [out])
+
+    def cp(out, a):
+        return add("c", {"v": (("cp", out, a), vcost(out, [a]))}, [a], [out])
+
+    def tp(out, a):
+        return add("c", {"v": (("tp", out, a), vcost(out, [a]))}, [a], [out])
+
+    def ms(out, val):
+        return add("c", {"v": (("ms", out, val), ("cyc", _size(out) // (2 if _two(out) else 1)))}, [], [out])
+
+    def act(out, a, func, bias=0.0, scale=1.0, alt=None):
+        alts = {"a": (("act", out, a, func, bias, scale), ("gat" if a[0] == "*" else "cyc", _size(a)))}
+        if alt:
+            alts["v"] = (alt, vcost(out, [a]))
+        return add("c", alts, [a, bias, scale], [out])
+
+    def acp(out, a, flex=True):
+        return act(out, a, F.Identity, alt=("cp", out, a) if flex else None)
+
+    def ascale(out, a, col, flex=True):
+        return act(out, a, F.Identity, 0.0, col, alt=("ts", out, a, col, None, A.mult, None) if flex else None)
+
+    def mm(items):
+        cyc, rd, wr = 0, [], []
+        for out, l, r, st, sp in items:
+            cyc += max(64, _size(r)) * (1 if _two(r) else 4)
+            rd += [l, r]
+            wr.append(out)
+        return add("c", {"p": (("mm", items), ("pe", cyc))}, rd, wr)
+
+    def iota(out, pat, base, mult):
+        return add("c", {"g": (("iota", out, pat, base, mult), ("cyc", 130 + 2 * _size(out)))}, [], [out])
+
+    def sel(out, a, pat, op, base, mult):
+        return add("c", {"g": (("sel", out, a, pat, op, base, mult), ("cyc", 170 + 2 * _size(out)))}, [a], [out])
+
+    def gcp(out, a):
+        return sel(out, a, [[0, _size(out)]], A.is_equal, 0, 0)
+
+    nd = [0]
+
+    def dma(out, a, nbytes, q="s"):
+        nd[0] += 1
+        return add("d", {q: (("dma", out, a), ("dma", nbytes))}, [a], [out], sem="d%d" % (nd[0] - 1))
+
+    def remote(out, a, nbytes, hop, k):
+        return add("r", {"g": (("rem", out, a, hop, k), ("dma", nbytes))}, [a], [out], sem="arr%d" % k)
+
+    S = slice
+    AL = S(None)
+    lent = {"kf": ("vfa", 0, 96), "kr": ("vfa", 96, 192), "bsf": ("vfa", 192, 288), "of": ("vfa", 288, 448), "orr": ("vfa", 448, 608),
+            "iw": ("vfa", 608, 672), "iy": ("vfa", 672, 736), "kb": ("loa", 0, 96), "ob": ("loa", 96, 256)}
+    full = lambda n: cols(*lent[n]) if n in lent else ap(n, AL)
+
+    dma(cols("sni", 0, 768), ap("sn", AL, S(0, 768)), 393216)
+    dma(full("kidc"), ap("kid", AL), 49152)
+    dma(cols("Vb", 0, 1536), ap("vn", AL), 393216, "a")
+    dma(full("Zb"), ap("zs", AL), 393216, "a")
+    dma(cols("sni", 768, 1536), ap("sn", AL, S(768, 1536)), 393216)
+    dma(full("bsc"), ap("bst", AL), 49152)
+    for j in range(2):
+        dma(full("nqi"), ap("nq", AL, S(768 * j, 768 * j + 768)), 393216)
+        cp(cols("Qt", 768 * j, 768 * j + 768), full("nqi"))
+
+    ci = lambda j: cols("ci", j, j + 1)
+    cf = lambda j: cols("cf", j, j + 1)
+    iota(ci(0), [[0, 1]], 0, 1)
+    iota(full("xi"), [[1, 160]], 0, 0)
+    ts(ci(1), ci(0), 15, None, A.bitwise_and)
+    ts(ci(2), ci(0), 4, 1, A.logical_shift_right, A.bitwise_and)
+    ts(ci(3), ci(0), 7, None, A.bitwise_and)
+    ts(ci(4), ci(0), 8, None, A.bitwise_and)
+    P16, G16, G15, P, PP16, M0, M1, MC, WA, DUM, PM, T16, S15, OWN, TMP = [cf(j) for j in range(15)]
+    ts(PP16, ci(0), 16.0, None, A.add)
+    ts(M0, ci(2), -1.0, 1.0, A.mult, A.add)
+    cp(M1, ci(2))
+    ts(full("IW0"), full("xi"), PP16, M0, A.is_equal, A.mult)
+    ts(full("IW1"), full("xi"), PP16, M1, A.is_equal, A.mult)
+    ts(TMP, ci(3), 32.0, None, A.mult)
+    ts(PM, ci(4), 2.0, TMP, A.mult, A.add)
+    ts(full("OP"), cols("xi", 0, 16), PM, None, A.add)
+    cp(P16, ci(1))
+    cp(P, ci(0))
+    tt(G16, P, P16, A.subtract)
+    ts(G15, G16, 15.0, None, A.add)
+    ts(WA, P16, 2.0, None, A.is_lt)
+    ts(full("U"), cols("xi", 0, 144), G15, K14, A.is_equal, A.mult)
+    ts(full("Ua"), cols("xi", 0, 144), G15, WA, A.is_equal, A.mult)
+    if any(v for k, v in ONACT.items() if k[0] in "EZ"):
+        ts(full("U2"), cols("xi", 0, 144), G15, 2 * K14, A.is_equal, A.mult)
+        ts(full("Un"), cols("xi", 0, 144), G15, -K14, A.is_equal, A.mult)
+    ts(full("idf"), cols("xi", 0, 128), P, None, A.is_equal)
+    ts(full("idb"), cols("xi", 0, 128), P, None, A.is_equal)
+    ts(full("nid"), cols("xi", 0, 128), P, -1.0, A.is_equal, A.mult)
+    ms(cols("CH", 0, 1536), 0.0)
+    cp(full("kf"), full("kidc"))
+    cp(full("kb"), full("kf"))
+    tt(full("kr"), full("kf"), full("kb"), A.subtract)
+    dma(ap("CH", S(0, 128, 16), S(0, 1536)), full("kf"), 49152)
+    dma(ap("CH", S(1, 128, 16), S(0, 1536)), full("kr"), 49152, "a")
+    P00, P10, Pa, Pb = cols("IW0", 16, 144), cols("IW0", 0, 128), cols("IW1", 32, 160), cols("IW1", 16, 144)
+    Ur = lambda n, r: cols(n, 15 - r, 143 - r)
+
+    def k2l(x, c):
+        n, lo = x
+        Y = "PY" + c
+        h0, h1 = cols(n, lo, lo + 128), cols(n, lo + 128, lo + 256)
+        mm([(ap(Y, AL, S(0, 8), 0, AL), P00, h0, True, False), (ap(Y, AL, S(0, 8), 0, AL), P10, h1, False, True),
+            (ap(Y, AL, S(0, 8), 1, AL), Pa, h0, True, False), (ap(Y, AL, S(0, 8), 1, AL), Pb, h1, False, True)])
+        tp(full("tr" + c), ap(Y, AL, S(0, 8), AL, AL))
+        return ind(full("tr" + c), full("OP"))
+
+    def s_in(tile, c, ch):
+        tag[0] = "i%d%s" % (tile, c)
+        cp(full("f1" + c), cols("sni", 768 * ch + tile, 768 * ch + 768, 3))
+        w = k2l(("f1" + c, 0), c)
+        act(full("sf" + c), w, F.Identity, K14, alt=("ts", full("sf" + c), w, K14, None, A.add, None))
+        ts(cols("su" + c, 256 * tile, 256 * tile + 256), full("sf" + c), -K14, None, A.add)
+
+    def z_in(tile, ch):
+        o = 2048 * tile + 1024 * ch
+        gcp(cols("zr", o, o + 256), cols("Zb", 768 * ch + tile, 768 * ch + 768, 3))
+        gcp(cols("zr", o + 256, o + 512), cols("Zb", 768 * ch + tile, 768 * ch + 768, 3))
+        gcp(cols("zr", o + 512, o + 1024), cols("zr", o, o + 512))
+
+    def psl(bank, a, b, step=1):
+        if bank.startswith("PY"):
+            assert step == 1
+            return ap(bank, AL, S(a // 32, b // 32), AL, AL)
+        return cols(bank, a, b, step)
+
+    def diag(bank, o, fam, X, first, relu=(), raw=None, pos=None):
+        ks = KS if not (0 in relu or 1 in relu) else [(0, 4), (4, 8), (8, 12), (12, 16)]
+        for k0, k1 in ks:
+            out = psl(bank, o + 16 * k0, o + 16 * k1)
+            src = [(fam, X)] if k0 // 4 not in relu else [("Un", raw), ("U2", pos)]
+            mm([(out, Ur(f, r), cols(x, 256 * k0 + r, 256 * k1, 16), first and r == 0 and j == 0,
+                 r == 15 and j == len(src) - 1 and (first or k1 == 16)) for j, (f, x) in zip(range(2), src) for r in range(16)])
+
+    flip = [0]
+
+    def dist(X, win, off, o, other, oo, on_act, XO=None, relu=(), pos=None):
+        done = []
+        XO = XO or X
+        for k in range(0, 16, 2):
+            x = cols(X, 256 * k, 256 * k + 512)
+            w = ind(win, cols(off, o + 16 * k, o + 16 * k + 32))
+            z = cols(other, oo, oo + 512)
+            if k // 4 in WIDE.get(tag[0], (0, 1, 2)) and k // 4 * 2 not in on_act and k // 4 * 2 + 1 not in on_act:
+                if k % 4 == 0:
+                    x = cols(X, 256 * k, 256 * k + 1024)
+                    tt(x, ind(win, cols(off, o + 16 * k, o + 16 * k + 64)), cols(other, oo, oo + 1024), A.subtract)
+                    if k // 4 in relu:
+                        ts(cols(pos, 256 * k, 256 * k + 1024), x, 0.0, None, A.max)
+                    else:
+                        act(cols(XO, 256 * k, 256 * k + 1024), x, F.Abs)
+            elif k // 4 in relu:
+                tt(x, w, z, A.subtract)
+                ts(cols(pos, 256 * k, 256 * k + 512), x, 0.0, None, A.max)
+            elif k // 2 in on_act:
+                E = full("PE%d" % flip[0])
+                flip[0] ^= 1
+                acp(x, w, False)
+                mm([(E, full("idb"), x, True, False), (E, full("nid"), z, False, True)])
+                act(cols(XO, 256 * k, 256 * k + 512), E, F.Abs)
+            else:
+                tt(x, w, z, A.subtract)
+                done.append(k)
+                if k % 4 == 2 or k // 2 + 1 in on_act or k >= 12:
+                    act(cols(XO, 256 * done[0], 256 * k + 512), cols(X, 256 * done[0], 256 * k + 512), F.Abs)
+                    done = []
+
+    def ds_pass(tile, c, ch, bank, o, X):
+        tag[0] = "s%d%s" % (tile, c)
+        dist(X, cols("Vb", 0, 1536), "su" + c, 256 * tile, "zr", 2048 * tile + 1024 * ch, ONACT["s%d%s" % (tile, c)])
+        mm([(psl(bank, o, o + 256), full("idf"), full("sf" + c), True, False)])
+        diag(bank, o, "U", X, False)
+        acp(full("Ks" + c), psl(bank, o, o + 256))
+
+    def child_pass(c, so, hi, bank, o):
+        tag[0] = "k%d%s" % (hi, c)
+        for k in range(0, 16, 2):
+            acp(cols("XA" + c, 256 * k, 256 * k + 512), ind(cols("CH", 0, hi), cols("su" + c, so + 16 * k, so + 16 * k + 32)))
+        diag(bank, o, "Ua", "XA" + c, True)
+        cp(full("eu" + c), psl(bank, o, o + 256))
+        act(full("ef" + c), psl(bank, o, o + 256), F.Identity, K14 + 4096.0,
+            alt=("ts", full("ef" + c), psl(bank, o, o + 256), K14 + 4096.0, None, A.add, None))
+
+    def vb_update(tile, v0, n, off, t2):
+        bt = cols("Bt", v0 + tile, v0 + 3 * n, 3)
+        acp(bt, ind(full("IO"), off))
+        ascale(t2, bt, MC)
+        tt(cols("VB", v0 + tile, v0 + 3 * n, 3), ind(full("Vb"), off), t2, A.add)
+        return bt
+
+    for ch, c in enumerate("ab"):
+        s_in(0, c, ch)
+        z_in(0, ch)
+        child_pass(c, 0, 1536, "PY" + c, 256)
+        ds_pass(0, c, ch, "PM", 256 * ch, "XZ" + c)
+    for ch, c in enumerate("ab"):
+        s_in(1, c, ch)
+        z_in(1, ch)
+
+    tag[0] = "const"
+    iota(cols("IO", 0, 4096), [[1, 4096]], 0, 0)
+    ms(cols("IO", 4096, 4112), -1.0)
+    iota(cols("Vb", 1536, 4096), [[0, 2560]], 0, 0)
+    ms(cols("Vb", 4096, 4112), 200.0)
+    iota(cols("it2", 0, 256), [[1024, 16], [0, 16]], 0, 0)
+    iota(cols("it2", 256, 512), [[0, 4], [4096, 4], [0, 16]], 0, 0)
+    iota(full("xl"), [[1, 8], [8, 2]], 0, 0)
+    iota(full("gid"), [[16, 64]], 16384 + 8192 + 3072, 0)
+    iota(cols("CH", 1536, 4112), [[1, 2576]], 1536, 0)
+    iota(cols("Qt", 1536, 4096), [[0, 2560]], 0, 0)
+    acp(full("PK"), full("it2"))
+    ts(MC, P16, 0.0, 1.0 / K14, A.is_equal, A.mult)
+    ts(DUM, P16, 4096.0, None, A.add)
+    ts(T16, P16, 16.0, None, A.mult)
+    ts(S15, P, 16.0, 15.0, A.mult, A.add)
+    ts(OWN, P16, 160.0, 1536.0, A.mult, A.add)
+    ts(full("gid"), full("gid"), P16, None, A.add)
+    ts(full("SL"), cols("xi", 0, 144), S15, None, A.is_equal)
+    ts(full("OB"), cols("xi", 0, 16), 0.0, P16, A.mult, A.add)
+    cp(full("OE"), cols("xi", 0, 16))
+    ts(full("OL"), full("xl"), T16, None, A.add)
+    iota(full("Wb"), [[0, 2048]], 128, 0)
+    sel(full("Wt"), full("Wb"), [[-1, 16], [0, 8], [1, 16]], A.is_equal, 0, 0)
+    sel(full("Wt"), full("Wt"), [[0, 16], [-16, 8], [0, 16]], A.is_ge, 0, 1)
+    sel(full("Wt"), full("Wt"), [[1, 16], [16, 8], [0, 16]], A.is_gt, 0, -1)
+    sel(full("Wb"), full("Wb"), [[-1, 16], [-16, 8], [0, 16]], A.is_equal, 0, 1)
+    ts(full("of"), full("xi"), OWN, None, A.add)
+    cp(full("ob"), full("of"))
+    tt(full("orr"), full("of"), full("ob"), A.subtract)
+    dma(ap("CH", S(1, 128, 16), S(1536, 4096)), full("orr"), 81920)
+    cp(full("bsf"), full("bsc"))
+    dma(ap("Bt", S(0, 8), AL), full("bsf"), 49152)
+    for j in range(2):
+        mm([(cols("PE0", 32 * j, 32 * j + 32), ap("SL", S(0, 8), S(15 - r, 143 - r)), ap("Bt", S(0, 8), S(1 + j + 3 * r, 1536, 48)),
+             r == 0, r == 15) for r in range(16)])
+    ts(full("iw"), cols("PE0", 0, 64), 0.0, 4097.0, A.is_lt, A.mult)
+    tt(full("iy"), cols("PE0", 0, 64), full("iw"), A.add)
+    cp(full("iu"), full("iy"))
+    for j in range(2):
+        vb_update(1 + j, 0, 512, cols("iu", 32 * j, 32 * j + 32), full("it2"))
+    s4, pk = cols("it2", 0, 256), cols("it2", 256, 512)
+    ascale(s4, cols("sni", 770, 1536, 3), 4096.0)["alts"].pop("a")
+    tt(cols("YS", 2, 768, 3), s4, cols("sni", 2, 768, 3), A.add)
+
+    def s_out(tile):
+        tag[0] = "o%d" % tile
+        ts(s4, full("Ma"), 4096.0, None, A.mult)
+        tt(pk, s4, full("Mb"), A.add)
+        acp(s4, ind(pk, full("OL")))
+        tp(full("pY"), s4)
+        y0, y1 = ap("pY", AL, AL, 0, AL), ap("pY", AL, AL, 1, AL)
+        mm([(cols("PM", 0, 128), P00, y0, True, False), (cols("PM", 0, 128), P10, y1, False, True),
+            (cols("PM", 128, 256), Pa, y0, True, False), (cols("PM", 128, 256), Pb, y1, False, True)])
+        acp(cols("YS", tile, 768, 3), cols("PM", 0, 256))
+
+    for t in range(3):
+        tile = TILE[t]
+        new0 = 1536 + 512 * t
+        for ch, c in enumerate("ab"):
+            X, Y = "PX" + c, "PY" + c
+            zo = 2048 * tile + 1024 * ch
+            tag[0] = "e%d%s" % (t, c)
+            mm([(cols(X, 0, 256), full("idf"), full("ef" + c), True, False)])
+            dist("XE" + c, cols("Vb", 0, [1536, 2048, 3584][t]), "eu" + c, 0, "zr", zo, ONACT["e%d%s" % (t, c)],
+                 None, ONACT["E%d%s" % (t, c)], "XA" + c)
+            diag(X, 0, "U", "XE" + c, False, ONACT["E%d%s" % (t, c)], "XE" + c, "XA" + c)
+            if t > 0:
+                tag[0] = "g%d%s" % (t, c)
+                gv = cols("GV%d" % (t - 1), 256 * ch, 256 * ch + 256)
+                yl, yh = psl(Y, 0, 256), psl(Y, 256, 512)
+                mm([(yh, full("idb"), gv, True, False), (yh, full("nid"), cols("zr", zo, zo + 256), False, True)])
+                act(cols("nt" + c, 0, 256), yh, F.Abs)
+                go = 32 * (t - 1) + 16 * ch
+                g16 = ap(Y, AL, 8, 0, AL)
+                mm([(g16, full("idf"), cols("gid", go, go + 16), True, False)] +
+                   [(g16, Ur("U", r), cols("nt" + c, r, 256, 16), False, r == 15) for r in range(16)])
+                acp(cols("tf" + c, 0, 16), g16)
+                acp(full("t1" + c), ind(cols("tf" + c, 0, 16), full("OB")))
+                acp(yl, full("t1" + c))
+        for ch, c in enumerate("ab"):
+            X, Y = "PX" + c, "PY" + c
+            yl = psl(Y, 0, 256)
+            tag[0] = "c%d%s" % (t, c)
+            ks = full(("Ks" if t < 2 else "Mc") + c)
+            tt(full("M" + c), cols(X, 0, 256), ks, A.min)
+            last = "M" + c
+            if t > 0:
+                ts(full("M2" + c), full("M" + c), 0xFFC000, None, A.bitwise_and)
+                tt(full("f1" + c), full("M2" + c), cols("PK", 0, 256), A.subtract)
+                tt(cols("f2" + c, 0, 128), cols("f1" + c, 0, 128), cols("f1" + c, 128, 256), A.max)
+                tt(cols("f2" + c, 128, 192), cols("f2" + c, 0, 64), cols("f2" + c, 64, 128), A.max)
+                tt(cols("f2" + c, 192, 224), cols("f2" + c, 128, 160), cols("f2" + c, 160, 192), A.max)
+                tt(cols("f2" + c, 224, 240), cols("f2" + c, 192, 208), cols("f2" + c, 208, 224), A.max)
+                ts(cols("tf" + c, 16, 32), cols("f2" + c, 224, 240), 1.0, None, A.add)
+                tt(full("t1" + c), ind(cols("tf" + c, 16, 32), full("OB")), full("f1" + c), A.subtract)
+                tt(yl, yl, full("t1" + c), A.mult)
+                tt(full("M2" + c), yl, full("M" + c), A.min)
+                last = "M2" + c
+            Mc, A1, L1, L2, L3 = ["%s%s" % (x, c) for x in ("Mc", "A1", "L1", "L2", "L3")]
+            ts(full(Mc), full(last), 0xFFCFFF, None, A.bitwise_and)
+            tt(full(A1), full(Mc), cols("PK", 256, 512), A.add)
+            tt(full(L1), ap(A1, AL, S(0, 16, 2), AL), ap(A1, AL, S(1, 16, 2), AL), A.min)
+            tt(full(L2), ap(L1, AL, S(0, 8, 2), AL), ap(L1, AL, S(1, 8, 2), AL), A.min)
+            ts(full(L2), full(L2), 0xFFCFFF, None, A.bitwise_and)
+            tt(ap(L3, AL, S(0, 4), AL), full(L2), cols("PK", 256, 320), A.add)
+            tt(ap(L3, AL, S(4, 6), AL), ap(L3, AL, S(0, 4, 2), AL), ap(L3, AL, S(1, 4, 2), AL), A.min)
+            tt(cols("ti" + c, 0, 16), ap(L3, AL, 4, AL), ap(L3, AL, 5, AL), A.min)
+            a32 = cols("ti" + c, 16, 32)
+            ts(a32, cols("ti" + c, 0, 16), 4095, None, A.bitwise_and)
+            au, a2u = cols("au" + c, 0, 16), cols("au" + c, 16, 32)
+            cp(au, a32)
+            act(cols("nt" + c, 256, 512), full(A1), F.Sign, 0.5 - 201.0 * K14)
+            mm([(cols(X, 256, 272), full("idb"), cols("nt" + c, 256 + 16 * k, 272 + 16 * k), k == 0, k == 15) for k in range(16)])
+            dd, yy, a2f, w1, w2 = [cols("tf" + c, 16 * j, 16 * j + 16) for j in range(2, 7)]
+            ts(dd, cols(X, 256, 272), -15.5, 8192.0, A.is_lt, A.mult)
+            tt(yy, a32, dd, A.add)
+            ts(a2u, yy, 4096.0, None, A.min)
+            ts(a2f, yy, 4096.0, None, A.min)
+            tag[0] = "q%d%s" % (t, c)
+            qa = ("qn%d" % t, 256 * ch) if t < 2 else ("ef" + c, 0)
+            acp(cols(qa[0], qa[1], qa[1] + 256), ind(cols("Qt", 0, 1536 if t == 0 else 4096), au))
+            cp(full("qu" + c), k2l(qa, c))
+            tag[0] = "l%d%s" % (t, c)
+            va = cols("va" + c, 0, 256)
+            acp(va, ind(cols("Vb", 0, [1536, 3584, 4096][t]), au))
+            gcp(cols("va" + c, 256, 512), va)
+            gcp(cols("va" + c, 512, 1024), cols("va" + c, 0, 512))
+            ascale(full("t1" + c), ind(full("IO"), au), MC)
+            bt = cols("Bt", 768 * ch + tile, 768 * ch + 768, 3)
+            acp(bt, ind(full("IO"), a2u))
+            dead = cols("nt" + c, 512, 768)
+            act(dead, bt, F.Relu, 0.0, -200.0, alt=("ts", dead, bt, -200.0, 0.0, A.mult, A.max))
+            xh = cols(X, 0, 256)
+            mm([(xh, full("idf"), full("t1" + c), True, False), (xh, full("idb"), va, False, False),
+                (xh, full("idb"), dead, False, True)])
+            acp(cols("VB", 768 * ch + tile, 768 * ch + 768, 3), xh)
+            x2 = cols(X, 256, 512)
+            mm([(x2, full("idf"), full("t1" + c), True, False), (x2, full("idb"), va, False, True)])
+            acp(cols("vf" + c, 0, 256), x2)
+            gcp(cols("vf" + c, 256, 512), cols("vf" + c, 0, 256))
+            gcp(cols("vf" + c, 512, 1024), cols("vf" + c, 0, 512))
+            tag[0] = "d%d%s" % (t, c)
+            eq = cols("nt" + c, 0, 256)
+            tt(eq, ind(a2f, full("OE")), bt, A.is_equal)
+            mm([(cols(X, 256, 272), cols("Wt", 128 * r, 128 * r + 128), cols("nt" + c, r, 256, 16), r == 0, r == 15) for r in range(16)])
+            ts(w1, cols(X, 256, 272), 0.0, 8192.0, A.is_gt, A.mult)
+            tt(w2, w1, yy, A.add)
+            ts(cols("au" + c, 32, 64, 2), w2, DUM, None, A.min)
+            ts(full("M" + c), full(Mc), 4095, None, A.bitwise_and)
+            if t == 1:
+                cp(cols("su" + c, 0, 256), full("M" + c))
+        for ch, c in enumerate("ab"):
+            X = "PX" + c
+            va = cols("va" + c, 0, 256)
+            zact = ONACT["z%d%s" % (t, c)]
+            tag[0] = "z%d%s" % (t, c)
+            dist("XZ" + c, full("Zb"), "qu" + c, 0, "va" + c, 0, [2 * j + i for j in zact for i in range(2)], "XA" + c,
+                 ONACT["Z%d%s" % (t, c)], "XA" + c)
+            diag(X, 0, "U", "XA" + c, True, ONACT["Z%d%s" % (t, c)], "XZ" + c, "XA" + c)
+            act(full("f2" + c), cols(X, 0, 256), F.Identity, FAR + 0.5, -1.0 / K14,
+                alt=("ts", full("f2" + c), cols(X, 0, 256), -1.0 / K14, FAR + 0.5, A.mult, A.add))
+            act(cols("lo" + c, 0, 256), va, F.Relu, -2.0, alt=("ts", cols("lo" + c, 0, 256), va, -2.0, 0.0, A.add, A.max))
+            ts(cols("lo" + c, 256, 512), va, 2.0, 63.0, A.add, A.min)
+        tag[0] = "x%d" % t
+        iota(full("SC"), [[1, 512]], new0, 0)
+        dma(ap("SC", S(1, 128, 16), AL), ap("CH", S(1, 128, 16), S(new0, new0 + 512)), 16384)
+        for ch, c in enumerate("ab"):
+            for m in range(15, -1, -1):
+                o = 256 * ch + 16 * m
+                cp(ind(full("CH"), cols("au" + c, 32 + 2 * m, 33 + 2 * m)), cols("SC", o, o + 16))
+        if t < 2:
+            qn = full("qn%d" % t)
+            remote(full("GQ%d" % t), qn, 262144, HOPS[t], 2 * t)
+            dma(cols("Qt", new0, new0 + 512), qn, 262144)
+            dma(cols("Qt", 3072 + 512 * t, 3584 + 512 * t), full("GQ%d" % t), 262144)
+        if t == 0:
+            s_out(0)
+            for ch, c in enumerate("ab"):
+                ds_pass(1, c, ch, "PM", 256 * ch, "XS")
+        if t == 2:
+            s_out(1)
+            dma(ap("ys", AL), full("YS"), 393216)
+            dma(ap("yk", AL), ap("CH", S(0, 128, 16), S(0, 4096)), 131072)
+            dma(ap("yb", AL), ap("Bt", S(0, 128, 16), AL), 49152)
+        for ch, c in enumerate("ab"):
+            X, Y = "PX" + c, "PY" + c
+            yl = psl(Y, 0, 256)
+            tag[0] = "b%d%s" % (t, c)
+            dist("XE" + c, full("VB"), "qu" + c, 0, "vf" + c, 0, [])
+            tag[0] = "h%d%s" % (t, c)
+            nat = lambda a, b: cols("nt" + c, 512 + a, 512 + b)
+            H = cols(X, 0, 256)
+            mm([(H, full("idb"), cols("va" + c, 0, 256), True, False)])
+            for kg in range(4):
+                for k0, k1 in KS4:
+                    if k0 // 4 != kg:
+                        continue
+                    a0, a1 = 16 * k0, 16 * k1
+                    mm([(psl(Y, a0, a1), Ur("U", r), cols("XE" + c, 256 * k0 + r, 256 * k1, 16), r == 0, r == 15) for r in range(16)])
+                    n2 = cols("nt" + c, 256 + a0, 256 + a1)
+                    act(n2, psl(Y, a0, a1), F.Sign, alt=("ts", n2, psl(Y, a0, a1), 0.0, None, A.is_gt, None))
+                    act(psl(Y, a0, a1), psl(Y, a0, a1), F.Abs, -FAR, 1.0 / K14)
+                    tt(psl(Y, a0, a1), psl(Y, a0, a1), cols("f2" + c, a0, a1), A.is_ge)
+                    tt(nat(a0, a1), psl(Y, a0, a1), n2, A.mult)
+                if kg == 3:
+                    c16 = ap(Y, AL, 8, 0, AL)
+                    mm([(c16, full("idb"), nat(16 * k, 16 * k + 16), k == 0, k == 15) for k in range(16)])
+                    cn = cols("nt" + c, 0, 16)
+                    act(cn, c16, F.Identity, 0.0, -1.0 / 128, alt=("ts", cn, c16, -1.0 / 128, None, A.mult, None))
+                    mm([(cols(X, r, 256, 16), cols("Wb", 128 * r, 128 * r + 128), cn, False, False) for r in range(16)])
+                for hf in range(2):
+                    E = "PE%d" % hf
+                    it = []
+                    for j in range(8):
+                        r = 8 * hf + j
+                        it += [(cols(E, j, 512, 8), full("idb"), cols("XZ" + c, 1024 * kg + r, 1024 * kg + 1024, 16), True, False)]
+                        if kg in ONACT["z%d%s" % (t, c)] and kg not in ONACT["Z%d%s" % (t, c)]:
+                            it += [(cols(E, j, 512, 8), full("nid"), cols("va" + c, r, 1024, 16), False, False)]
+                        it += [(cols(E, j, 512, 8), cols("Wb", 128 * r, 128 * r + 128), nat(64 * kg, 64 * kg + 64), False, True)]
+                    mm(it)
+                    so = ap("sg" + c, AL, S(64 * kg, 64 * kg + 64), S(8 * hf, 8 * hf + 8))
+                    act(so, full(E), F.Sign, alt=("ts", so, full(E), 1.0, -1.0, A.min, A.max))
+                mm([(H, full("idb"), ap("sg" + c, AL, S(16 * k, 16 * k + 16), AL), False, k == 15) for k in range(4 * kg, 4 * kg + 4)])
+            tt(H, H, cols("lo" + c, 0, 256), A.max)
+            tt(cols("Vb", new0 + 256 * ch, new0 + 256 * ch + 256), H, cols("lo" + c, 256, 512), A.min)
+            if t == 2:
+                dma(ap("yv", AL, S(1024 + 256 * ch, 1280 + 256 * ch)), cols("Vb", new0 + 256 * ch, new0 + 256 * ch + 256), 65536)
+        if t < 2:
+            nv = cols("Vb", new0, new0 + 512)
+            remote(full("GV%d" % t), nv, 131072, HOPS[t], 2 * t + 1)
+            dma(ap("yv", AL, S(512 * t, 512 * t + 512)), nv, 131072)
+            dma(cols("Vb", 3072 + 512 * t, 3584 + 512 * t), full("GV%d" % t), 131072)
+            for ch, c in enumerate("ab"):
+                child_pass(c, 256 * (1 - t), [2048, 4096][t], "PM", 256 * ch)
+    assert nd[0] <= NDMA
+    return ops
+
+
+def depend(ops):
+    hist = {}
+    for o in ops:
+        d = {}
+        for acc, w in [(x, False) for x in o["rd"]] + [(x, True) for x in o["wr"]]:
+            m = _mask(acc)[0]
+            ps = _chain(acc)
+            row = _row(acc)
+            for (n, hm, hw, hr) in hist.get(acc[0], []):
+                if n == o["n"] or (row is not None and hr is not None and row != hr):
+                    continue
+                if (hm & m) and (w or hw):
+                    d[n] = True
+                elif ps:
+                    d.setdefault(n, False)
+        o["deps"] = d
+        for acc, w in [(x, False) for x in o["rd"]] + [(x, True) for x in o["wr"]]:
+            m = _mask(acc)[0]
+            h = hist.setdefault(acc[0], [])
+            if w and not _chain(acc) and acc[1][0] == slice(None):
+                h[:] = [(n, hm & ~m, hw, hr) for (n, hm, hw, hr) in h if hm & ~m]
+            if _chain(acc):
+                h[:] = [x for x in h if x[0] != o["n"]][-3:]
+                m = (1 << 512) - 1
+                w = True
+            h.append((o["n"], m, w, _row(acc)))
+
+
+def _row(x):
+    p = x[1][0]
+    return p.start if p.step == 16 else None
+
+
+def _chain(x):
+    return _psum(x) and x[0] != "PK"
+
+
+def _times(o, e, C):
+    kind, n = o["alts"][e][1]
+    if kind == "dma":
+        return (60.0 if e != "g" else 1000.0), C["dma"] + n / 150.0
+    if kind == "pe":
+        t = n * C["pe"]
+    elif kind == "cyc":
+        t = max(n, 64) * C["cyc"]
+    else:
+        t = (50.0 if e == "v" else 65.0) * C["cyc"] / 0.83 + n * C[kind] * C["cyc"]
+    return t, t
+
+
+def schedule(ops, C):
+    succ = [[] for _ in ops]
+    for o in ops:
+        for d in o["deps"]:
+            succ[d].append(o["n"])
+    prio = [0.0] * len(ops)
+    for o in reversed(ops):
+        e = list(o["alts"])[0]
+        prio[o["n"]] = _times(o, e, C)[1] + C["lat"] + max([prio[s] for s in succ[o["n"]]] or [0.0])
+    bias = [1000.0 * BIAS.get(o["tag"] + list(o["alts"])[0], 0) for o in ops]
+    order = forward(ops, C, succ, [p + b for p, b in zip(prio, bias)])
+    for _ in range(C["turns"]):
+        order = forward(ops, C, succ, backward(ops, C, succ))
+    return order
+
+
+def backward(ops, C, succ):
+    tm = [_times(o, o["e"], C) for o in ops]
+    left = [len(s) for s in succ]
+    ready = [t[1] - t[0] for t in tm]
+    avail = [o["n"] for o in ops if not succ[o["n"]]]
+    free = dict((e, 0.0) for e in "vapgs")
+    out = [0.0] * len(ops)
+    while avail:
+        n = min(avail, key=lambda k: (max(free[ops[k]["e"]], ready[k]), -ops[k]["t0"] - tm[k][0]))
+        e = ops[n]["e"]
+        end = max(free[e], ready[n]) + tm[n][0]
+        free[e] = out[n] = end
+        avail.remove(n)
+        for d in ops[n]["deps"]:
+            lag = 0.0 if (e == "p" and ops[d]["e"] == "p") else tm[d][1] - tm[d][0] + C["lat"]
+            ready[d] = max(ready[d], end + lag)
+            left[d] -= 1
+            if left[d] == 0:
+                avail.append(d)
+    return out
+
+
+def forward(ops, C, succ, prio):
+    left = [len(o["deps"]) for o in ops]
+    ready_at = [0.0] * len(ops)
+    avail = [o["n"] for o in ops if not o["deps"]]
+    free = dict((e, 0.0) for e in "vapgs")
+    order = []
+    while avail:
+        best = None
+        for n in avail:
+            alts = list(ops[n]["alts"])
+            for j, e in enumerate(alts):
+                st = max(free[e], ready_at[n])
+                if j > 0:
+                    if free[alts[0]] <= st + C["alt"]:
+                        continue
+                    st_key = (st, 1, -prio[n])
+                else:
+                    st_key = (st, 0, -prio[n])
+                if best is None or st_key < best[0]:
+                    best = (st_key, n, e, st)
+        _, n, e, st = best
+        o = ops[n]
+        busy, done = _times(o, e, C)
+        o["e"], o["t0"], o["t1"] = e, st, st + done
+        free[e] = st + busy
+        avail.remove(n)
+        order.append(n)
+        for s in succ[n]:
+            pe_pair = e == "p" and "p" in ops[s]["alts"]
+            ready_at[s] = max(ready_at[s], st + (busy if pe_pair else done + C["lat"]))
+            left[s] -= 1
+            if left[s] == 0:
+                avail.append(s)
+    return order
+
+
+def plan():
+    ops = build()
+    depend(ops)
+    order = schedule(ops, COST)
+    needs = [False] * len(ops)
+    for o in ops:
+        for d, hard in o["deps"].items():
+            same = ops[d]["e"] == o["e"] and ops[d]["kind"] == "c" and o["kind"] == "c"
+            if not (same and (o["e"] == "p" or not hard)):
+                needs[d] = True
+    count = dict((e, 0) for e in "vapg")
+    know = dict((e, {}) for e in "vapgs")
+    for n in order:
+        o = ops[n]
+        e = o["e"]
+        waits = {}
+        for d, hard in o["deps"].items():
+            p = ops[d]
+            same = p["e"] == e and p["kind"] == "c" and o["kind"] == "c"
+            if same and (e == "p" or not hard):
+                continue
+            s, val = p["sig"]
+            if know[e].get(s, 0) < val:
+                waits[s] = max(waits.get(s, 0), val)
+        keep = {}
+        for s, val in waits.items():
+            covered = False
+            for d in o["deps"]:
+                p = ops[d]
+                if p["sig"] and p["sig"][0] != s and waits.get(p["sig"][0], 0) >= p["sig"][1] and p["vc"].get(s, 0) >= val:
+                    covered = True
+            if not covered:
+                keep[s] = val
+        for d in o["deps"]:
+            p = ops[d]
+            if p["sig"] and max(know[e].get(p["sig"][0], 0), waits.get(p["sig"][0], 0)) >= p["sig"][1]:
+                for s, val in p["vc"].items():
+                    know[e][s] = max(know[e].get(s, 0), val)
+        for s, val in waits.items():
+            know[e][s] = max(know[e].get(s, 0), val)
+        o["waits"] = keep
+        o["vc"] = dict(know[e]) if o["kind"] != "r" else {}
+        if o["kind"] != "c":
+            o["sig"] = (o["sem"], 16)
+        elif needs[n] or e != "p":
+            count[e] += 1
+            o["sig"] = (e, count[e])
+        else:
+            o["sig"] = None
+    return ops, order, count
+
+
+_plan = []
+
+
+def rank_program(g, core, T, topo):
+    rank = T.rank_of(core)
+    if rank is None:
+        return
+    if not _plan:
+        _plan.append(plan())
+    ops, order, count = _plan[0]
+    queue = {"v": g.vector, "a": g.scalar, "p": g.tensor, "g": g, "s": g.sync}
+    nrank = len(T.cores)
+
+    def X(x):
+        if not isinstance(x, tuple):
+            return x
+        if x[0] == "*":
+            return X(x[1]).indirect(X(x[2]))
+        return T[x[0]][x[1]]
+
+    sent = 0
+    for n in order:
+        o = ops[n]
+        q = queue[o["e"]]
+        for s, val in o["waits"].items():
+            q.wait_ge(T.sem[s], val)
+        call = o["alts"][o["e"]][0]
+        k = call[0]
+        if k == "tt":
+            i = q.tensor_tensor(X(call[1]), X(call[2]), X(call[3]), call[4])
+        elif k == "ts":
+            if call[6] is None:
+                i = q.tensor_scalar(X(call[1]), X(call[2]), X(call[3]), None, call[5])
+            else:
+                i = q.tensor_scalar(X(call[1]), X(call[2]), X(call[3]), X(call[4]), call[5], call[6])
+        elif k == "cp":
+            i = q.tensor_copy(X(call[1]), X(call[2]))
+        elif k == "tp":
+            i = q.transpose(X(call[1]), X(call[2]))
+        elif k == "ms":
+            i = q.memset(X(call[1]), call[2])
+        elif k == "act":
+            i = q.activation(X(call[1]), X(call[2]), call[3], X(call[4]), X(call[5]))
+        elif k == "mm":
+            for out, l, r, st, sp in call[1]:
+                i = q.matmul(X(out), X(l), X(r), st, sp)
+        elif k == "iota":
+            if SCRATCH[call[1][0]][2] == I32:
+                i = q.iota(X(call[1]), call[2], call[3], call[4])
+            else:
+                i = q.iota(X(call[1]), call[2], call[3], call[4], allow_small_or_imprecise_dtypes=True)
+        elif k == "sel":
+            i = q.affine_select(X(call[1]), X(call[2]), call[3], call[4], 0.0, call[5], call[6])
+        elif k == "dma":
+            i = q.dma_start(X(call[1]), X(call[2]))
+        else:
+            dst = T.cores[(rank + call[3]) % nrank]
+            rid, pid, _ = topo.addr(dst)
+            assert len(topo.engines(core, dst)) == o["sig"][1]
+            q.remote_dma(X(call[1]), X(call[2]), T.sem[o["sem"]], T.sem.sent, pid, rid, topo.mask(core, dst))
+            sent += o["sig"][1]
+            continue
+        if o["sig"]:
+            i.then_inc(T.sem[o["sig"][0]], 16 if o["kind"] == "d" else 1)
+    for e in "vapg":
+        g.wait_ge(T.sem[e], count[e])
+    g.wait_ge(T.sem.sent, sent)
+    for o in ops:
+        if o["kind"] != "c":
+            g.wait_ge(T.sem[o["sem"]], 16)

@@ -1,10 +1,12 @@
+import math
 from concourse.mybir import dt, AluOpType, AxisListType, ActivationFunctionType
 
 A = AluOpType
 F = ActivationFunctionType
 BF, F32, I32, U16 = "bfloat16", "float32", "int32", "uint16"
 HOPS, TILE = [1, 3], [0, 1, 1]
-K14 = 16384.0
+PARENTS = [1536, 3584, 4096]
+K = 32768.0
 FAR = 1009.0
 
 SCRATCH = {}
@@ -15,52 +17,51 @@ def _sb(name, shape, dtype):
 
 
 for _n, _w, _d in [("Vb", 4112, BF), ("IO", 4112, F32), ("CH", 4112, F32), ("Qt", 4096, F32), ("VB", 1536, F32),
-                   ("Bt", 1536, F32), ("Zb", 1536, BF), ("sni", 1536, I32), ("nqi", 768, I32), ("SC", 512, F32),
+                   ("Bt", 1536, F32), ("Zb", 1536, BF), ("sni", 1536, I32), ("SC", 512, F32),
                    ("YS", 768, F32), ("Wb", 2048, BF), ("Wt", 2048, BF), ("XS", 4096, BF),
-                   ("xi", 160, F32), ("xl", 16, F32), ("U", 144, BF), ("Ua", 144, BF), ("U2", 144, BF), ("Un", 144, BF),
+                   ("xi", 160, F32), ("xl", 16, F32), ("U", 144, BF), ("U2", 144, BF), ("Ua", 144, BF), ("Ue", 144, BF),
+                   ("Us", 144, BF), ("Un", 144, BF), ("Wn", 128, BF), ("Wa", 128, BF), ("Wk", 128, BF), ("idB", 128, BF),
                    ("IW0", 160, F32), ("IW1", 160, F32), ("idb", 128, BF), ("nid", 128, BF), ("idf", 128, F32),
-                   ("SL", 144, F32), ("ci", 8, I32), ("cf", 16, F32),
+                   ("SL", 144, BF), ("ci", 16, I32), ("cf", 32, F32), ("kbb", 256, BF), ("z16", 64, F32), ("gx", 128, BF), ("rm", 32, F32),
                    ("OB", 16, U16), ("OE", 16, U16), ("OP", 16, U16), ("OL", 16, U16), ("gid", 64, F32),
-                   ("kidc", 96, I32), ("bsc", 96, I32), ("iu", 64, U16), ("it2", 512, F32),
+                   ("kidc", 96, I32), ("bsc", 96, I32), ("iu", 96, U16), ("it2", 512, F32),
                    ("qn0", 512, F32), ("qn1", 512, F32), ("GQ0", 512, F32), ("GQ1", 512, F32), ("GV0", 512, BF), ("GV1", 512, BF),
                    ("zr", 4096, BF)]:
     _sb(_n, [_w], _d)
 _sb("pY", [8, 2, 16], F32)
 for _c in "ab":
     for _n, _s, _d in [("XE", [4096], BF), ("XZ", [4096], BF), ("XA", [4096], BF),
-                       ("sg", [256, 16], BF), ("f1", [256], F32), ("f2", [256], F32), ("Ks", [256], F32),
+                       ("sg", [256, 16], BF), ("f1", [256], F32), ("f2", [256], F32), ("Ks", [256], F32), ("zc", [256], F32),
                        ("ef", [256], F32), ("sf", [256], F32), ("su", [512], U16), ("eu", [256], U16), ("qu", [256], U16),
-                       ("M", [256], I32), ("M2", [256], I32), ("Mc", [16, 16], I32), ("A1", [16, 16], F32), ("L1", [8, 16], F32),
-                       ("L2", [4, 16], I32), ("L3", [8, 16], F32), ("tr", [256], F32), ("ti", [32], I32), ("tf", [128], F32),
+                       ("M", [256], I32), ("M2", [256], I32), ("Mc", [256], I32), ("L1", [128], F32),
+                       ("L2", [64], I32), ("L3", [96], F32), ("tr", [256], F32), ("ti", [32], I32), ("tf", [96], F32),
                        ("au", [64], U16), ("va", [1024], BF), ("vf", [1024], F32), ("t1", [256], F32),
                        ("lo", [512], BF), ("nt", [768], BF)]:
         _sb(_n + _c, _s, _d)
-for _n in ["PXa", "PXb", "PE0", "PE1", "PM", "PK"]:
+for _n in ["PXa", "PXb", "PE0", "PE1", "PE2", "PM"]:
     SCRATCH[_n] = ("psum", [128, 512], F32)
 for _n in ["PYa", "PYb"]:
     SCRATCH[_n] = ("psum", [128, 16, 2, 16], F32)
 
-NDMA = 40
-SEMAPHORES = ["v", "a", "p", "g", "sent"] + ["d%d" % _i for _i in range(NDMA)] + ["arr%d" % _i for _i in range(4)]
+NDMA = 90
+SEMAPHORES = ["v", "a", "p", "g", "sent"] + ["d%d" % _i for _i in range(NDMA)] + ["arr%d" % _i for _i in range(6)]
 
-COST = {"cyc": 1.0, "gat": 1.56, "sca": 3.8, "pe": 0.55, "lat": 90.0, "dma": 2000.0, "alt": 500.0, "turns": 1}
+COST = {"cyc": 1.0, "gat": 1.56, "sca": 3.8, "pe": 0.55, "lat": 90.0, "dma": 2600.0, "issue": 1300.0, "rate": 110.0, "alt": 1000.0, "look": 120.0,
+        "shifts": 300, "tries": 105000, "heat": 0.00005, "whole": 0.1, "seed": 1}
+SPREAD = [{"gat": 1.3, "sca": 3.0, "lat": 100.0, "dma": 2000.0, "issue": 1000.0, "rate": 150.0},
+          {"gat": 2.0, "sca": 4.5, "lat": 150.0, "pe": 0.5, "dma": 3200.0, "issue": 1600.0, "rate": 90.0}]
 KS = [(0, 8), (8, 12), (12, 16)]
-BIAS = {'z2ba':-2,'z2bp':-2,'z2bv':-1,'i1ba':10,'i1bp':10,'i1bv':10,'k4096aa':-1,'k4096ap':19,'k4096av':-1,'i0aa':10,'i0ap':10,'i0av':10,'b0aa':-1,'b0av':9,'q2ba':-1,'k1536ap':-20,'e2bv':-5,'o0v':5,'b1aa':1,'b1av':1,'g1aa':1,'q1aa':20,'q1ap':20,'q1av':20,'l2ba':-1,'l2bp':-1,'x1v':20,'c1aa':10,'c1ap':10,'c1av':10,'h1aa':4,'e2ba':-1,'i0ba':1,'i0bp':1,'i0bv':1,'z1ba':-1,'z1bp':-1,'z1bv':-1,'l1ba':1,'loadv':-1,'h1ap':10,'h1av':5,'d2ap':10,'d2av':10,'e1aa':1,'e1ap':1,'d1ap':2,'d1av':3,'b0ba':-5,'c0aa':1,'c0ap':1,'c0av':1,'h2aa':5,'h2ap':5,'h2as':5,'h2av':5,'e2aa':20,'b2ba':-1,'b2bv':-1,'c1ba':5,'c1bp':5,'c1bv':5,'i1ap':5,'d0av':-2,'q1bv':-2,'s0bv':-20,'d1bv':5,'h0aa':9,'x0g':-1,'x0s':-1,'x0v':-1,'e2av':1,'l0ap':5,'h0ap':10,'h0av':10,'k2048aa':-5,'q0bv':1,'s1ba':-2,'s1bp':-2,'s1bv':-2,'h0ba':2,'h0bg':2,'h0bp':2,'h0bs':2,'h0bv':2}
-WIDE = {}
-KS4 = [(0, 8), (8, 12), (12, 16)]
-ONACT = {"s0a": [], "s0b": [], "s1a": [], "s1b": [], "e0a": [], "e0b": [], "e1a": [], "e1b": [], "e2a": [], "e2b": [],
-         "z0a": [], "z0b": [], "z1a": [], "z1b": [], "z2a": [], "z2b": [],
-         "E0a": [], "E0b": [], "E1a": [], "E1b": [], "E2a": [], "E2b": [],
-         "Z0a": [], "Z0b": [], "Z1a": [], "Z1b": [], "Z2a": [], "Z2b": []}
-ONACT.update({'s0a':[1],'s0b':[2],'s1a':[2,4,5],'s1b':[0,2,4,6],'e0b':[0],'e1a':[4,5],'e1b':[5,7],'e2a':[0,1,6],'e2b':[0],'z0a':[0,3],'z1a':[1],'z1b':[2],'z2a':[1],'z2b':[0]})
-BIAS = {'c1av':32,'c2av':8,'q1av':-12,'q2av':2,'q1aa':5,'q2aa':2,'x0v':22,'d1bv':22,'d0av':5,'d0bv':10,'loada':10,'loadg':13,'loads':18,'loadv':10,'q1ap':-20,'g1ba':83,'g1bp':95,'q2ba':22,'q2bp':22,'q2bv':22,'x1g':-5,'x1s':10,'q2ap':-13,'s1ap':-2,'s0ba':20,'s0bp':10,'s0bv':10,'q1bv':-2,'z2bv':8,'x0g':-8,'s0ap':-5,'e2aa':2,'e2ap':2,'e2av':-14,'i0aa':17,'i0ag':9,'i0ap':-9,'i0av':3,'i1ba':-20,'z0bv':-3,'h1ba':3,'h1bg':-2,'h1bp':3,'h1bs':3,'h1bv':3,'s1aa':11,'s1av':30,'d1bp':9,'e1ap':1,'h0av':54,'g2bp':-25,'z2ba':3,'z2bp':-12,'h2bp':34,'o0p':52,'e1bp':42,'l2aa':2,'c1bv':42,'e1aa':-1,'c0ba':2,'c0bp':-5,'d1ap':-30,'h1aa':19,'b2av':9,'l1bg':1,'i1bg':10,'z0ba':-5,'z0bp':-33,'l2ba':-11,'l2bg':-6,'l2bp':-6,'g2aa':2,'g2ap':8,'i1bv':-12,'h2ba':67,'h2bs':42,'h2bv':24,'q0ba':-11,'b1bv':45,'z1aa':-5,'z1ap':-7,'z1av':15,'x2g':-12,'x2s':-2,'x2v':-17,'c2ba':-52,'e0bv':10,'s1bv':10,'x0s':-3,'q0aa':1,'q0ap':1,'z1ba':13,'d2ap':20,'i0ba':9,'i0bg':-3,'i0bp':-2,'i0bv':4,'e2bp':-10,'d0ap':-5,'o1a':33,'c2bp':-12,'c2bv':-35,'k2048ba':9,'k2048bp':-3,'k2048bv':-11,'c0av':17,'e0ap':-21,'z1bp':-4,'z1bv':-14,'g1ap':17,'k1536aa':-5,'k1536ap':-5,'k1536av':5,'z2ap':5,'k1536ba':-1,'k1536bv':-2,'c1aa':20,'c1ap':22,'h2av':35,'q0bp':-11,'q0bv':-1,'o0a':20,'o0v':24,'e0aa':-1,'e0av':-1,'i1aa':-5,'i1ag':-2,'h0bv':21,'h2aa':38,'h2ap':65,'h2as':38,'l1ba':-2,'l1bp':-2,'l0ag':-5,'c1ba':32,'o1v':63,'o1s':18,'k4096aa':-2,'c1bp':22,'b0ba':-14,'h0ba':51,'c0aa':-2,'c0ap':5,'q1bp':-3,'h0aa':-3,'h0ap':-6,'k4096ba':-1,'e2bv':5,'k4096bp':-1,'k4096bv':-1,'h0bs':16,'h0bg':-4,'h0bp':-4,'constg':2,'k2048aa':30,'k2048ap':10,'k2048av':12,'h1ap':23,'s0av':9,'s0aa':-1,'h1av':40,'o1p':40,'g2ba':-20,'b2ba':20,'consta':-1,'d2bp':-12,'b1aa':20,'l0aa':-1,'e0bp':-10}
-
-WIDE = {'e2b':[0,2],'b2a':[1,2]}
-ONACT.update({'s0a':[2],'s0b':[2],'s1a':[0,2,5],'s1b':[0,2,4,6],'e0b':[0],'e1a':[4,5],'e1b':[5,7],'e2a':[0,1,6],'e2b':[0],'z0a':[0,3],'z1a':[1],'z1b':[2],'z2a':[1],'z2b':[0]})
-BIAS = {'c1av':17,'c2av':-21,'q1av':-2,'q2av':6,'q1aa':5,'q2aa':6,'x0v':24,'d1bv':-5,'d0bv':19,'loada':14,'loadg':17,'loads':22,'loadv':14,'q1ap':-20,'g1ba':98,'g1bp':115,'q2ba':18,'q2bp':15,'q2bv':16,'x1g':5,'x1s':2,'q2ap':-31,'s1ap':3,'s0ba':20,'s0bp':20,'s0bv':15,'q1bv':-2,'z2bv':10,'x0g':-6,'s0ap':1,'e2aa':3,'e2ap':-6,'e2av':-12,'i0aa':14,'i0ag':6,'i0av':23,'i1ba':-20,'z0bv':-3,'h1ba':-4,'h1bg':-5,'h1bp':8,'h1bs':-2,'h1bv':-2,'s1aa':14,'s1av':35,'d1bp':4,'e1ap':26,'h0av':54,'g2bp':-7,'z2ba':5,'z2bp':-21,'h2bp':-21,'o0p':31,'e1bp':22,'l2aa':10,'c1bv':60,'e1aa':-2,'c0ba':16,'c0bp':-3,'d1ap':-46,'h1aa':19,'b2av':29,'l1bg':-2,'i1bg':10,'z0ba':-25,'z0bp':-33,'l2ba':7,'l2bg':-20,'l2bp':-10,'g2aa':7,'g2ap':3,'i1bv':-14,'h2ba':-26,'h2bs':-26,'h2bv':-26,'q0ba':-11,'b1bv':45,'z1aa':-5,'z1ap':-7,'z1av':3,'x2v':-10,'c2ba':-43,'e0bv':9,'s1bv':10,'x0s':-1,'q0aa':-6,'z1ba':13,'d2ap':40,'i0ba':9,'i0bp':-2,'i0bv':4,'e2bp':-5,'d0ap':5,'c2bp':-2,'c2bv':-25,'k2048ba':2,'k2048bp':-9,'k2048bv':2,'c0av':20,'e0ap':-19,'z1bv':-14,'g1ap':12,'k1536aa':-4,'k1536ap':-4,'k1536av':-4,'z2ap':26,'k1536ba':-1,'k1536bv':-3,'c1aa':3,'c1ap':27,'h2av':65,'q0bp':-11,'q0bv':-1,'o0a':19,'o0v':23,'e0aa':-1,'e0av':-1,'i1aa':-5,'i1ag':-2,'h0bv':45,'h2aa':63,'h2ap':95,'h2as':88,'l1ba':-7,'l1bp':-7,'l0ag':-5,'c1ba':50,'o1v':20,'k4096aa':-4,'c1bp':40,'b0ba':-19,'h0ba':65,'c0aa':20,'c0ap':20,'q1bp':-4,'h0aa':-3,'h0ap':-6,'k4096ba':-1,'e2bv':4,'k4096bp':-1,'k4096bv':-2,'h0bs':30,'h0bg':32,'h0bp':10,'constg':10,'k2048aa':30,'k2048ap':-2,'k2048av':10,'h1ap':43,'s0av':35,'s0aa':5,'h1av':40,'g2ba':-2,'b2ba':26,'d2bp':-38,'b1aa':10,'l0aa':-1,'e0bp':-13,'x1v':-8,'c2aa':-19,'c2ap':-3,'constp':-2,'i1ap':-2,'b2bv':16,'c0bv':24,'z0aa':4,'z0ap':5,'z0av':7,'e0ba':-1,'d2bv':-11,'z2aa':4,'z2av':3,'l1aa':-1,'b2aa':10,'d2av':-4,'s1ba':-10,'b1ba':-10,'l2ag':10,'l0bg':-1,'k1536bp':-10,'d0bp':-11,'l2ap':8,'q1ba':-5,'k4096ap':-1,'l0ap':10,'l0ba':-1,'l0bp':-1,'i1bp':2}
-if not any(_v for _k, _v in ONACT.items() if _k[0] in "EZ"):
-    SCRATCH.pop("U2")
-    SCRATCH.pop("Un")
+KH = [(0, 4), (4, 8), (8, 12), (12, 16)]
+KC = [KH, KH, KH]
+SPLIT = "sezb"
+PAIR = {}
+MULT = {"h2b": (0, 1, 2, 3)}
+OWNB = ""
+BYMAX = {"s0": True, "s1": False, "e0": True, "e1": False, "e2": False}
+WAYS = {"s0a": "mmmm", "s0b": "mmmm", "e0a": "mmmm", "e0b": "mmmm", "s1a": "dddd", "s1b": "ddpd",
+        "e1a": "pvvv", "e1b": "pvvv", "e2a": "pvvv", "e2b": "pvvv",
+        "z0a": "rrvv", "z0b": "rvvv", "z1a": "rrvv", "z1b": "rrvv", "z2a": "rrvv", "z2b": "rrvv"}
+BIAS = {"w": 300}
 
 
 def ap(name, *idx):
@@ -69,6 +70,10 @@ def ap(name, *idx):
 
 def cols(name, a, b, step=1):
     return (name, (slice(None), slice(a, b, step)))
+
+
+def node(name, a, b):
+    return cols(name, 16 + a, 16 + b)
 
 
 def ind(win, off):
@@ -112,9 +117,8 @@ def _psum(x):
 def build():
     ops = []
     tag = ["load"]
-
-    def enumerate(names):
-        return [(1, names[0]), (0, names[1])]
+    part = [None]
+    halves = [(1, "a"), (0, "b")]
 
     def add(kind, alts, reads, writes, **kw):
         rd, wr = [], []
@@ -127,7 +131,7 @@ def build():
                 rd.append(x[2])
             else:
                 wr.append(x)
-        o = dict(kind=kind, alts=alts, rd=[x for x in rd if x[0] in SCRATCH], wr=[x for x in wr if x[0] in SCRATCH], n=len(ops), tag=tag[0])
+        o = dict(kind=kind, alts=alts, rd=[x for x in rd if x[0] in SCRATCH], wr=[x for x in wr if x[0] in SCRATCH], n=len(ops), tag=tag[0], q=part[0])
         o.update(kw)
         ops.append(o)
         return o
@@ -166,8 +170,12 @@ def build():
     def acp(out, a, flex=True):
         return act(out, a, F.Identity, alt=("cp", out, a) if flex else None)
 
-    def ascale(out, a, col, flex=True):
-        return act(out, a, F.Identity, 0.0, col, alt=("ts", out, a, col, None, A.mult, None) if flex else None)
+    def lin(out, a, scale, bias):
+        return act(out, a, F.Identity, bias, scale, alt=("ts", out, a, scale, bias, A.mult, A.add))
+
+    def put(out, a):
+        return add("c", {"a": (("act", out, a, F.Silu, 0.0, 1.0), ("sca", _size(out))), "v": (("cp", out, a), ("sca", _size(out)))},
+                   [a], [out])
 
     def mm(items):
         cyc, rd, wr = 0, [], []
@@ -184,42 +192,59 @@ def build():
         return add("c", {"g": (("sel", out, a, pat, op, base, mult), ("cyc", 170 + 2 * _size(out)))}, [a], [out])
 
     def gcp(out, a):
-        return sel(out, a, [[0, _size(out)]], A.is_equal, 0, 0)
+        o = sel(out, a, [[0, _size(out)]], A.is_equal, 0, 0)
+        o["alts"]["v"] = (("cp", out, a), vcost(out, [a]))
+        return o
 
     nd = [0]
 
-    def dma(out, a, nbytes, q="s"):
+    def dma(out, a, nbytes, q="s", after=()):
         nd[0] += 1
-        return add("d", {q: (("dma", out, a), ("dma", nbytes))}, [a], [out], sem="d%d" % (nd[0] - 1))
+        return add("d", {q: (("dma", out, a), ("dma", nbytes))}, [a] + list(after), [out], sem="d%d" % (nd[0] - 1))
+
+    def dadd(out, a, nbytes):
+        nd[0] += 1
+        return add("d", {"g": (("dma", out, a, True), ("dma", 2 * nbytes))}, [a, out], [out], sem="d%d" % (nd[0] - 1))
 
     def remote(out, a, nbytes, hop, k):
         return add("r", {"g": (("rem", out, a, hop, k), ("dma", nbytes))}, [a], [out], sem="arr%d" % k)
 
     S = slice
     AL = S(None)
-    lent = {"kf": ("vfa", 0, 96), "kr": ("vfa", 96, 192), "bsf": ("vfa", 192, 288), "of": ("vfa", 288, 448), "orr": ("vfa", 448, 608),
-            "iw": ("vfa", 608, 672), "iy": ("vfa", 672, 736), "kb": ("loa", 0, 96), "ob": ("loa", 96, 256)}
+    lent = {"k32": ("vfa", 0, 96), "bsf": ("vfa", 192, 288), "of": ("vfa", 288, 448), "orr": ("vfa", 448, 608),
+            "oh": ("vfa", 608, 768), "o32": ("vfa", 768, 928), "kb": ("nta", 0, 96), "kr": ("nta", 96, 192), "ob": ("nta", 192, 352), "t2": ("lob", 0, 512)}
+    lent.update(bh=("nta", 352, 448), bl=("nta", 448, 544), K1a=("zca", 0, 256), K1b=("zcb", 0, 256))
     full = lambda n: cols(*lent[n]) if n in lent else ap(n, AL)
 
-    dma(cols("sni", 0, 768), ap("sn", AL, S(0, 768)), 393216)
     dma(full("kidc"), ap("kid", AL), 49152)
-    dma(cols("Vb", 0, 1536), ap("vn", AL), 393216, "a")
-    dma(full("Zb"), ap("zs", AL), 393216, "a")
+    dma(node("Vb", 0, 1536), ap("vn", AL), 393216, "a")
     dma(cols("sni", 768, 1536), ap("sn", AL, S(768, 1536)), 393216)
+    dma(full("Zb"), ap("zs", AL), 393216, "a")
+    dma(cols("sni", 0, 768), ap("sn", AL, S(0, 768)), 393216)
     dma(full("bsc"), ap("bst", AL), 49152)
-    for j in range(2):
-        dma(full("nqi"), ap("nq", AL, S(768 * j, 768 * j + 768)), 393216)
-        cp(cols("Qt", 768 * j, 768 * j + 768), full("nqi"))
+    for j in range(6):
+        stage = full(["Mca", "Mcb", "Ma", "Mb"][j % 4])
+        dma(stage, ap("nq", AL, S(256 * j, 256 * j + 256)), 131072, after=[full("Zb")])
+        cp(cols("Qt", 256 * j, 256 * j + 256), stage)
 
     ci = lambda j: cols("ci", j, j + 1)
     cf = lambda j: cols("cf", j, j + 1)
     iota(ci(0), [[0, 1]], 0, 1)
+    iota(ci(5), [[0, 1]], 13, 1)
+    iota(ci(8), [[0, 1]], 15, 1)
     iota(full("xi"), [[1, 160]], 0, 0)
+    iota(full("xl"), [[1, 4], [4, 4]], 0, 0)
+    iota(full("kbb"), [[8192, 4], [0, 64]], 0, 0)
     ts(ci(1), ci(0), 15, None, A.bitwise_and)
     ts(ci(2), ci(0), 4, 1, A.logical_shift_right, A.bitwise_and)
     ts(ci(3), ci(0), 7, None, A.bitwise_and)
     ts(ci(4), ci(0), 8, None, A.bitwise_and)
-    P16, G16, G15, P, PP16, M0, M1, MC, WA, DUM, PM, T16, S15, OWN, TMP = [cf(j) for j in range(15)]
+    ts(ci(5), ci(5), 15, 2, A.bitwise_and, A.logical_shift_right)
+    ts(ci(8), ci(8), 15, 1, A.bitwise_and, A.logical_shift_right)
+    ts(ci(6), ci(0), 2, 3, A.logical_shift_right, A.bitwise_and)
+    ts(ci(7), ci(0), 3, None, A.bitwise_and)
+    (P16, G16, G15, P, PP16, M0, M1, IB, WA, DUM, PM, T16, S15, OWN, TMP,
+     WE, WS, TN, TA, T7, T8, H8, B126, TM2, TM3) = [cf(j) for j in range(25)]
     ts(PP16, ci(0), 16.0, None, A.add)
     ts(M0, ci(2), -1.0, 1.0, A.mult, A.add)
     cp(M1, ci(2))
@@ -227,28 +252,75 @@ def build():
     ts(full("IW1"), full("xi"), PP16, M1, A.is_equal, A.mult)
     ts(TMP, ci(3), 32.0, None, A.mult)
     ts(PM, ci(4), 2.0, TMP, A.mult, A.add)
-    ts(full("OP"), cols("xi", 0, 16), PM, None, A.add)
+    ts(full("OP"), full("xl"), PM, None, A.add)
     cp(P16, ci(1))
     cp(P, ci(0))
-    tt(G16, P, P16, A.subtract)
+    ts(G16, ci(1), -1.0, P, A.mult, A.add)
     ts(G15, G16, 15.0, None, A.add)
-    ts(WA, P16, 2.0, None, A.is_lt)
-    ts(full("U"), cols("xi", 0, 144), G15, K14, A.is_equal, A.mult)
-    ts(full("Ua"), cols("xi", 0, 144), G15, WA, A.is_equal, A.mult)
-    if any(v for k, v in ONACT.items() if k[0] in "EZ"):
-        ts(full("U2"), cols("xi", 0, 144), G15, 2 * K14, A.is_equal, A.mult)
-        ts(full("Un"), cols("xi", 0, 144), G15, -K14, A.is_equal, A.mult)
-    ts(full("idf"), cols("xi", 0, 128), P, None, A.is_equal)
-    ts(full("idb"), cols("xi", 0, 128), P, None, A.is_equal)
-    ts(full("nid"), cols("xi", 0, 128), P, -1.0, A.is_equal, A.mult)
-    ms(cols("CH", 0, 1536), 0.0)
-    cp(full("kf"), full("kidc"))
-    cp(full("kb"), full("kf"))
-    tt(full("kr"), full("kf"), full("kb"), A.subtract)
-    dma(ap("CH", S(0, 128, 16), S(0, 1536)), full("kf"), 49152)
-    dma(ap("CH", S(1, 128, 16), S(0, 1536)), full("kr"), 49152, "a")
+    ts(WA, ci(8), 0.0, None, A.is_equal)
+    ts(WS, ci(5), 1.0, K, A.is_equal, A.mult)
+    ts(TM2, ci(5), 0.0, K, A.is_equal, A.mult)
+    ts(WE, TM2, WA, None, A.add)
+    ts(TN, ci(6), G16, 3.0, A.add, A.add)
+    ts(TA, TN, 4.0, None, A.add)
+    ts(T7, ci(3), 16.0, None, A.mult)
+    ts(H8, ci(4), 0.125, 1.0, A.mult, A.add)
+    ts(T8, ci(3), 16.0, H8, A.mult, A.add)
+    ts(DUM, P16, 2.5, 126.0, A.is_gt, A.mult)
+    ts(TM3, P16, 0.0, -32.0, A.is_equal, A.mult)
+    ts(B126, DUM, TM3, None, A.add)
+    x128, x144 = cols("xi", 0, 128), cols("xi", 0, 144)
+    ts(full("Wn"), x128, TN, -1.0, A.is_equal, A.mult)
+    ts(full("Wa"), x128, TA, -1.0, A.is_equal, A.mult)
+    ts(full("idB"), x128, T8, None, A.is_equal)
+    ts(full("nid"), x128, T7, None, A.is_equal)
+    tt(full("Wk"), full("nid"), full("idB"), A.add)
+    ts(full("U2"), x144, G15, 2 * K, A.is_equal, A.mult)
+    ts(full("U"), x144, G15, K, A.is_equal, A.mult)
+    ts(full("Un"), x144, G15, -K, A.is_equal, A.mult)
+    ts(full("Ue"), x144, G15, WE, A.is_equal, A.mult)
+    ts(full("Us"), x144, G15, WS, A.is_equal, A.mult)
+    if not all(BYMAX["e%d" % t] for t in range(3)):
+        ts(full("Ua"), x144, G15, WA, A.is_equal, A.mult)
+    ts(full("idf"), x128, P, None, A.is_equal)
+    ts(full("idb"), x128, P, None, A.is_equal)
+    ts(full("nid"), x128, P, -1.0, A.is_equal, A.mult)
+    ts(full("idB"), x128, P, 2.0 ** 26, A.is_equal, A.mult)
+    ts(full("OB"), cols("xi", 0, 16), 0.0, P16, A.mult, A.add)
     P00, P10, Pa, Pb = cols("IW0", 16, 144), cols("IW0", 0, 128), cols("IW1", 32, 160), cols("IW1", 16, 144)
     Ur = lambda n, r: cols(n, 15 - r, 143 - r)
+
+    tag[0] = "w"
+    iota(full("gx"), [[16, 8], [0, 16]], 0, 0)
+    ts(full("gx"), full("gx"), G16, 128.0, A.is_equal, A.mult)
+    ts(cols("rm", 0, 16), cols("xi", 0, 16), P16, None, A.is_equal)
+    ts(cols("rm", 16, 32), cols("xi", 0, 16), P16, None, A.is_gt)
+    for r in range(16):
+        act(cols("Wb", 128 * r, 128 * r + 128), full("gx"), F.Identity, 0.0, cols("rm", r, r + 1))
+        act(cols("Wt", 128 * r, 128 * r + 128), Ur("U", r), F.Identity, 0.0, cols("rm", 16 + r, 17 + r))
+
+    tag[0] = "table"
+    cp(full("iu"), full("kidc"))
+    cp(full("kb"), full("kidc"))
+    ts(full("k32"), full("kidc"), 32.0, None, A.add)
+    tt(full("kr"), full("k32"), full("kb"), A.subtract)
+    dma(ap("XS", S(0, 8), S(1536, 3072)), full("kb"), 24576)
+    dma(ap("XS", S(8, 16), S(1536, 3072)), full("kr"), 24576, "a")
+    acp(cols("XS", 0, 1536), ind(node("Vb", 0, 1536), full("iu")))
+    for j, bank in enumerate(["PE0", "PE1", "PXb"]):
+        lo, hi = 512 * j, 512 * j + 512
+        it = [(full(bank), full("Wa"), node("Vb", lo, hi), True, False)]
+        for p in range(16):
+            a, b = max(lo, 96 * p), min(hi, 96 * p + 96)
+            if a < b:
+                it.append((cols(bank, a - lo, b - lo), full("Wn"), cols("XS", 16 * (a - 96 * p) + p, 16 * (b - 96 * p), 16), False, False))
+        it.append((full(bank), ap("Wk", S(0, 16), AL), ap("XS", S(0, 16), S(1536 + lo, 1536 + hi)), False, True))
+        mm(it)
+        lin(node("CH", lo, hi), full(bank), 1.0, B126)
+    for tile in range(2):
+        o = cols("PM", 32 * tile, 32 * tile + 32)
+        mm([(o, Ur("U", r), cols("Zb", tile + 3 * r, 1536, 48), r == 0, r == 15) for r in range(16)])
+    lin(full("z16"), cols("PM", 0, 64), -1.0, -1016.0 * K)
 
     def k2l(x, c):
         n, lo = x
@@ -262,9 +334,9 @@ def build():
     def s_in(tile, c, ch):
         tag[0] = "i%d%s" % (tile, c)
         cp(full("f1" + c), cols("sni", 768 * ch + tile, 768 * ch + 768, 3))
-        w = k2l(("f1" + c, 0), c)
-        act(full("sf" + c), w, F.Identity, K14, alt=("ts", full("sf" + c), w, K14, None, A.add, None))
-        ts(cols("su" + c, 256 * tile, 256 * tile + 256), full("sf" + c), -K14, None, A.add)
+        off = 0.0 if BYMAX["s%d" % tile] else -512.0 * K
+        lin(full("sf" + c), k2l(("f1" + c, 0), c), 1.0, off)
+        ts(cols("su" + c, 256 * tile, 256 * tile + 256), full("sf" + c), -off, None, A.add)
 
     def z_in(tile, ch):
         o = 2048 * tile + 1024 * ch
@@ -272,128 +344,170 @@ def build():
         gcp(cols("zr", o + 256, o + 512), cols("Zb", 768 * ch + tile, 768 * ch + 768, 3))
         gcp(cols("zr", o + 512, o + 1024), cols("zr", o, o + 512))
 
+    def z_sum(tile, c, ch):
+        o = 32 * tile + 16 * ch
+        tt(full("zc" + c), ind(cols("z16", o, o + 16), full("OB")), full("kbb"), A.add)
+
     def psl(bank, a, b, step=1):
         if bank.startswith("PY"):
             assert step == 1
             return ap(bank, AL, S(a // 32, b // 32), AL, AL)
         return cols(bank, a, b, step)
 
-    def diag(bank, o, fam, X, first, relu=(), raw=None, pos=None):
-        ks = KS if not (0 in relu or 1 in relu) else [(0, 4), (4, 8), (8, 12), (12, 16)]
-        for k0, k1 in ks:
+    def rows(x, k0, k1, r=None):
+        if x.startswith("sg"):
+            return ap(x, AL, S(16 * k0, 16 * k1), AL if r is None else r)
+        return cols(x, 256 * k0, 256 * k1) if r is None else cols(x, 256 * k0 + r, 256 * k1, 16)
+
+    def diag(bank, o, terms, first, last=None, after=None):
+        terms = terms if isinstance(terms, dict) else dict((q, terms) for q in range(4))
+        for k0, k1 in KS if terms[0] == terms[1] and not after else KH:
+            part[0] = (k1 - 1) // 4
             out = psl(bank, o + 16 * k0, o + 16 * k1)
-            src = [(fam, X)] if k0 // 4 not in relu else [("Un", raw), ("U2", pos)]
-            mm([(out, Ur(f, r), cols(x, 256 * k0 + r, 256 * k1, 16), first and r == 0 and j == 0,
-                 r == 15 and j == len(src) - 1 and (first or k1 == 16)) for j, (f, x) in zip(range(2), src) for r in range(16)])
+            it = [[out, Ur(f, r), rows(x, k0, k1, r), False, False] for f, x in terms[k0 // 4] for r in range(16)]
+            if last:
+                it.append([out, full("idf"), cols(last, 16 * k0, 16 * k1), False, False])
+            it[0][3] = first
+            it[-1][4] = first or k1 == 16
+            mm([tuple(x) for x in it])
+            if after:
+                after(16 * k0, 16 * k1)
+        part[0] = None
 
     flip = [0]
 
-    def dist(X, win, off, o, other, oo, on_act, XO=None, relu=(), pos=None):
-        done = []
+    def spare():
+        flip[0] = (flip[0] + 1) % 3
+        return "PE%d" % flip[0]
+
+    def dist(X, win, off, o, other, oo, XO=None, XR=None):
         XO = XO or X
-        for k in range(0, 16, 2):
-            x = cols(X, 256 * k, 256 * k + 512)
-            w = ind(win, cols(off, o + 16 * k, o + 16 * k + 32))
-            z = cols(other, oo, oo + 512)
-            if k // 4 in WIDE.get(tag[0], (0, 1, 2)) and k // 4 * 2 not in on_act and k // 4 * 2 + 1 not in on_act:
-                if k % 4 == 0:
-                    x = cols(X, 256 * k, 256 * k + 1024)
-                    tt(x, ind(win, cols(off, o + 16 * k, o + 16 * k + 64)), cols(other, oo, oo + 1024), A.subtract)
-                    if k // 4 in relu:
-                        ts(cols(pos, 256 * k, 256 * k + 1024), x, 0.0, None, A.max)
-                    else:
-                        act(cols(XO, 256 * k, 256 * k + 1024), x, F.Abs)
-            elif k // 4 in relu:
-                tt(x, w, z, A.subtract)
-                ts(cols(pos, 256 * k, 256 * k + 512), x, 0.0, None, A.max)
-            elif k // 2 in on_act:
-                E = full("PE%d" % flip[0])
-                flip[0] ^= 1
-                acp(x, w, False)
-                mm([(E, full("idb"), x, True, False), (E, full("nid"), z, False, True)])
-                act(cols(XO, 256 * k, 256 * k + 512), E, F.Abs)
-            else:
-                tt(x, w, z, A.subtract)
-                done.append(k)
-                if k % 4 == 2 or k // 2 + 1 in on_act or k >= 12:
-                    act(cols(XO, 256 * done[0], 256 * k + 512), cols(X, 256 * done[0], 256 * k + 512), F.Abs)
-                    done = []
+        terms = {}
+        for q, way in zip(range(4), WAYS.get(tag[0], "vvvv")):
+            n = 2 if way == "p" or (q == 3 and way in "vmw" and tag[0][0] in SPLIT) else 4
+            part[0] = q
+            for k in range(4 * q, 4 * q + 4, n):
+                x = cols(X, 256 * k, 256 * (k + n))
+                w = ind(win, cols(off, o + 16 * k, o + 16 * (k + n)))
+                z = cols(other, oo, oo + 256 * n)
+                if way == "m":
+                    tt(x, w, z, A.max)
+                    continue
+                if way in "dr":
+                    act(x, w, F.Identity, 0.0, -1.0)
+                    dadd(x, z, 262144)
+                elif way == "p":
+                    acp(x, w, False)
+                    E = full(spare())
+                    mm([(E, full("idb"), x, True, False), (E, full("nid"), z, False, True)])
+                    x = E
+                else:
+                    tt(x, w, z, A.subtract)
+                if way in "rw":
+                    ts(rows(XR, k, k + n), x, 0.0, None, A.max)
+                else:
+                    act(cols(XO, 256 * k, 256 * (k + n)), x, F.Abs)
+            terms[q] = [("U2", X)] if way == "m" else [("U2", XR), ("Un", X)] if way in "rw" else [("U", XO)]
+        part[0] = None
+        return terms
 
-    def ds_pass(tile, c, ch, bank, o, X):
+    def s_pass(tile, c, ch, X):
         tag[0] = "s%d%s" % (tile, c)
-        dist(X, cols("Vb", 0, 1536), "su" + c, 256 * tile, "zr", 2048 * tile + 1024 * ch, ONACT["s%d%s" % (tile, c)])
-        mm([(psl(bank, o, o + 256), full("idf"), full("sf" + c), True, False)])
-        diag(bank, o, "U", X, False)
-        acp(full("Ks" + c), psl(bank, o, o + 256))
+        mx = BYMAX["s%d" % tile]
+        o = 256 * ch
+        out = psl("PM", o, o + 256)
+        terms = dist(X, node("Vb", 0, 1536), "su" + c, 256 * tile, "zr", 2048 * tile + 1024 * ch, None, "sgb")
+        if not mx:
+            mm([(out, full("idb"), full("kbb"), True, False)])
+            diag("PM", o, terms, False, "sf" + c)
+        elif tile == 0:
+            mm([(out, full("idf"), full("zc" + c), True, False)])
+            diag("PM", o, [("U2", X), ("Us", "XA" + c)], False, "sf" + c)
+        else:
+            z_sum(1, c, ch)
+            mm([(out, full("idf"), full("zc" + c), True, False)])
+            diag("PM", o, [("U2", X)], False)
+        acp(full(["Ks", "K1"][tile] + c), out)
 
-    def child_pass(c, so, hi, bank, o):
-        tag[0] = "k%d%s" % (hi, c)
-        for k in range(0, 16, 2):
-            acp(cols("XA" + c, 256 * k, 256 * k + 512), ind(cols("CH", 0, hi), cols("su" + c, so + 16 * k, so + 16 * k + 32)))
-        diag(bank, o, "Ua", "XA" + c, True)
-        cp(full("eu" + c), psl(bank, o, o + 256))
-        act(full("ef" + c), psl(bank, o, o + 256), F.Identity, K14 + 4096.0,
-            alt=("ts", full("ef" + c), psl(bank, o, o + 256), K14 + 4096.0, None, A.add, None))
+    def child_pass(t, c, ch, so, hi, bank, o):
+        tag[0] = "k%d%s" % (t, c)
+        mx = BYMAX["e%d" % t]
+        for k0, k1 in KC[t]:
+            part[0] = k0 // 4
+            acp(rows("XA" + c, k0, k1), ind(node("CH", 0, hi), cols("su" + c, so + 16 * k0, so + 16 * k1)))
+        Y = psl(bank, o, o + 256)
+        diag(bank, o, [("Ue" if mx else "Ua", "XA" + c)], True)
+        if mx:
+            ts(full("M2" + c), Y, -32.0, None, A.add)
+            ts(full("M2" + c), full("M2" + c), 4095, None, A.bitwise_and)
+            cp(full("eu" + c), full("M2" + c))
+        else:
+            ts(full("eu" + c), Y, -32.0, None, A.add)
+        lin(full("ef" + c), Y, 1.0, 4064.0 if mx else 4064.0 - 512.0 * K)
+        if t == 1 and BYMAX["s1"]:
+            E = spare()
+            mm([(cols(E, 0, 256), full("idf"), full("K1" + c), True, False)])
+            diag(E, 0, [("Us", "XA" + c)], False, "sf" + c)
+            acp(full("K1" + c), cols(E, 0, 256))
 
-    def vb_update(tile, v0, n, off, t2):
-        bt = cols("Bt", v0 + tile, v0 + 3 * n, 3)
-        acp(bt, ind(full("IO"), off))
-        ascale(t2, bt, MC)
-        tt(cols("VB", v0 + tile, v0 + 3 * n, 3), ind(full("Vb"), off), t2, A.add)
-        return bt
-
-    for ch, c in enumerate("ab"):
+    for ch, c in halves:
         s_in(0, c, ch)
         z_in(0, ch)
-        child_pass(c, 0, 1536, "PY" + c, 256)
-        ds_pass(0, c, ch, "PM", 256 * ch, "XZ" + c)
-    for ch, c in enumerate("ab"):
+        z_sum(0, c, ch)
+        child_pass(0, c, ch, 0, 1536, "PX" + c, 256)
+        s_pass(0, c, ch, "XZ" + c)
+    for ch, c in halves:
         s_in(1, c, ch)
         z_in(1, ch)
 
     tag[0] = "const"
-    iota(cols("IO", 0, 4096), [[1, 4096]], 0, 0)
-    ms(cols("IO", 4096, 4112), -1.0)
-    iota(cols("Vb", 1536, 4096), [[0, 2560]], 0, 0)
-    ms(cols("Vb", 4096, 4112), 200.0)
-    iota(cols("it2", 0, 256), [[1024, 16], [0, 16]], 0, 0)
-    iota(cols("it2", 256, 512), [[0, 4], [4096, 4], [0, 16]], 0, 0)
+    iota(cols("IO", 0, 1552), [[1, 1552]], -16, 0)
+    iota(node("IO", 1536, 4096), [[1, 2560]], 1536, 0)
+    iota(node("Vb", 2048, 3072), [[0, 1024]], 0, 0)
+    ms(cols("Vb", 0, 16), 200.0)
+    iota(cols("it2", 0, 256), [[2048, 4], [8192, 4], [0, 16]], 0, 0)
     iota(full("xl"), [[1, 8], [8, 2]], 0, 0)
-    iota(full("gid"), [[16, 64]], 16384 + 8192 + 3072, 0)
-    iota(cols("CH", 1536, 4112), [[1, 2576]], 1536, 0)
-    iota(cols("Qt", 1536, 4096), [[0, 2560]], 0, 0)
-    acp(full("PK"), full("it2"))
-    ts(MC, P16, 0.0, 1.0 / K14, A.is_equal, A.mult)
-    ts(DUM, P16, 4096.0, None, A.add)
-    ts(T16, P16, 16.0, None, A.mult)
-    ts(S15, P, 16.0, 15.0, A.mult, A.add)
+    iota(full("gid"), [[16, 64]], int(-512 * K) + 4096 + 3072, 0)
+    iota(node("CH", 1536, 4096), [[0, 2560]], 126, 0)
+    iota(cols("Qt", 2048, 3072), [[0, 1024]], 0, 0)
+    for ch, c in halves:
+        acp(psl("PY" + c, 256, 512), cols("it2", 0, 256))
+    ts(IB, P16, -2048.0, 2.0 ** -18, A.add, A.mult)
+    ts(TMP, ci(6), 16.0, None, A.mult)
+    ts(T16, ci(7), 64.0, TMP, A.mult, A.add)
+    ts(S15, T7, 15.0, None, A.add)
     ts(OWN, P16, 160.0, 1536.0, A.mult, A.add)
     ts(full("gid"), full("gid"), P16, None, A.add)
-    ts(full("SL"), cols("xi", 0, 144), S15, None, A.is_equal)
-    ts(full("OB"), cols("xi", 0, 16), 0.0, P16, A.mult, A.add)
+    ts(full("SL"), x144, S15, None, A.is_equal)
     cp(full("OE"), cols("xi", 0, 16))
     ts(full("OL"), full("xl"), T16, None, A.add)
-    iota(full("Wb"), [[0, 2048]], 128, 0)
-    sel(full("Wt"), full("Wb"), [[-1, 16], [0, 8], [1, 16]], A.is_equal, 0, 0)
-    sel(full("Wt"), full("Wt"), [[0, 16], [-16, 8], [0, 16]], A.is_ge, 0, 1)
-    sel(full("Wt"), full("Wt"), [[1, 16], [16, 8], [0, 16]], A.is_gt, 0, -1)
-    sel(full("Wb"), full("Wb"), [[-1, 16], [-16, 8], [0, 16]], A.is_equal, 0, 1)
     ts(full("of"), full("xi"), OWN, None, A.add)
     cp(full("ob"), full("of"))
-    tt(full("orr"), full("of"), full("ob"), A.subtract)
-    dma(ap("CH", S(1, 128, 16), S(1536, 4096)), full("orr"), 81920)
+    acp(full("oh"), full("ob"))
+    lin(full("o32"), full("of"), 1.0, 32.0)
+    tt(full("orr"), full("o32"), full("ob"), A.subtract)
+    for row, x in enumerate(["of", "oh", "orr"]):
+        dma(ap("CH", S(row, 128, 16), S(1552, 4112)), full(x), 81920)
     cp(full("bsf"), full("bsc"))
-    dma(ap("Bt", S(0, 8), AL), full("bsf"), 49152)
+    dma(ap("Bt", S(0, 128, 16), AL), full("bsf"), 49152)
+    cp(full("bh"), full("bsc"))
+    tt(full("bl"), full("bsc"), full("bh"), A.subtract)
+    dma(ap("sga", S(0, 8), S(0, 96), AL), full("bh"), 24576)
+    dma(ap("sga", S(8, 16), S(0, 96), AL), full("bl"), 24576)
+    it = []
+    for r in range(16):
+        v = 3 * r + 1
+        for j, n in [(0, 2)] if v % 16 < 15 else [(0, 1), (1, 1)]:
+            it.append((cols("PE2", j, 64, 3 - n), ap("SL", S(0, 16), S(15 - r, 143 - r)),
+                       ap("sga", S(0, 16), S((v + j) // 16, 96, 3), S((v + j) % 16, (v + j) % 16 + n)), r == 0, r == 15))
+    mm(it)
     for j in range(2):
-        mm([(cols("PE0", 32 * j, 32 * j + 32), ap("SL", S(0, 8), S(15 - r, 143 - r)), ap("Bt", S(0, 8), S(1 + j + 3 * r, 1536, 48)),
-             r == 0, r == 15) for r in range(16)])
-    ts(full("iw"), cols("PE0", 0, 64), 0.0, 4097.0, A.is_lt, A.mult)
-    tt(full("iy"), cols("PE0", 0, 64), full("iw"), A.add)
-    cp(full("iu"), full("iy"))
-    for j in range(2):
-        vb_update(1 + j, 0, 512, cols("iu", 32 * j, 32 * j + 32), full("it2"))
+        off = cols("iu", 32 * j, 32 * j + 32)
+        ts(off, cols("PE2", j, 64, 2), 16.0, None, A.add)
+        lin(full("t2"), ind(cols("IO", 0, 1552), off), 2.0 ** -18, IB)
+        tt(cols("VB", 1 + j, 1536, 3), ind(cols("Vb", 0, 1552), off), full("t2"), A.add)
     s4, pk = cols("it2", 0, 256), cols("it2", 256, 512)
-    ascale(s4, cols("sni", 770, 1536, 3), 4096.0)["alts"].pop("a")
+    ts(s4, cols("sni", 770, 1536, 3), 4096.0, None, A.mult)
     tt(cols("YS", 2, 768, 3), s4, cols("sni", 2, 768, 3), A.add)
 
     def s_out(tile):
@@ -407,185 +521,232 @@ def build():
             (cols("PM", 128, 256), Pa, y0, True, False), (cols("PM", 128, 256), Pb, y1, False, True)])
         acp(cols("YS", tile, 768, 3), cols("PM", 0, 256))
 
+    def children(t, c, ch):
+        tag[0] = "x%d%s" % (t, c)
+        new0 = 1536 + 512 * t + 256 * ch
+        terms = []
+        if t == 0 and BYMAX["s1"]:
+            terms.append(("Wa", cols("va" + c, 0, 256)))
+        if t < 2 and BYMAX["e%d" % (t + 1)]:
+            terms.append(("Wn", node("Vb", new0, new0 + 256)))
+        sc = cols("SC", 256 * ch, 256 * ch + 256)
+        if terms:
+            x2 = cols("PX" + c, 256, 512)
+            mm([(x2, full(w), x, j == 0, j == len(terms) - 1) for j, (w, x) in enumerate(terms)])
+            tt(sc, x2, sc, A.add)
+        for m in range(15, -1, -1):
+            o = 256 * ch + 16 * m
+            put(ind(cols("CH", 0, 16 + PARENTS[t]), cols("au" + c, 32 + 2 * m, 33 + 2 * m)), cols("SC", o, o + 16))
+
     for t in range(3):
         tile = TILE[t]
         new0 = 1536 + 512 * t
-        for ch, c in enumerate("ab"):
+        late = t < 2 and BYMAX["e%d" % (t + 1)]
+        for ch, c in halves:
             X, Y = "PX" + c, "PY" + c
             zo = 2048 * tile + 1024 * ch
             tag[0] = "e%d%s" % (t, c)
-            mm([(cols(X, 0, 256), full("idf"), full("ef" + c), True, False)])
-            dist("XE" + c, cols("Vb", 0, [1536, 2048, 3584][t]), "eu" + c, 0, "zr", zo, ONACT["e%d%s" % (t, c)],
-                 None, ONACT["E%d%s" % (t, c)], "XA" + c)
-            diag(X, 0, "U", "XE" + c, False, ONACT["E%d%s" % (t, c)], "XE" + c, "XA" + c)
-            if t > 0:
+            mx = BYMAX["e%d" % t]
+            if mx:
+                mm([(cols(X, 0, 256), full("idf"), full("zc" + c), True, False)])
+            else:
+                mm([(cols(X, 0, 256), full("idb"), full("kbb"), True, False)])
+            terms = dist("XE" + c, node("Vb", 0, [1536, 2048, 3584][t]), "eu" + c, 0, "zr", zo, None, "XA" + c)
+            diag(X, 0, terms, False, "ef" + c)
+            if t == 0:
+                s_pass(1, c, ch, "XS")
+            else:
                 tag[0] = "g%d%s" % (t, c)
                 gv = cols("GV%d" % (t - 1), 256 * ch, 256 * ch + 256)
-                yl, yh = psl(Y, 0, 256), psl(Y, 256, 512)
+                E = spare()
+                yh = cols(E, 0, 256)
                 mm([(yh, full("idb"), gv, True, False), (yh, full("nid"), cols("zr", zo, zo + 256), False, True)])
                 act(cols("nt" + c, 0, 256), yh, F.Abs)
                 go = 32 * (t - 1) + 16 * ch
-                g16 = ap(Y, AL, 8, 0, AL)
+                g16 = cols(E, 256, 272)
                 mm([(g16, full("idf"), cols("gid", go, go + 16), True, False)] +
                    [(g16, Ur("U", r), cols("nt" + c, r, 256, 16), False, r == 15) for r in range(16)])
                 acp(cols("tf" + c, 0, 16), g16)
                 acp(full("t1" + c), ind(cols("tf" + c, 0, 16), full("OB")))
-                acp(yl, full("t1" + c))
-        for ch, c in enumerate("ab"):
+        for ch, c in halves:
             X, Y = "PX" + c, "PY" + c
             yl = psl(Y, 0, 256)
             tag[0] = "c%d%s" % (t, c)
-            ks = full(("Ks" if t < 2 else "Mc") + c)
-            tt(full("M" + c), cols(X, 0, 256), ks, A.min)
+            tt(full("M" + c), cols(X, 0, 256), full(["Ks", "K1", "Mc"][t] + c), A.min)
             last = "M" + c
             if t > 0:
-                ts(full("M2" + c), full("M" + c), 0xFFC000, None, A.bitwise_and)
-                tt(full("f1" + c), full("M2" + c), cols("PK", 0, 256), A.subtract)
-                tt(cols("f2" + c, 0, 128), cols("f1" + c, 0, 128), cols("f1" + c, 128, 256), A.max)
-                tt(cols("f2" + c, 128, 192), cols("f2" + c, 0, 64), cols("f2" + c, 64, 128), A.max)
-                tt(cols("f2" + c, 192, 224), cols("f2" + c, 128, 160), cols("f2" + c, 160, 192), A.max)
-                tt(cols("f2" + c, 224, 240), cols("f2" + c, 192, 208), cols("f2" + c, 208, 224), A.max)
-                ts(cols("tf" + c, 16, 32), cols("f2" + c, 224, 240), 1.0, None, A.add)
-                tt(full("t1" + c), ind(cols("tf" + c, 16, 32), full("OB")), full("f1" + c), A.subtract)
-                tt(yl, yl, full("t1" + c), A.mult)
+                f1, f2 = "f1" + c, "f2" + c
+                ts(full("M2" + c), full("M" + c), -32768, None, A.bitwise_and)
+                tt(full(f1), full("M2" + c), psl(Y, 256, 512), A.subtract)
+                mm([(yl, full("idf"), full("t1" + c), True, False), (yl, full("idb"), full("kbb"), False, False)])
+                tt(cols(f2, 0, 128), cols(f1, 0, 128), cols(f1, 128, 256), A.max)
+                tt(cols(f2, 128, 192), cols(f2, 0, 64), cols(f2, 64, 128), A.max)
+                tt(cols(f2, 192, 224), cols(f2, 128, 160), cols(f2, 160, 192), A.max)
+                tt(cols("tf" + c, 16, 32), cols(f2, 192, 208), cols(f2, 208, 224), A.max)
+                tt(cols("nt" + c, 0, 256), ind(cols("tf" + c, 16, 32), full("OB")), full(f1), A.is_gt)
+                mm([(yl, full("idB"), cols("nt" + c, 0, 256), False, True)])
                 tt(full("M2" + c), yl, full("M" + c), A.min)
                 last = "M2" + c
-            Mc, A1, L1, L2, L3 = ["%s%s" % (x, c) for x in ("Mc", "A1", "L1", "L2", "L3")]
-            ts(full(Mc), full(last), 0xFFCFFF, None, A.bitwise_and)
-            tt(full(A1), full(Mc), cols("PK", 256, 512), A.add)
-            tt(full(L1), ap(A1, AL, S(0, 16, 2), AL), ap(A1, AL, S(1, 16, 2), AL), A.min)
-            tt(full(L2), ap(L1, AL, S(0, 8, 2), AL), ap(L1, AL, S(1, 8, 2), AL), A.min)
-            ts(full(L2), full(L2), 0xFFCFFF, None, A.bitwise_and)
-            tt(ap(L3, AL, S(0, 4), AL), full(L2), cols("PK", 256, 320), A.add)
-            tt(ap(L3, AL, S(4, 6), AL), ap(L3, AL, S(0, 4, 2), AL), ap(L3, AL, S(1, 4, 2), AL), A.min)
-            tt(cols("ti" + c, 0, 16), ap(L3, AL, 4, AL), ap(L3, AL, 5, AL), A.min)
+            L1, L2, L3 = ["%s%s" % (x, c) for x in ("L1", "L2", "L3")]
+            tt(full(L1), cols(last, 0, 128), cols(last, 128, 256), A.min)
+            tt(full(L2), cols(L1, 0, 64), cols(L1, 64, 128), A.min)
+            ts(full(L2), full(L2), -28673, None, A.bitwise_and)
+            tt(cols(L3, 0, 64), full(L2), psl(Y, 256, 320), A.add)
+            tt(cols(L3, 64, 96), cols(L3, 0, 32), cols(L3, 32, 64), A.min)
+            tt(cols("ti" + c, 0, 16), cols(L3, 64, 80), cols(L3, 80, 96), A.min)
             a32 = cols("ti" + c, 16, 32)
             ts(a32, cols("ti" + c, 0, 16), 4095, None, A.bitwise_and)
             au, a2u = cols("au" + c, 0, 16), cols("au" + c, 16, 32)
             cp(au, a32)
-            act(cols("nt" + c, 256, 512), full(A1), F.Sign, 0.5 - 201.0 * K14)
-            mm([(cols(X, 256, 272), full("idb"), cols("nt" + c, 256 + 16 * k, 272 + 16 * k), k == 0, k == 15) for k in range(16)])
-            dd, yy, a2f, w1, w2 = [cols("tf" + c, 16 * j, 16 * j + 16) for j in range(2, 7)]
-            ts(dd, cols(X, 256, 272), -15.5, 8192.0, A.is_lt, A.mult)
-            tt(yy, a32, dd, A.add)
-            ts(a2u, yy, 4096.0, None, A.min)
-            ts(a2f, yy, 4096.0, None, A.min)
+            ts(cols("nt" + c, 256, 512), full(last), (200.0 - 512.0) * K, None, A.is_ge)
+            far = cols(spare() if "k" in OWNB else X, 256, 272)
+            mm([(far, full("idb"), cols("nt" + c, 256 + 16 * k, 272 + 16 * k), k == 0, k == 15) for k in range(16)])
+            dd, a2f, w1, w2 = [cols("tf" + c, 16 * j, 16 * j + 16) for j in range(2, 6)]
+            act(dd, far, F.Relu, 8192.0, -8192.0, alt=("ts", dd, far, 0.5, 8192.0, A.is_lt, A.mult))
+            tt(a2f, a32, dd, A.subtract)
+            ts(a2u, a2f, 16.0, 15.0, A.add, A.max)
             tag[0] = "q%d%s" % (t, c)
             qa = ("qn%d" % t, 256 * ch) if t < 2 else ("ef" + c, 0)
-            acp(cols(qa[0], qa[1], qa[1] + 256), ind(cols("Qt", 0, 1536 if t == 0 else 4096), au))
+            acp(cols(qa[0], qa[1], qa[1] + 256), ind(cols("Qt", 0, PARENTS[t]), au))
             cp(full("qu" + c), k2l(qa, c))
             tag[0] = "l%d%s" % (t, c)
             va = cols("va" + c, 0, 256)
-            acp(va, ind(cols("Vb", 0, [1536, 3584, 4096][t]), au))
+            acp(va, ind(node("Vb", 0, PARENTS[t]), au))
             gcp(cols("va" + c, 256, 512), va)
             gcp(cols("va" + c, 512, 1024), cols("va" + c, 0, 512))
-            ascale(full("t1" + c), ind(full("IO"), au), MC)
-            bt = cols("Bt", 768 * ch + tile, 768 * ch + 768, 3)
-            acp(bt, ind(full("IO"), a2u))
-            dead = cols("nt" + c, 512, 768)
-            act(dead, bt, F.Relu, 0.0, -200.0, alt=("ts", dead, bt, -200.0, 0.0, A.mult, A.max))
-            xh = cols(X, 0, 256)
-            mm([(xh, full("idf"), full("t1" + c), True, False), (xh, full("idb"), va, False, False),
-                (xh, full("idb"), dead, False, True)])
-            acp(cols("VB", 768 * ch + tile, 768 * ch + 768, 3), xh)
-            x2 = cols(X, 256, 512)
-            mm([(x2, full("idf"), full("t1" + c), True, False), (x2, full("idb"), va, False, True)])
+            t1 = cols("lo" + c, 0, 256)
+            lin(t1, ind(node("IO", 0, PARENTS[t]), au), 2.0 ** -18, IB)
+            x2 = cols(spare() if "v" in OWNB else X, 256, 512)
+            mm([(x2, full("idb"), t1, True, False), (x2, full("idb"), va, False, True)])
             acp(cols("vf" + c, 0, 256), x2)
             gcp(cols("vf" + c, 256, 512), cols("vf" + c, 0, 256))
             gcp(cols("vf" + c, 512, 1024), cols("vf" + c, 0, 512))
+            bt = cols("Bt", 768 * ch + tile, 768 * ch + 768, 3)
+            acp(bt, ind(cols("IO", 0, 16 + PARENTS[t]), a2u))
+            tt(cols("VB", 768 * ch + tile, 768 * ch + 768, 3), ind(cols("Vb", 0, 16 + PARENTS[t]), a2u), t1, A.add)
             tag[0] = "d%d%s" % (t, c)
             eq = cols("nt" + c, 0, 256)
             tt(eq, ind(a2f, full("OE")), bt, A.is_equal)
-            mm([(cols(X, 256, 272), cols("Wt", 128 * r, 128 * r + 128), cols("nt" + c, r, 256, 16), r == 0, r == 15) for r in range(16)])
-            ts(w1, cols(X, 256, 272), 0.0, 8192.0, A.is_gt, A.mult)
-            tt(w2, w1, yy, A.add)
-            ts(cols("au" + c, 32, 64, 2), w2, DUM, None, A.min)
-            ts(full("M" + c), full(Mc), 4095, None, A.bitwise_and)
+            dup = cols("PM" if str(t) in OWNB else spare() if "d" in OWNB else X, 256, 272)
+            mm([(dup, cols("Wt", 128 * r, 128 * r + 128), cols("nt" + c, r, 256, 16), r == 0, r == 15) for r in range(16)])
+            tt(w2, a2f, dup, A.subtract)
+            ts(cols("au" + c, 32, 64, 2), w2, 16.0, P16, A.add, A.max)
+            if t == 1:
+                ts(full("Mc" + c), full(last), -4097, None, A.bitwise_and)
+            ts(full("M" + c), full(last), 4095, None, A.bitwise_and)
             if t == 1:
                 cp(cols("su" + c, 0, 256), full("M" + c))
-        for ch, c in enumerate("ab"):
+        for ch, c in halves:
             X = "PX" + c
             va = cols("va" + c, 0, 256)
-            zact = ONACT["z%d%s" % (t, c)]
             tag[0] = "z%d%s" % (t, c)
-            dist("XZ" + c, full("Zb"), "qu" + c, 0, "va" + c, 0, [2 * j + i for j in zact for i in range(2)], "XA" + c,
-                 ONACT["Z%d%s" % (t, c)], "XA" + c)
-            diag(X, 0, "U", "XA" + c, True, ONACT["Z%d%s" % (t, c)], "XZ" + c, "XA" + c)
-            act(full("f2" + c), cols(X, 0, 256), F.Identity, FAR + 0.5, -1.0 / K14,
-                alt=("ts", full("f2" + c), cols(X, 0, 256), -1.0 / K14, FAR + 0.5, A.mult, A.add))
+            diag(X, 0, dist("XZ" + c, full("Zb"), "qu" + c, 0, "va" + c, 0, "XA" + c, "XA" + c), True, None,
+                 lambda a, b: lin(cols("f2" + c, a, b), cols(X, a, b), -1.0 / K / K, (FAR + 0.5) / K))
             act(cols("lo" + c, 0, 256), va, F.Relu, -2.0, alt=("ts", cols("lo" + c, 0, 256), va, -2.0, 0.0, A.add, A.max))
             ts(cols("lo" + c, 256, 512), va, 2.0, 63.0, A.add, A.min)
         tag[0] = "x%d" % t
-        iota(full("SC"), [[1, 512]], new0, 0)
-        dma(ap("SC", S(1, 128, 16), AL), ap("CH", S(1, 128, 16), S(new0, new0 + 512)), 16384)
-        for ch, c in enumerate("ab"):
-            for m in range(15, -1, -1):
-                o = 256 * ch + 16 * m
-                cp(ind(full("CH"), cols("au" + c, 32 + 2 * m, 33 + 2 * m)), cols("SC", o, o + 16))
+        gcp(full("SC"), node("CH", new0, new0 + 512))
+        if not late:
+            for ch, c in halves:
+                children(t, c, ch)
+        tag[0] = "x%d" % t
         if t < 2:
             qn = full("qn%d" % t)
-            remote(full("GQ%d" % t), qn, 262144, HOPS[t], 2 * t)
+            remote(full("GQ%d" % t), qn, 262144, HOPS[t], 3 * t + 2)
             dma(cols("Qt", new0, new0 + 512), qn, 262144)
             dma(cols("Qt", 3072 + 512 * t, 3584 + 512 * t), full("GQ%d" % t), 262144)
         if t == 0:
             s_out(0)
-            for ch, c in enumerate("ab"):
-                ds_pass(1, c, ch, "PM", 256 * ch, "XS")
         if t == 2:
             s_out(1)
             dma(ap("ys", AL), full("YS"), 393216)
-            dma(ap("yk", AL), ap("CH", S(0, 128, 16), S(0, 4096)), 131072)
+            dma(full("Ksa"), ap("CH", S(0, 128, 16), S(16, 4112)), 131072)
+            cp(full("Mca"), full("Ksa"))
+            cp(full("Ksb"), full("Mca"))
+            dma(ap("yk", AL), full("Ksb"), 131072)
             dma(ap("yb", AL), ap("Bt", S(0, 128, 16), AL), 49152)
-        for ch, c in enumerate("ab"):
+        for ch, c in halves:
             X, Y = "PX" + c, "PY" + c
-            yl = psl(Y, 0, 256)
             tag[0] = "b%d%s" % (t, c)
-            dist("XE" + c, full("VB"), "qu" + c, 0, "vf" + c, 0, [])
+            dist("XE" + c, full("VB"), "qu" + c, 0, "vf" + c, 0)
             tag[0] = "h%d%s" % (t, c)
             nat = lambda a, b: cols("nt" + c, 512 + a, 512 + b)
             H = cols(X, 0, 256)
+            mult = MULT.get(tag[0], ())
             mm([(H, full("idb"), cols("va" + c, 0, 256), True, False)])
             for kg in range(4):
-                for k0, k1 in KS4:
+                part[0] = kg
+                for k0, k1 in KH:
                     if k0 // 4 != kg:
                         continue
                     a0, a1 = 16 * k0, 16 * k1
-                    mm([(psl(Y, a0, a1), Ur("U", r), cols("XE" + c, 256 * k0 + r, 256 * k1, 16), r == 0, r == 15) for r in range(16)])
-                    n2 = cols("nt" + c, 256 + a0, 256 + a1)
-                    act(n2, psl(Y, a0, a1), F.Sign, alt=("ts", n2, psl(Y, a0, a1), 0.0, None, A.is_gt, None))
-                    act(psl(Y, a0, a1), psl(Y, a0, a1), F.Abs, -FAR, 1.0 / K14)
-                    tt(psl(Y, a0, a1), psl(Y, a0, a1), cols("f2" + c, a0, a1), A.is_ge)
-                    tt(nat(a0, a1), psl(Y, a0, a1), n2, A.mult)
-                if kg == 3:
-                    c16 = ap(Y, AL, 8, 0, AL)
-                    mm([(c16, full("idb"), nat(16 * k, 16 * k + 16), k == 0, k == 15) for k in range(16)])
+                    y = psl(Y, a0, a1)
+                    mm([(y, Ur("U", r), cols("XE" + c, 256 * k0 + r, 256 * k1, 16), r == 0, r == 15) for r in range(16)])
+                    act(cols("t1" + c, a0, a1), y, F.Abs, -FAR / K, 1.0 / K / K)
+                    tt(y, y, cols("t1" + c, a0, a1), A.min)
+                    tt(nat(a0, a1), y, cols("f2" + c, a0, a1), A.is_lt if kg in mult else A.is_ge)
+                way = WAYS.get("z%d%s" % (t, c), "vvvv")[kg]
+                sgn = "nid" if way in "dr" else "idb"
+                if kg in mult:
+                    assert way != "p"
+                    for hf in range(2):
+                        E = spare()
+                        mm([(cols(E, 64 * j, 64 * j + 64), cols("Wb", 128 * r, 128 * r + 128), nat(64 * kg, 64 * kg + 64), True, True)
+                            for j, r in enumerate(range(8 * hf, 8 * hf + 8))])
+                        for j, r in enumerate(range(8 * hf, 8 * hf + 8)):
+                            tt(rows("sg" + c, 4 * kg, 4 * kg + 4, r), rows("XZ" + c, 4 * kg, 4 * kg + 4, r), cols(E, 64 * j, 64 * j + 64), A.mult)
+                    for k in range(4 * kg, 4 * kg + 4, 2):
+                        so = rows("sg" + c, k, k + 2)
+                        o = act(so, so, F.Sign, alt=("ts", so, so, 1.0, -1.0, A.min, A.max))
+                        o["alts"] = {"v": o["alts"]["v"], "a": o["alts"]["a"]}
+                        mm([(H, full(sgn), rows("sg" + c, j, j + 1), False, j == 15) for j in (k, k + 1)])
+                    continue
+                plain = [k for k in range(4) if k not in mult]
+                if kg == plain[-1]:
+                    c64 = psl(Y, 0, 64)
+                    mm([(c64, full("idb"), nat(64 * k, 64 * k + 64), k == plain[0], k == kg) for k in plain])
                     cn = cols("nt" + c, 0, 16)
-                    act(cn, c16, F.Identity, 0.0, -1.0 / 128, alt=("ts", cn, c16, -1.0 / 128, None, A.mult, None))
+                    lin(cols("nt" + c, 64, 128), c64, -1.0 / 128, 0.0)
+                    tt(cols("nt" + c, 32, 64), cols("nt" + c, 64, 96), cols("nt" + c, 96, 128), A.add)
+                    tt(cn, cols("nt" + c, 32, 48), cols("nt" + c, 48, 64), A.add)
                     mm([(cols(X, r, 256, 16), cols("Wb", 128 * r, 128 * r + 128), cn, False, False) for r in range(16)])
                 for hf in range(2):
-                    E = "PE%d" % hf
+                    E = spare()
                     it = []
                     for j in range(8):
                         r = 8 * hf + j
-                        it += [(cols(E, j, 512, 8), full("idb"), cols("XZ" + c, 1024 * kg + r, 1024 * kg + 1024, 16), True, False)]
-                        if kg in ONACT["z%d%s" % (t, c)] and kg not in ONACT["Z%d%s" % (t, c)]:
+                        it += [(cols(E, j, 512, 8), full(sgn), cols("XZ" + c, 1024 * kg + r, 1024 * kg + 1024, 16), True, False)]
+                        if way == "p":
                             it += [(cols(E, j, 512, 8), full("nid"), cols("va" + c, r, 1024, 16), False, False)]
                         it += [(cols(E, j, 512, 8), cols("Wb", 128 * r, 128 * r + 128), nat(64 * kg, 64 * kg + 64), False, True)]
                     mm(it)
                     so = ap("sg" + c, AL, S(64 * kg, 64 * kg + 64), S(8 * hf, 8 * hf + 8))
                     act(so, full(E), F.Sign, alt=("ts", so, full(E), 1.0, -1.0, A.min, A.max))
-                mm([(H, full("idb"), ap("sg" + c, AL, S(16 * k, 16 * k + 16), AL), False, k == 15) for k in range(4 * kg, 4 * kg + 4)])
+                pair = PAIR.get(tag[0], ())
+                if kg + 1 in pair:
+                    continue
+                k0 = 4 * kg
+                if kg in pair:
+                    k0 -= 4
+                    dadd(rows("sg" + c, k0, k0 + 4), rows("sg" + c, k0 + 4, k0 + 8), 262144)
+                mm([(H, full("idb"), rows("sg" + c, k, k + 1), False, kg == 3 and k == k0 + 3) for k in range(k0, k0 + 4)])
+            part[0] = None
             tt(H, H, cols("lo" + c, 0, 256), A.max)
-            tt(cols("Vb", new0 + 256 * ch, new0 + 256 * ch + 256), H, cols("lo" + c, 256, 512), A.min)
+            nv = node("Vb", new0 + 256 * ch, new0 + 256 * ch + 256)
+            tt(nv, H, cols("lo" + c, 256, 512), A.min)
             if t == 2:
-                dma(ap("yv", AL, S(1024 + 256 * ch, 1280 + 256 * ch)), cols("Vb", new0 + 256 * ch, new0 + 256 * ch + 256), 65536)
+                dma(ap("yv", AL, S(1024 + 256 * ch, 1280 + 256 * ch)), nv, 65536)
+            else:
+                remote(cols("GV%d" % t, 256 * ch, 256 * ch + 256), nv, 65536, HOPS[t], 3 * t + ch)
+            if late:
+                children(t, c, ch)
         if t < 2:
-            nv = cols("Vb", new0, new0 + 512)
-            remote(full("GV%d" % t), nv, 131072, HOPS[t], 2 * t + 1)
+            tag[0] = "y%d" % t
+            nv = node("Vb", new0, new0 + 512)
             dma(ap("yv", AL, S(512 * t, 512 * t + 512)), nv, 131072)
-            dma(cols("Vb", 3072 + 512 * t, 3584 + 512 * t), full("GV%d" % t), 131072)
-            for ch, c in enumerate("ab"):
-                child_pass(c, 256 * (1 - t), [2048, 4096][t], "PM", 256 * ch)
+            dma(node("Vb", 3072 + 512 * t, 3584 + 512 * t), full("GV%d" % t), 131072)
+            for ch, c in halves:
+                child_pass(t + 1, c, ch, 256 * (1 - t), [2048, 4096][t], "PM", 256 * ch)
     assert nd[0] <= NDMA
     return ops
 
@@ -599,7 +760,7 @@ def depend(ops):
             ps = _chain(acc)
             row = _row(acc)
             for (n, hm, hw, hr) in hist.get(acc[0], []):
-                if n == o["n"] or (row is not None and hr is not None and row != hr):
+                if n == o["n"] or (row is not None and hr is not None and not (row & hr)):
                     continue
                 if (hm & m) and (w or hw):
                     d[n] = True
@@ -620,17 +781,17 @@ def depend(ops):
 
 def _row(x):
     p = x[1][0]
-    return p.start if p.step == 16 else None
+    return None if p == slice(None) else set(range(128)[p])
 
 
 def _chain(x):
-    return _psum(x) and x[0] != "PK"
+    return _psum(x)
 
 
 def _times(o, e, C):
     kind, n = o["alts"][e][1]
     if kind == "dma":
-        return (60.0 if e != "g" else 1000.0), C["dma"] + n / 150.0
+        return (60.0 if e != "g" else C["issue"]), C["dma"] + n / C["rate"]
     if kind == "pe":
         t = n * C["pe"]
     elif kind == "cyc":
@@ -640,7 +801,34 @@ def _times(o, e, C):
     return t, t
 
 
-def schedule(ops, C):
+def length(ops, order, C):
+    free, end = dict((e, 0.0) for e in "vapgs"), [0.0] * len(ops)
+    for n in order:
+        e = ops[n]["e"]
+        st = max([free[e]] + [end[d] + (0.0 if e == "p" == ops[d]["e"] else C["lat"]) for d in ops[n]["deps"]])
+        busy, done = _times(ops[n], e, C)
+        free[e], end[n] = st + busy, st + done
+    return max(end)
+
+
+def climb(ops, C):
+    tags = sorted(set(o["tag"] for o in ops))
+    tables = [dict(BIAS), dict(BIAS)]
+    best, seed = None, C["seed"]
+    for it in range(C["shifts"] + 1):
+        seed = (seed * 6364136223846793005 + 1442695040888963407) % 2 ** 64
+        new = [dict(x) for x in tables]
+        if it:
+            x, k = new[(seed >> 50) % 5 < 3], tags[(seed >> 30) % len(tags)]
+            x[k] = x.get(k, 0) + [-10, -4, -2, -1, 1, 2, 4, 10][seed >> 20 & 7]
+        order = schedule(ops, C, *new)
+        c = sum(length(ops, order, dict(C, **f)) / f["gat"] ** 0.5 for f in SPREAD)
+        if best is None or c <= best:
+            best, tables = c, new
+    return schedule(ops, C, *tables)
+
+
+def schedule(ops, C, first=None, second=None):
     succ = [[] for _ in ops]
     for o in ops:
         for d in o["deps"]:
@@ -649,11 +837,14 @@ def schedule(ops, C):
     for o in reversed(ops):
         e = list(o["alts"])[0]
         prio[o["n"]] = _times(o, e, C)[1] + C["lat"] + max([prio[s] for s in succ[o["n"]]] or [0.0])
-    bias = [1000.0 * BIAS.get(o["tag"] + list(o["alts"])[0], 0) for o in ops]
-    order = forward(ops, C, succ, [p + b for p, b in zip(prio, bias)])
-    for _ in range(C["turns"]):
-        order = forward(ops, C, succ, backward(ops, C, succ))
-    return order
+    def urgent(prio, table):
+        prio = [p + 1000.0 * table.get(o["tag"], 0) for p, o in zip(prio, ops)]
+        for o in reversed(ops):
+            prio[o["n"]] = max([prio[o["n"]]] + [prio[s] + 1.0 for s in succ[o["n"]]])
+        return prio
+
+    forward(ops, C, succ, urgent(prio, first or BIAS))
+    return forward(ops, C, succ, urgent(backward(ops, C, succ), second or BIAS))
 
 
 def backward(ops, C, succ):
@@ -685,20 +876,15 @@ def forward(ops, C, succ, prio):
     free = dict((e, 0.0) for e in "vapgs")
     order = []
     while avail:
-        best = None
+        cand = []
         for n in avail:
             alts = list(ops[n]["alts"])
             for j, e in enumerate(alts):
                 st = max(free[e], ready_at[n])
-                if j > 0:
-                    if free[alts[0]] <= st + C["alt"]:
-                        continue
-                    st_key = (st, 1, -prio[n])
-                else:
-                    st_key = (st, 0, -prio[n])
-                if best is None or st_key < best[0]:
-                    best = (st_key, n, e, st)
-        _, n, e, st = best
+                if j == 0 or free[alts[0]] > st + C["alt"]:
+                    cand.append((st, j, n, e))
+        t0, _, _, e = min(cand)
+        st, _, n, _ = max((x for x in cand if x[3] == e and x[0] <= t0 + C["look"]), key=lambda x: (-x[1], prio[x[2]]))
         o = ops[n]
         busy, done = _times(o, e, C)
         o["e"], o["t0"], o["t1"] = e, st, st + done
@@ -714,10 +900,143 @@ def forward(ops, C, succ, prio):
     return order
 
 
+def polish(ops, order, C):
+    n = len(ops)
+    anc, pre, suc = [0] * n, [], [[] for _ in ops]
+    for o in ops:
+        keep, cov = [], 0
+        for d in sorted(o["deps"], reverse=True):
+            if not (cov >> d) & 1:
+                keep.append(d)
+                suc[d].append(o["n"])
+            cov |= anc[d] | (1 << d)
+        anc[o["n"]] = cov
+        pre.append(keep)
+    figs = [dict(C, **x) for x in SPREAD]
+    names = "vapgs"
+    tm = [[dict((names.index(e), _times(o, e, f)) for e in o["alts"]) for o in ops] for f in figs]
+    eng = [names.index(o["e"]) for o in ops]
+    STEP = 32
+
+    def run(order, eng, j, first, old):
+        t, lat = tm[j], figs[j]["lat"]
+        k = first // STEP
+        end, marks = list(old[0]), old[1][:k + 1]
+        free = list(marks[k])
+        for a in range(k * STEP, n, STEP):
+            if a > k * STEP:
+                marks.append(tuple(free))
+            for v in order[a:a + STEP]:
+                e = eng[v]
+                st = free[e]
+                if e == 2:
+                    for d in pre[v]:
+                        x = end[d] if eng[d] == 2 else end[d] + lat
+                        if x > st:
+                            st = x
+                else:
+                    st -= lat
+                    for d in pre[v]:
+                        if end[d] > st:
+                            st = end[d]
+                    st += lat
+                b, dn = t[v][e]
+                free[e] = st + b
+                end[v] = st + dn
+        return end, marks
+
+    def longest(order, eng, j, end):
+        t, lat = tm[j], figs[j]["lat"]
+        before, last = [-1] * n, [-1] * 5
+        for v in order:
+            before[v] = last[eng[v]]
+            last[eng[v]] = v
+        v, way = end.index(max(end)), []
+        while v >= 0:
+            way.append(v)
+            st = end[v] - t[v][eng[v]][1]
+            w = [d for d in pre[v] if end[d] + (0.0 if eng[d] == 2 == eng[v] else lat) > st - 0.01]
+            v = w[0] if w else before[v]
+        return way
+
+    state = [run(order, eng, j, 0, ([0.0] * n, [(0.0,) * 5])) for j in range(len(figs))]
+    base = [max(s[0]) for s in state]
+    cur = 1.0
+    best = (cur, order, eng)
+    parts = {}
+    for o in ops:
+        parts.setdefault((o["tag"], o["q"]), []).append(o["n"])
+    kin = [parts[(o["tag"], o["q"])] for o in ops]
+    seed = C["seed"]
+    way = None
+    for it in range(C["tries"]):
+        seed = (seed * 6364136223846793005 + 1442695040888963407) % 2 ** 64
+        r0, r1, r2, r3 = [(seed >> s & 4095) / 4096.0 for s in (52, 40, 28, 16)]
+        if way is None:
+            j = it % len(figs)
+            way = longest(order, eng, j, state[j][0])
+            pos = [0] * n
+            for p, v in enumerate(order):
+                pos[v] = p
+        v = way[int(r0 * len(way))]
+        p, e, k = pos[v], eng[v], [1, 1, 1, 2, 3, 5, 8][int(r2 * 7)]
+        new, neng, q = order, eng, p
+        if r1 > 1.0 - C["whole"]:
+            k = [3, 6, 12, 24, 48][int(r2 * 5)]
+            new, at = list(order), list(pos)
+            mine = sorted(kin[v], key=lambda x: pos[x])
+            if seed >> 8 & 1:
+                for x in mine:
+                    a = at[x]
+                    b = max([a - k] + [at[d] + 1 for d in pre[x]] + [0])
+                    new[b:a + 1] = [x] + new[b:a]
+                    for y in range(b, a + 1):
+                        at[new[y]] = y
+                    q = min(q, b)
+            else:
+                for x in reversed(mine):
+                    a = at[x]
+                    b = min([a + k] + [at[s] - 1 for s in suc[x]] + [n - 1])
+                    new[a:b + 1] = new[a + 1:b + 1] + [x]
+                    for y in range(a, b + 1):
+                        at[new[y]] = y
+                q = pos[mine[0]]
+        elif r1 < 0.2:
+            if len(tm[0][v]) < 2:
+                continue
+            neng = list(eng)
+            neng[v] = sum(tm[0][v]) - e
+        elif r1 < 0.65:
+            lo = max([pos[d] for d in pre[v]] or [-1]) + 1
+            while q > lo and k:
+                q -= 1
+                k -= eng[order[q]] == e
+            if q == p:
+                continue
+            new = order[:q] + [v] + order[q:p] + order[p + 1:]
+        else:
+            hi = min([pos[s] for s in suc[v]] or [n]) - 1
+            while q < hi and k:
+                q += 1
+                k -= eng[order[q]] == e
+            if q == p:
+                continue
+            new = order[:p] + order[p + 1:q + 1] + [v] + order[q + 1:]
+        trial = [run(new, neng, j, min(p, q), state[j]) for j in range(len(figs))]
+        c = sum(max(s[0]) / b for s, b in zip(trial, base)) / len(figs)
+        if c <= cur or r3 < math.exp((cur - c) / (C["heat"] * (1.0 - it / C["tries"]) + 1e-5)):
+            order, eng, cur, state, way = new, neng, c, trial, None
+            if c < best[0]:
+                best = (c, order, eng)
+    for o in ops:
+        o["e"] = names[best[2][o["n"]]]
+    return best[1]
+
+
 def plan():
     ops = build()
     depend(ops)
-    order = schedule(ops, COST)
+    order = polish(ops, climb(ops, COST), COST)
     needs = [False] * len(ops)
     for o in ops:
         for d, hard in o["deps"].items():
@@ -808,7 +1127,10 @@ def rank_program(g, core, T, topo):
         elif k == "ms":
             i = q.memset(X(call[1]), call[2])
         elif k == "act":
-            i = q.activation(X(call[1]), X(call[2]), call[3], X(call[4]), X(call[5]))
+            if call[1][0] == "*":
+                i = q.activation(X(call[1]), X(call[2]), call[3])
+            else:
+                i = q.activation(X(call[1]), X(call[2]), call[3], X(call[4]), X(call[5]))
         elif k == "mm":
             for out, l, r, st, sp in call[1]:
                 i = q.matmul(X(out), X(l), X(r), st, sp)
@@ -820,7 +1142,10 @@ def rank_program(g, core, T, topo):
         elif k == "sel":
             i = q.affine_select(X(call[1]), X(call[2]), call[3], call[4], 0.0, call[5], call[6])
         elif k == "dma":
-            i = q.dma_start(X(call[1]), X(call[2]))
+            if len(call) > 3:
+                i = q.dma_start(X(call[1]), X(call[2]), accum_op=A.add)
+            else:
+                i = q.dma_start(X(call[1]), X(call[2]))
         else:
             dst = T.cores[(rank + call[3]) % nrank]
             rid, pid, _ = topo.addr(dst)

import math
from concourse.mybir import dt, AluOpType, AxisListType, ActivationFunctionType

A = AluOpType
F = ActivationFunctionType
BF, F32, I32, U16 = "bfloat16", "float32", "int32", "uint16"
HOPS, TILE = [1, 3], [0, 1, 1]
PARENTS = [1536, 3584, 4096]
K = 32768.0
FAR = 1009.0

SCRATCH = {}


def _sb(name, shape, dtype):
    SCRATCH[name] = ("sbuf", [128] + list(shape), dtype)


for _n, _w, _d in [("Vb", 4112, BF), ("IO", 4112, F32), ("CH", 4112, F32), ("Qt", 4096, F32), ("VB", 1536, F32),
                   ("Bt", 1536, F32), ("Zb", 1536, BF), ("sni", 1536, I32), ("SC", 512, F32),
                   ("YS", 768, F32), ("Wb", 2048, BF), ("Wt", 2048, BF), ("XS", 4096, BF),
                   ("xi", 160, F32), ("xl", 16, F32), ("U", 144, BF), ("U2", 144, BF), ("Ua", 144, BF), ("Ue", 144, BF),
                   ("Us", 144, BF), ("Un", 144, BF), ("Wn", 128, BF), ("Wa", 128, BF), ("Wk", 128, BF), ("idB", 128, BF),
                   ("IW0", 160, F32), ("IW1", 160, F32), ("idb", 128, BF), ("nid", 128, BF), ("idf", 128, F32),
                   ("SL", 144, BF), ("ci", 16, I32), ("cf", 32, F32), ("kbb", 256, BF), ("z16", 64, F32), ("gx", 128, BF), ("rm", 32, F32),
                   ("OB", 16, U16), ("OE", 16, U16), ("OP", 16, U16), ("OL", 16, U16), ("gid", 64, F32),
                   ("kidc", 96, I32), ("bsc", 96, I32), ("iu", 96, U16), ("it2", 512, F32),
                   ("qn0", 512, F32), ("qn1", 512, F32), ("GQ0", 512, F32), ("GQ1", 512, F32), ("GV0", 512, BF), ("GV1", 512, BF),
                   ("zr", 4096, BF)]:
    _sb(_n, [_w], _d)
_sb("pY", [8, 2, 16], F32)
for _c in "ab":
    for _n, _s, _d in [("XE", [4096], BF), ("XZ", [4096], BF), ("XA", [4096], BF),
                       ("sg", [256, 16], BF), ("f1", [256], F32), ("f2", [256], F32), ("Ks", [256], F32), ("zc", [256], F32),
                       ("ef", [256], F32), ("sf", [256], F32), ("su", [512], U16), ("eu", [256], U16), ("qu", [256], U16),
                       ("M", [256], I32), ("M2", [256], I32), ("Mc", [256], I32), ("L1", [128], F32),
                       ("L2", [64], I32), ("L3", [96], F32), ("tr", [256], F32), ("ti", [32], I32), ("tf", [96], F32),
                       ("au", [64], U16), ("va", [1024], BF), ("vf", [1024], F32), ("t1", [256], F32),
                       ("lo", [512], BF), ("nt", [768], BF)]:
        _sb(_n + _c, _s, _d)
for _n in ["PXa", "PXb", "PE0", "PE1", "PE2", "PM"]:
    SCRATCH[_n] = ("psum", [128, 512], F32)
for _n in ["PYa", "PYb"]:
    SCRATCH[_n] = ("psum", [128, 16, 2, 16], F32)

NDMA = 90
SEMAPHORES = ["v", "a", "p", "g", "sent"] + ["d%d" % _i for _i in range(NDMA)] + ["arr%d" % _i for _i in range(6)]

COST = {"cyc": 1.0, "gat": 1.56, "sca": 3.8, "pe": 0.55, "lat": 90.0, "dma": 2600.0, "issue": 1300.0, "rate": 110.0, "alt": 1000.0, "look": 120.0,
        "shifts": 300, "tries": 105000, "heat": 0.00005, "whole": 0.1, "seed": 1}
SPREAD = [{"gat": 1.3, "sca": 3.0, "lat": 100.0, "dma": 2000.0, "issue": 1000.0, "rate": 150.0},
          {"gat": 2.0, "sca": 4.5, "lat": 150.0, "pe": 0.5, "dma": 3200.0, "issue": 1600.0, "rate": 90.0}]
KS = [(0, 8), (8, 12), (12, 16)]
KH = [(0, 4), (4, 8), (8, 12), (12, 16)]
KC = [KH, KH, KH]
SPLIT = "sezb"
PAIR = {}
MULT = {"h2b": (0, 1, 2, 3)}
OWNB = ""
BYMAX = {"s0": True, "s1": False, "e0": True, "e1": False, "e2": False}
WAYS = {"s0a": "mmmm", "s0b": "mmmm", "e0a": "mmmm", "e0b": "mmmm", "s1a": "dddd", "s1b": "ddpd",
        "e1a": "pvvv", "e1b": "pvvv", "e2a": "pvvv", "e2b": "pvvv",
        "z0a": "rrvv", "z0b": "rvvv", "z1a": "rrvv", "z1b": "rrvv", "z2a": "rrvv", "z2b": "rrvv"}
BIAS = {"w": 300}


def ap(name, *idx):
    return (name, idx)


def cols(name, a, b, step=1):
    return (name, (slice(None), slice(a, b, step)))


def node(name, a, b):
    return cols(name, 16 + a, 16 + b)


def ind(win, off):
    return ("*", win, off)


_masks = {}


def _mask(x):
    name, idx = x
    key = (name, repr(idx))
    if key not in _masks:
        shape = SCRATCH[name][1][1:]
        idx = list(idx[1:]) + [slice(None)] * (len(shape) + 1 - max(len(idx), 1))
        offs = [0]
        for d, (n, i) in enumerate(zip(shape, idx)):
            r = range(n)[i] if isinstance(i, slice) else [i]
            offs = [o * n + j for o in offs for j in r]
        m = 0
        for o in offs:
            m |= 1 << o
        _masks[key] = (m, len(offs))
    return _masks[key]


def _size(x):
    if x[0] == "*":
        return 16 * _size(x[2])
    return _mask(x)[1]


def _two(x):
    return SCRATCH[x[1][0] if x[0] == "*" else x[0]][2] in (BF, U16)


def _psum(x):
    return x[0] != "*" and x[0] in SCRATCH and SCRATCH[x[0]][0] == "psum"


def build():
    ops = []
    tag = ["load"]
    part = [None]
    halves = [(1, "a"), (0, "b")]

    def add(kind, alts, reads, writes, **kw):
        rd, wr = [], []
        for x in reads:
            if isinstance(x, tuple):
                rd += [x[1], x[2]] if x[0] == "*" else [x]
        for x in writes:
            if x[0] == "*":
                wr.append(x[1])
                rd.append(x[2])
            else:
                wr.append(x)
        o = dict(kind=kind, alts=alts, rd=[x for x in rd if x[0] in SCRATCH], wr=[x for x in wr if x[0] in SCRATCH], n=len(ops), tag=tag[0], q=part[0])
        o.update(kw)
        ops.append(o)
        return o

    def vcost(out, ins, tt=False):
        if out[0] == "*":
            return ("sca", _size(out))
        if ins[0][0] == "*":
            return ("gat", _size(ins[0]))
        n = _size(out)
        if tt:
            return ("cyc", n if (_psum(ins[0]) or _psum(ins[1])) else 2 * n)
        return ("cyc", n // 2 if all(_two(x) for x in [out] + ins) else n)

    def tt(out, a, b, op):
        return add("c", {"v": (("tt", out, a, b, op), vcost(out, [a, b], True))}, [a, b], [out])

    def ts(out, a, s1, s2, op0, op1=None):
        return add("c", {"v": (("ts", out, a, s1, s2, op0, op1), vcost(out, [a]))}, [a, s1, s2], [out])

    def cp(out, a):
        return add("c", {"v": (("cp", out, a), vcost(out, [a]))}, [a], [out])

    def tp(out, a):
        return add("c", {"v": (("tp", out, a), vcost(out, [a]))}, [a], [out])

    def ms(out, val):
        return add("c", {"v": (("ms", out, val), ("cyc", _size(out) // (2 if _two(out) else 1)))}, [], [out])

    def act(out, a, func, bias=0.0, scale=1.0, alt=None):
        alts = {"a": (("act", out, a, func, bias, scale), ("gat" if a[0] == "*" else "cyc", _size(a)))}
        if alt:
            alts["v"] = (alt, vcost(out, [a]))
        return add("c", alts, [a, bias, scale], [out])

    def acp(out, a, flex=True):
        return act(out, a, F.Identity, alt=("cp", out, a) if flex else None)

    def lin(out, a, scale, bias):
        return act(out, a, F.Identity, bias, scale, alt=("ts", out, a, scale, bias, A.mult, A.add))

    def put(out, a):
        return add("c", {"a": (("act", out, a, F.Silu, 0.0, 1.0), ("sca", _size(out))), "v": (("cp", out, a), ("sca", _size(out)))},
                   [a], [out])

    def mm(items):
        cyc, rd, wr = 0, [], []
        for out, l, r, st, sp in items:
            cyc += max(64, _size(r)) * (1 if _two(r) else 4)
            rd += [l, r]
            wr.append(out)
        return add("c", {"p": (("mm", items), ("pe", cyc))}, rd, wr)

    def iota(out, pat, base, mult):
        return add("c", {"g": (("iota", out, pat, base, mult), ("cyc", 130 + 2 * _size(out)))}, [], [out])

    def sel(out, a, pat, op, base, mult):
        return add("c", {"g": (("sel", out, a, pat, op, base, mult), ("cyc", 170 + 2 * _size(out)))}, [a], [out])

    def gcp(out, a):
        o = sel(out, a, [[0, _size(out)]], A.is_equal, 0, 0)
        o["alts"]["v"] = (("cp", out, a), vcost(out, [a]))
        return o

    nd = [0]

    def dma(out, a, nbytes, q="s", after=()):
        nd[0] += 1
        return add("d", {q: (("dma", out, a), ("dma", nbytes))}, [a] + list(after), [out], sem="d%d" % (nd[0] - 1))

    def dadd(out, a, nbytes):
        nd[0] += 1
        return add("d", {"g": (("dma", out, a, True), ("dma", 2 * nbytes))}, [a, out], [out], sem="d%d" % (nd[0] - 1))

    def remote(out, a, nbytes, hop, k):
        return add("r", {"g": (("rem", out, a, hop, k), ("dma", nbytes))}, [a], [out], sem="arr%d" % k)

    S = slice
    AL = S(None)
    lent = {"k32": ("vfa", 0, 96), "bsf": ("vfa", 192, 288), "of": ("vfa", 288, 448), "orr": ("vfa", 448, 608),
            "oh": ("vfa", 608, 768), "o32": ("vfa", 768, 928), "kb": ("nta", 0, 96), "kr": ("nta", 96, 192), "ob": ("nta", 192, 352), "t2": ("lob", 0, 512)}
    lent.update(bh=("nta", 352, 448), bl=("nta", 448, 544), K1a=("zca", 0, 256), K1b=("zcb", 0, 256))
    full = lambda n: cols(*lent[n]) if n in lent else ap(n, AL)

    dma(full("kidc"), ap("kid", AL), 49152)
    dma(node("Vb", 0, 1536), ap("vn", AL), 393216, "a")
    dma(cols("sni", 768, 1536), ap("sn", AL, S(768, 1536)), 393216)
    dma(full("Zb"), ap("zs", AL), 393216, "a")
    dma(cols("sni", 0, 768), ap("sn", AL, S(0, 768)), 393216)
    dma(full("bsc"), ap("bst", AL), 49152)
    for j in range(6):
        stage = full(["Mca", "Mcb", "Ma", "Mb"][j % 4])
        dma(stage, ap("nq", AL, S(256 * j, 256 * j + 256)), 131072, after=[full("Zb")])
        cp(cols("Qt", 256 * j, 256 * j + 256), stage)

    ci = lambda j: cols("ci", j, j + 1)
    cf = lambda j: cols("cf", j, j + 1)
    iota(ci(0), [[0, 1]], 0, 1)
    iota(ci(5), [[0, 1]], 13, 1)
    iota(ci(8), [[0, 1]], 15, 1)
    iota(full("xi"), [[1, 160]], 0, 0)
    iota(full("xl"), [[1, 4], [4, 4]], 0, 0)
    iota(full("kbb"), [[8192, 4], [0, 64]], 0, 0)
    ts(ci(1), ci(0), 15, None, A.bitwise_and)
    ts(ci(2), ci(0), 4, 1, A.logical_shift_right, A.bitwise_and)
    ts(ci(3), ci(0), 7, None, A.bitwise_and)
    ts(ci(4), ci(0), 8, None, A.bitwise_and)
    ts(ci(5), ci(5), 15, 2, A.bitwise_and, A.logical_shift_right)
    ts(ci(8), ci(8), 15, 1, A.bitwise_and, A.logical_shift_right)
    ts(ci(6), ci(0), 2, 3, A.logical_shift_right, A.bitwise_and)
    ts(ci(7), ci(0), 3, None, A.bitwise_and)
    (P16, G16, G15, P, PP16, M0, M1, IB, WA, DUM, PM, T16, S15, OWN, TMP,
     WE, WS, TN, TA, T7, T8, H8, B126, TM2, TM3) = [cf(j) for j in range(25)]
    ts(PP16, ci(0), 16.0, None, A.add)
    ts(M0, ci(2), -1.0, 1.0, A.mult, A.add)
    cp(M1, ci(2))
    ts(full("IW0"), full("xi"), PP16, M0, A.is_equal, A.mult)
    ts(full("IW1"), full("xi"), PP16, M1, A.is_equal, A.mult)
    ts(TMP, ci(3), 32.0, None, A.mult)
    ts(PM, ci(4), 2.0, TMP, A.mult, A.add)
    ts(full("OP"), full("xl"), PM, None, A.add)
    cp(P16, ci(1))
    cp(P, ci(0))
    ts(G16, ci(1), -1.0, P, A.mult, A.add)
    ts(G15, G16, 15.0, None, A.add)
    ts(WA, ci(8), 0.0, None, A.is_equal)
    ts(WS, ci(5), 1.0, K, A.is_equal, A.mult)
    ts(TM2, ci(5), 0.0, K, A.is_equal, A.mult)
    ts(WE, TM2, WA, None, A.add)
    ts(TN, ci(6), G16, 3.0, A.add, A.add)
    ts(TA, TN, 4.0, None, A.add)
    ts(T7, ci(3), 16.0, None, A.mult)
    ts(H8, ci(4), 0.125, 1.0, A.mult, A.add)
    ts(T8, ci(3), 16.0, H8, A.mult, A.add)
    ts(DUM, P16, 2.5, 126.0, A.is_gt, A.mult)
    ts(TM3, P16, 0.0, -32.0, A.is_equal, A.mult)
    ts(B126, DUM, TM3, None, A.add)
    x128, x144 = cols("xi", 0, 128), cols("xi", 0, 144)
    ts(full("Wn"), x128, TN, -1.0, A.is_equal, A.mult)
    ts(full("Wa"), x128, TA, -1.0, A.is_equal, A.mult)
    ts(full("idB"), x128, T8, None, A.is_equal)
    ts(full("nid"), x128, T7, None, A.is_equal)
    tt(full("Wk"), full("nid"), full("idB"), A.add)
    ts(full("U2"), x144, G15, 2 * K, A.is_equal, A.mult)
    ts(full("U"), x144, G15, K, A.is_equal, A.mult)
    ts(full("Un"), x144, G15, -K, A.is_equal, A.mult)
    ts(full("Ue"), x144, G15, WE, A.is_equal, A.mult)
    ts(full("Us"), x144, G15, WS, A.is_equal, A.mult)
    if not all(BYMAX["e%d" % t] for t in range(3)):
        ts(full("Ua"), x144, G15, WA, A.is_equal, A.mult)
    ts(full("idf"), x128, P, None, A.is_equal)
    ts(full("idb"), x128, P, None, A.is_equal)
    ts(full("nid"), x128, P, -1.0, A.is_equal, A.mult)
    ts(full("idB"), x128, P, 2.0 ** 26, A.is_equal, A.mult)
    ts(full("OB"), cols("xi", 0, 16), 0.0, P16, A.mult, A.add)
    P00, P10, Pa, Pb = cols("IW0", 16, 144), cols("IW0", 0, 128), cols("IW1", 32, 160), cols("IW1", 16, 144)
    Ur = lambda n, r: cols(n, 15 - r, 143 - r)

    tag[0] = "w"
    iota(full("gx"), [[16, 8], [0, 16]], 0, 0)
    ts(full("gx"), full("gx"), G16, 128.0, A.is_equal, A.mult)
    ts(cols("rm", 0, 16), cols("xi", 0, 16), P16, None, A.is_equal)
    ts(cols("rm", 16, 32), cols("xi", 0, 16), P16, None, A.is_gt)
    for r in range(16):
        act(cols("Wb", 128 * r, 128 * r + 128), full("gx"), F.Identity, 0.0, cols("rm", r, r + 1))
        act(cols("Wt", 128 * r, 128 * r + 128), Ur("U", r), F.Identity, 0.0, cols("rm", 16 + r, 17 + r))

    tag[0] = "table"
    cp(full("iu"), full("kidc"))
    cp(full("kb"), full("kidc"))
    ts(full("k32"), full("kidc"), 32.0, None, A.add)
    tt(full("kr"), full("k32"), full("kb"), A.subtract)
    dma(ap("XS", S(0, 8), S(1536, 3072)), full("kb"), 24576)
    dma(ap("XS", S(8, 16), S(1536, 3072)), full("kr"), 24576, "a")
    acp(cols("XS", 0, 1536), ind(node("Vb", 0, 1536), full("iu")))
    for j, bank in enumerate(["PE0", "PE1", "PXb"]):
        lo, hi = 512 * j, 512 * j + 512
        it = [(full(bank), full("Wa"), node("Vb", lo, hi), True, False)]
        for p in range(16):
            a, b = max(lo, 96 * p), min(hi, 96 * p + 96)
            if a < b:
                it.append((cols(bank, a - lo, b - lo), full("Wn"), cols("XS", 16 * (a - 96 * p) + p, 16 * (b - 96 * p), 16), False, False))
        it.append((full(bank), ap("Wk", S(0, 16), AL), ap("XS", S(0, 16), S(1536 + lo, 1536 + hi)), False, True))
        mm(it)
        lin(node("CH", lo, hi), full(bank), 1.0, B126)
    for tile in range(2):
        o = cols("PM", 32 * tile, 32 * tile + 32)
        mm([(o, Ur("U", r), cols("Zb", tile + 3 * r, 1536, 48), r == 0, r == 15) for r in range(16)])
    lin(full("z16"), cols("PM", 0, 64), -1.0, -1016.0 * K)

    def k2l(x, c):
        n, lo = x
        Y = "PY" + c
        h0, h1 = cols(n, lo, lo + 128), cols(n, lo + 128, lo + 256)
        mm([(ap(Y, AL, S(0, 8), 0, AL), P00, h0, True, False), (ap(Y, AL, S(0, 8), 0, AL), P10, h1, False, True),
            (ap(Y, AL, S(0, 8), 1, AL), Pa, h0, True, False), (ap(Y, AL, S(0, 8), 1, AL), Pb, h1, False, True)])
        tp(full("tr" + c), ap(Y, AL, S(0, 8), AL, AL))
        return ind(full("tr" + c), full("OP"))

    def s_in(tile, c, ch):
        tag[0] = "i%d%s" % (tile, c)
        cp(full("f1" + c), cols("sni", 768 * ch + tile, 768 * ch + 768, 3))
        off = 0.0 if BYMAX["s%d" % tile] else -512.0 * K
        lin(full("sf" + c), k2l(("f1" + c, 0), c), 1.0, off)
        ts(cols("su" + c, 256 * tile, 256 * tile + 256), full("sf" + c), -off, None, A.add)

    def z_in(tile, ch):
        o = 2048 * tile + 1024 * ch
        gcp(cols("zr", o, o + 256), cols("Zb", 768 * ch + tile, 768 * ch + 768, 3))
        gcp(cols("zr", o + 256, o + 512), cols("Zb", 768 * ch + tile, 768 * ch + 768, 3))
        gcp(cols("zr", o + 512, o + 1024), cols("zr", o, o + 512))

    def z_sum(tile, c, ch):
        o = 32 * tile + 16 * ch
        tt(full("zc" + c), ind(cols("z16", o, o + 16), full("OB")), full("kbb"), A.add)

    def psl(bank, a, b, step=1):
        if bank.startswith("PY"):
            assert step == 1
            return ap(bank, AL, S(a // 32, b // 32), AL, AL)
        return cols(bank, a, b, step)

    def rows(x, k0, k1, r=None):
        if x.startswith("sg"):
            return ap(x, AL, S(16 * k0, 16 * k1), AL if r is None else r)
        return cols(x, 256 * k0, 256 * k1) if r is None else cols(x, 256 * k0 + r, 256 * k1, 16)

    def diag(bank, o, terms, first, last=None, after=None):
        terms = terms if isinstance(terms, dict) else dict((q, terms) for q in range(4))
        for k0, k1 in KS if terms[0] == terms[1] and not after else KH:
            part[0] = (k1 - 1) // 4
            out = psl(bank, o + 16 * k0, o + 16 * k1)
            it = [[out, Ur(f, r), rows(x, k0, k1, r), False, False] for f, x in terms[k0 // 4] for r in range(16)]
            if last:
                it.append([out, full("idf"), cols(last, 16 * k0, 16 * k1), False, False])
            it[0][3] = first
            it[-1][4] = first or k1 == 16
            mm([tuple(x) for x in it])
            if after:
                after(16 * k0, 16 * k1)
        part[0] = None

    flip = [0]

    def spare():
        flip[0] = (flip[0] + 1) % 3
        return "PE%d" % flip[0]

    def dist(X, win, off, o, other, oo, XO=None, XR=None):
        XO = XO or X
        terms = {}
        for q, way in zip(range(4), WAYS.get(tag[0], "vvvv")):
            n = 2 if way == "p" or (q == 3 and way in "vmw" and tag[0][0] in SPLIT) else 4
            part[0] = q
            for k in range(4 * q, 4 * q + 4, n):
                x = cols(X, 256 * k, 256 * (k + n))
                w = ind(win, cols(off, o + 16 * k, o + 16 * (k + n)))
                z = cols(other, oo, oo + 256 * n)
                if way == "m":
                    tt(x, w, z, A.max)
                    continue
                if way in "dr":
                    act(x, w, F.Identity, 0.0, -1.0)
                    dadd(x, z, 262144)
                elif way == "p":
                    acp(x, w, False)
                    E = full(spare())
                    mm([(E, full("idb"), x, True, False), (E, full("nid"), z, False, True)])
                    x = E
                else:
                    tt(x, w, z, A.subtract)
                if way in "rw":
                    ts(rows(XR, k, k + n), x, 0.0, None, A.max)
                else:
                    act(cols(XO, 256 * k, 256 * (k + n)), x, F.Abs)
            terms[q] = [("U2", X)] if way == "m" else [("U2", XR), ("Un", X)] if way in "rw" else [("U", XO)]
        part[0] = None
        return terms

    def s_pass(tile, c, ch, X):
        tag[0] = "s%d%s" % (tile, c)
        mx = BYMAX["s%d" % tile]
        o = 256 * ch
        out = psl("PM", o, o + 256)
        terms = dist(X, node("Vb", 0, 1536), "su" + c, 256 * tile, "zr", 2048 * tile + 1024 * ch, None, "sgb")
        if not mx:
            mm([(out, full("idb"), full("kbb"), True, False)])
            diag("PM", o, terms, False, "sf" + c)
        elif tile == 0:
            mm([(out, full("idf"), full("zc" + c), True, False)])
            diag("PM", o, [("U2", X), ("Us", "XA" + c)], False, "sf" + c)
        else:
            z_sum(1, c, ch)
            mm([(out, full("idf"), full("zc" + c), True, False)])
            diag("PM", o, [("U2", X)], False)
        acp(full(["Ks", "K1"][tile] + c), out)

    def child_pass(t, c, ch, so, hi, bank, o):
        tag[0] = "k%d%s" % (t, c)
        mx = BYMAX["e%d" % t]
        for k0, k1 in KC[t]:
            part[0] = k0 // 4
            acp(rows("XA" + c, k0, k1), ind(node("CH", 0, hi), cols("su" + c, so + 16 * k0, so + 16 * k1)))
        Y = psl(bank, o, o + 256)
        diag(bank, o, [("Ue" if mx else "Ua", "XA" + c)], True)
        if mx:
            ts(full("M2" + c), Y, -32.0, None, A.add)
            ts(full("M2" + c), full("M2" + c), 4095, None, A.bitwise_and)
            cp(full("eu" + c), full("M2" + c))
        else:
            ts(full("eu" + c), Y, -32.0, None, A.add)
        lin(full("ef" + c), Y, 1.0, 4064.0 if mx else 4064.0 - 512.0 * K)
        if t == 1 and BYMAX["s1"]:
            E = spare()
            mm([(cols(E, 0, 256), full("idf"), full("K1" + c), True, False)])
            diag(E, 0, [("Us", "XA" + c)], False, "sf" + c)
            acp(full("K1" + c), cols(E, 0, 256))

    for ch, c in halves:
        s_in(0, c, ch)
        z_in(0, ch)
        z_sum(0, c, ch)
        child_pass(0, c, ch, 0, 1536, "PX" + c, 256)
        s_pass(0, c, ch, "XZ" + c)
    for ch, c in halves:
        s_in(1, c, ch)
        z_in(1, ch)

    tag[0] = "const"
    iota(cols("IO", 0, 1552), [[1, 1552]], -16, 0)
    iota(node("IO", 1536, 4096), [[1, 2560]], 1536, 0)
    iota(node("Vb", 2048, 3072), [[0, 1024]], 0, 0)
    ms(cols("Vb", 0, 16), 200.0)
    iota(cols("it2", 0, 256), [[2048, 4], [8192, 4], [0, 16]], 0, 0)
    iota(full("xl"), [[1, 8], [8, 2]], 0, 0)
    iota(full("gid"), [[16, 64]], int(-512 * K) + 4096 + 3072, 0)
    iota(node("CH", 1536, 4096), [[0, 2560]], 126, 0)
    iota(cols("Qt", 2048, 3072), [[0, 1024]], 0, 0)
    for ch, c in halves:
        acp(psl("PY" + c, 256, 512), cols("it2", 0, 256))
    ts(IB, P16, -2048.0, 2.0 ** -18, A.add, A.mult)
    ts(TMP, ci(6), 16.0, None, A.mult)
    ts(T16, ci(7), 64.0, TMP, A.mult, A.add)
    ts(S15, T7, 15.0, None, A.add)
    ts(OWN, P16, 160.0, 1536.0, A.mult, A.add)
    ts(full("gid"), full("gid"), P16, None, A.add)
    ts(full("SL"), x144, S15, None, A.is_equal)
    cp(full("OE"), cols("xi", 0, 16))
    ts(full("OL"), full("xl"), T16, None, A.add)
    ts(full("of"), full("xi"), OWN, None, A.add)
    cp(full("ob"), full("of"))
    acp(full("oh"), full("ob"))
    lin(full("o32"), full("of"), 1.0, 32.0)
    tt(full("orr"), full("o32"), full("ob"), A.subtract)
    for row, x in enumerate(["of", "oh", "orr"]):
        dma(ap("CH", S(row, 128, 16), S(1552, 4112)), full(x), 81920)
    cp(full("bsf"), full("bsc"))
    dma(ap("Bt", S(0, 128, 16), AL), full("bsf"), 49152)
    cp(full("bh"), full("bsc"))
    tt(full("bl"), full("bsc"), full("bh"), A.subtract)
    dma(ap("sga", S(0, 8), S(0, 96), AL), full("bh"), 24576)
    dma(ap("sga", S(8, 16), S(0, 96), AL), full("bl"), 24576)
    it = []
    for r in range(16):
        v = 3 * r + 1
        for j, n in [(0, 2)] if v % 16 < 15 else [(0, 1), (1, 1)]:
            it.append((cols("PE2", j, 64, 3 - n), ap("SL", S(0, 16), S(15 - r, 143 - r)),
                       ap("sga", S(0, 16), S((v + j) // 16, 96, 3), S((v + j) % 16, (v + j) % 16 + n)), r == 0, r == 15))
    mm(it)
    for j in range(2):
        off = cols("iu", 32 * j, 32 * j + 32)
        ts(off, cols("PE2", j, 64, 2), 16.0, None, A.add)
        lin(full("t2"), ind(cols("IO", 0, 1552), off), 2.0 ** -18, IB)
        tt(cols("VB", 1 + j, 1536, 3), ind(cols("Vb", 0, 1552), off), full("t2"), A.add)
    s4, pk = cols("it2", 0, 256), cols("it2", 256, 512)
    ts(s4, cols("sni", 770, 1536, 3), 4096.0, None, A.mult)
    tt(cols("YS", 2, 768, 3), s4, cols("sni", 2, 768, 3), A.add)

    def s_out(tile):
        tag[0] = "o%d" % tile
        ts(s4, full("Ma"), 4096.0, None, A.mult)
        tt(pk, s4, full("Mb"), A.add)
        acp(s4, ind(pk, full("OL")))
        tp(full("pY"), s4)
        y0, y1 = ap("pY", AL, AL, 0, AL), ap("pY", AL, AL, 1, AL)
        mm([(cols("PM", 0, 128), P00, y0, True, False), (cols("PM", 0, 128), P10, y1, False, True),
            (cols("PM", 128, 256), Pa, y0, True, False), (cols("PM", 128, 256), Pb, y1, False, True)])
        acp(cols("YS", tile, 768, 3), cols("PM", 0, 256))

    def children(t, c, ch):
        tag[0] = "x%d%s" % (t, c)
        new0 = 1536 + 512 * t + 256 * ch
        terms = []
        if t == 0 and BYMAX["s1"]:
            terms.append(("Wa", cols("va" + c, 0, 256)))
        if t < 2 and BYMAX["e%d" % (t + 1)]:
            terms.append(("Wn", node("Vb", new0, new0 + 256)))
        sc = cols("SC", 256 * ch, 256 * ch + 256)
        if terms:
            x2 = cols("PX" + c, 256, 512)
            mm([(x2, full(w), x, j == 0, j == len(terms) - 1) for j, (w, x) in enumerate(terms)])
            tt(sc, x2, sc, A.add)
        for m in range(15, -1, -1):
            o = 256 * ch + 16 * m
            put(ind(cols("CH", 0, 16 + PARENTS[t]), cols("au" + c, 32 + 2 * m, 33 + 2 * m)), cols("SC", o, o + 16))

    for t in range(3):
        tile = TILE[t]
        new0 = 1536 + 512 * t
        late = t < 2 and BYMAX["e%d" % (t + 1)]
        for ch, c in halves:
            X, Y = "PX" + c, "PY" + c
            zo = 2048 * tile + 1024 * ch
            tag[0] = "e%d%s" % (t, c)
            mx = BYMAX["e%d" % t]
            if mx:
                mm([(cols(X, 0, 256), full("idf"), full("zc" + c), True, False)])
            else:
                mm([(cols(X, 0, 256), full("idb"), full("kbb"), True, False)])
            terms = dist("XE" + c, node("Vb", 0, [1536, 2048, 3584][t]), "eu" + c, 0, "zr", zo, None, "XA" + c)
            diag(X, 0, terms, False, "ef" + c)
            if t == 0:
                s_pass(1, c, ch, "XS")
            else:
                tag[0] = "g%d%s" % (t, c)
                gv = cols("GV%d" % (t - 1), 256 * ch, 256 * ch + 256)
                E = spare()
                yh = cols(E, 0, 256)
                mm([(yh, full("idb"), gv, True, False), (yh, full("nid"), cols("zr", zo, zo + 256), False, True)])
                act(cols("nt" + c, 0, 256), yh, F.Abs)
                go = 32 * (t - 1) + 16 * ch
                g16 = cols(E, 256, 272)
                mm([(g16, full("idf"), cols("gid", go, go + 16), True, False)] +
                   [(g16, Ur("U", r), cols("nt" + c, r, 256, 16), False, r == 15) for r in range(16)])
                acp(cols("tf" + c, 0, 16), g16)
                acp(full("t1" + c), ind(cols("tf" + c, 0, 16), full("OB")))
        for ch, c in halves:
            X, Y = "PX" + c, "PY" + c
            yl = psl(Y, 0, 256)
            tag[0] = "c%d%s" % (t, c)
            tt(full("M" + c), cols(X, 0, 256), full(["Ks", "K1", "Mc"][t] + c), A.min)
            last = "M" + c
            if t > 0:
                f1, f2 = "f1" + c, "f2" + c
                ts(full("M2" + c), full("M" + c), -32768, None, A.bitwise_and)
                tt(full(f1), full("M2" + c), psl(Y, 256, 512), A.subtract)
                mm([(yl, full("idf"), full("t1" + c), True, False), (yl, full("idb"), full("kbb"), False, False)])
                tt(cols(f2, 0, 128), cols(f1, 0, 128), cols(f1, 128, 256), A.max)
                tt(cols(f2, 128, 192), cols(f2, 0, 64), cols(f2, 64, 128), A.max)
                tt(cols(f2, 192, 224), cols(f2, 128, 160), cols(f2, 160, 192), A.max)
                tt(cols("tf" + c, 16, 32), cols(f2, 192, 208), cols(f2, 208, 224), A.max)
                tt(cols("nt" + c, 0, 256), ind(cols("tf" + c, 16, 32), full("OB")), full(f1), A.is_gt)
                mm([(yl, full("idB"), cols("nt" + c, 0, 256), False, True)])
                tt(full("M2" + c), yl, full("M" + c), A.min)
                last = "M2" + c
            L1, L2, L3 = ["%s%s" % (x, c) for x in ("L1", "L2", "L3")]
            tt(full(L1), cols(last, 0, 128), cols(last, 128, 256), A.min)
            tt(full(L2), cols(L1, 0, 64), cols(L1, 64, 128), A.min)
            ts(full(L2), full(L2), -28673, None, A.bitwise_and)
            tt(cols(L3, 0, 64), full(L2), psl(Y, 256, 320), A.add)
            tt(cols(L3, 64, 96), cols(L3, 0, 32), cols(L3, 32, 64), A.min)
            tt(cols("ti" + c, 0, 16), cols(L3, 64, 80), cols(L3, 80, 96), A.min)
            a32 = cols("ti" + c, 16, 32)
            ts(a32, cols("ti" + c, 0, 16), 4095, None, A.bitwise_and)
            au, a2u = cols("au" + c, 0, 16), cols("au" + c, 16, 32)
            cp(au, a32)
            ts(cols("nt" + c, 256, 512), full(last), (200.0 - 512.0) * K, None, A.is_ge)
            far = cols(spare() if "k" in OWNB else X, 256, 272)
            mm([(far, full("idb"), cols("nt" + c, 256 + 16 * k, 272 + 16 * k), k == 0, k == 15) for k in range(16)])
            dd, a2f, w1, w2 = [cols("tf" + c, 16 * j, 16 * j + 16) for j in range(2, 6)]
            act(dd, far, F.Relu, 8192.0, -8192.0, alt=("ts", dd, far, 0.5, 8192.0, A.is_lt, A.mult))
            tt(a2f, a32, dd, A.subtract)
            ts(a2u, a2f, 16.0, 15.0, A.add, A.max)
            tag[0] = "q%d%s" % (t, c)
            qa = ("qn%d" % t, 256 * ch) if t < 2 else ("ef" + c, 0)
            acp(cols(qa[0], qa[1], qa[1] + 256), ind(cols("Qt", 0, PARENTS[t]), au))
            cp(full("qu" + c), k2l(qa, c))
            tag[0] = "l%d%s" % (t, c)
            va = cols("va" + c, 0, 256)
            acp(va, ind(node("Vb", 0, PARENTS[t]), au))
            gcp(cols("va" + c, 256, 512), va)
            gcp(cols("va" + c, 512, 1024), cols("va" + c, 0, 512))
            t1 = cols("lo" + c, 0, 256)
            lin(t1, ind(node("IO", 0, PARENTS[t]), au), 2.0 ** -18, IB)
            x2 = cols(spare() if "v" in OWNB else X, 256, 512)
            mm([(x2, full("idb"), t1, True, False), (x2, full("idb"), va, False, True)])
            acp(cols("vf" + c, 0, 256), x2)
            gcp(cols("vf" + c, 256, 512), cols("vf" + c, 0, 256))
            gcp(cols("vf" + c, 512, 1024), cols("vf" + c, 0, 512))
            bt = cols("Bt", 768 * ch + tile, 768 * ch + 768, 3)
            acp(bt, ind(cols("IO", 0, 16 + PARENTS[t]), a2u))
            tt(cols("VB", 768 * ch + tile, 768 * ch + 768, 3), ind(cols("Vb", 0, 16 + PARENTS[t]), a2u), t1, A.add)
            tag[0] = "d%d%s" % (t, c)
            eq = cols("nt" + c, 0, 256)
            tt(eq, ind(a2f, full("OE")), bt, A.is_equal)
            dup = cols("PM" if str(t) in OWNB else spare() if "d" in OWNB else X, 256, 272)
            mm([(dup, cols("Wt", 128 * r, 128 * r + 128), cols("nt" + c, r, 256, 16), r == 0, r == 15) for r in range(16)])
            tt(w2, a2f, dup, A.subtract)
            ts(cols("au" + c, 32, 64, 2), w2, 16.0, P16, A.add, A.max)
            if t == 1:
                ts(full("Mc" + c), full(last), -4097, None, A.bitwise_and)
            ts(full("M" + c), full(last), 4095, None, A.bitwise_and)
            if t == 1:
                cp(cols("su" + c, 0, 256), full("M" + c))
        for ch, c in halves:
            X = "PX" + c
            va = cols("va" + c, 0, 256)
            tag[0] = "z%d%s" % (t, c)
            diag(X, 0, dist("XZ" + c, full("Zb"), "qu" + c, 0, "va" + c, 0, "XA" + c, "XA" + c), True, None,
                 lambda a, b: lin(cols("f2" + c, a, b), cols(X, a, b), -1.0 / K / K, (FAR + 0.5) / K))
            act(cols("lo" + c, 0, 256), va, F.Relu, -2.0, alt=("ts", cols("lo" + c, 0, 256), va, -2.0, 0.0, A.add, A.max))
            ts(cols("lo" + c, 256, 512), va, 2.0, 63.0, A.add, A.min)
        tag[0] = "x%d" % t
        gcp(full("SC"), node("CH", new0, new0 + 512))
        if not late:
            for ch, c in halves:
                children(t, c, ch)
        tag[0] = "x%d" % t
        if t < 2:
            qn = full("qn%d" % t)
            remote(full("GQ%d" % t), qn, 262144, HOPS[t], 3 * t + 2)
            dma(cols("Qt", new0, new0 + 512), qn, 262144)
            dma(cols("Qt", 3072 + 512 * t, 3584 + 512 * t), full("GQ%d" % t), 262144)
        if t == 0:
            s_out(0)
        if t == 2:
            s_out(1)
            dma(ap("ys", AL), full("YS"), 393216)
            dma(full("Ksa"), ap("CH", S(0, 128, 16), S(16, 4112)), 131072)
            cp(full("Mca"), full("Ksa"))
            cp(full("Ksb"), full("Mca"))
            dma(ap("yk", AL), full("Ksb"), 131072)
            dma(ap("yb", AL), ap("Bt", S(0, 128, 16), AL), 49152)
        for ch, c in halves:
            X, Y = "PX" + c, "PY" + c
            tag[0] = "b%d%s" % (t, c)
            dist("XE" + c, full("VB"), "qu" + c, 0, "vf" + c, 0)
            tag[0] = "h%d%s" % (t, c)
            nat = lambda a, b: cols("nt" + c, 512 + a, 512 + b)
            H = cols(X, 0, 256)
            mult = MULT.get(tag[0], ())
            mm([(H, full("idb"), cols("va" + c, 0, 256), True, False)])
            for kg in range(4):
                part[0] = kg
                for k0, k1 in KH:
                    if k0 // 4 != kg:
                        continue
                    a0, a1 = 16 * k0, 16 * k1
                    y = psl(Y, a0, a1)
                    mm([(y, Ur("U", r), cols("XE" + c, 256 * k0 + r, 256 * k1, 16), r == 0, r == 15) for r in range(16)])
                    act(cols("t1" + c, a0, a1), y, F.Abs, -FAR / K, 1.0 / K / K)
                    tt(y, y, cols("t1" + c, a0, a1), A.min)
                    tt(nat(a0, a1), y, cols("f2" + c, a0, a1), A.is_lt if kg in mult else A.is_ge)
                way = WAYS.get("z%d%s" % (t, c), "vvvv")[kg]
                sgn = "nid" if way in "dr" else "idb"
                if kg in mult:
                    assert way != "p"
                    for hf in range(2):
                        E = spare()
                        mm([(cols(E, 64 * j, 64 * j + 64), cols("Wb", 128 * r, 128 * r + 128), nat(64 * kg, 64 * kg + 64), True, True)
                            for j, r in enumerate(range(8 * hf, 8 * hf + 8))])
                        for j, r in enumerate(range(8 * hf, 8 * hf + 8)):
                            tt(rows("sg" + c, 4 * kg, 4 * kg + 4, r), rows("XZ" + c, 4 * kg, 4 * kg + 4, r), cols(E, 64 * j, 64 * j + 64), A.mult)
                    for k in range(4 * kg, 4 * kg + 4, 2):
                        so = rows("sg" + c, k, k + 2)
                        o = act(so, so, F.Sign, alt=("ts", so, so, 1.0, -1.0, A.min, A.max))
                        o["alts"] = {"v": o["alts"]["v"], "a": o["alts"]["a"]}
                        mm([(H, full(sgn), rows("sg" + c, j, j + 1), False, j == 15) for j in (k, k + 1)])
                    continue
                plain = [k for k in range(4) if k not in mult]
                if kg == plain[-1]:
                    c64 = psl(Y, 0, 64)
                    mm([(c64, full("idb"), nat(64 * k, 64 * k + 64), k == plain[0], k == kg) for k in plain])
                    cn = cols("nt" + c, 0, 16)
                    lin(cols("nt" + c, 64, 128), c64, -1.0 / 128, 0.0)
                    tt(cols("nt" + c, 32, 64), cols("nt" + c, 64, 96), cols("nt" + c, 96, 128), A.add)
                    tt(cn, cols("nt" + c, 32, 48), cols("nt" + c, 48, 64), A.add)
                    mm([(cols(X, r, 256, 16), cols("Wb", 128 * r, 128 * r + 128), cn, False, False) for r in range(16)])
                for hf in range(2):
                    E = spare()
                    it = []
                    for j in range(8):
                        r = 8 * hf + j
                        it += [(cols(E, j, 512, 8), full(sgn), cols("XZ" + c, 1024 * kg + r, 1024 * kg + 1024, 16), True, False)]
                        if way == "p":
                            it += [(cols(E, j, 512, 8), full("nid"), cols("va" + c, r, 1024, 16), False, False)]
                        it += [(cols(E, j, 512, 8), cols("Wb", 128 * r, 128 * r + 128), nat(64 * kg, 64 * kg + 64), False, True)]
                    mm(it)
                    so = ap("sg" + c, AL, S(64 * kg, 64 * kg + 64), S(8 * hf, 8 * hf + 8))
                    act(so, full(E), F.Sign, alt=("ts", so, full(E), 1.0, -1.0, A.min, A.max))
                pair = PAIR.get(tag[0], ())
                if kg + 1 in pair:
                    continue
                k0 = 4 * kg
                if kg in pair:
                    k0 -= 4
                    dadd(rows("sg" + c, k0, k0 + 4), rows("sg" + c, k0 + 4, k0 + 8), 262144)
                mm([(H, full("idb"), rows("sg" + c, k, k + 1), False, kg == 3 and k == k0 + 3) for k in range(k0, k0 + 4)])
            part[0] = None
            tt(H, H, cols("lo" + c, 0, 256), A.max)
            nv = node("Vb", new0 + 256 * ch, new0 + 256 * ch + 256)
            tt(nv, H, cols("lo" + c, 256, 512), A.min)
            if t == 2:
                dma(ap("yv", AL, S(1024 + 256 * ch, 1280 + 256 * ch)), nv, 65536)
            else:
                remote(cols("GV%d" % t, 256 * ch, 256 * ch + 256), nv, 65536, HOPS[t], 3 * t + ch)
            if late:
                children(t, c, ch)
        if t < 2:
            tag[0] = "y%d" % t
            nv = node("Vb", new0, new0 + 512)
            dma(ap("yv", AL, S(512 * t, 512 * t + 512)), nv, 131072)
            dma(node("Vb", 3072 + 512 * t, 3584 + 512 * t), full("GV%d" % t), 131072)
            for ch, c in halves:
                child_pass(t + 1, c, ch, 256 * (1 - t), [2048, 4096][t], "PM", 256 * ch)
    assert nd[0] <= NDMA
    return ops


def depend(ops):
    hist = {}
    for o in ops:
        d = {}
        for acc, w in [(x, False) for x in o["rd"]] + [(x, True) for x in o["wr"]]:
            m = _mask(acc)[0]
            ps = _chain(acc)
            row = _row(acc)
            for (n, hm, hw, hr) in hist.get(acc[0], []):
                if n == o["n"] or (row is not None and hr is not None and not (row & hr)):
                    continue
                if (hm & m) and (w or hw):
                    d[n] = True
                elif ps:
                    d.setdefault(n, False)
        o["deps"] = d
        for acc, w in [(x, False) for x in o["rd"]] + [(x, True) for x in o["wr"]]:
            m = _mask(acc)[0]
            h = hist.setdefault(acc[0], [])
            if w and not _chain(acc) and acc[1][0] == slice(None):
                h[:] = [(n, hm & ~m, hw, hr) for (n, hm, hw, hr) in h if hm & ~m]
            if _chain(acc):
                h[:] = [x for x in h if x[0] != o["n"]][-3:]
                m = (1 << 512) - 1
                w = True
            h.append((o["n"], m, w, _row(acc)))


def _row(x):
    p = x[1][0]
    return None if p == slice(None) else set(range(128)[p])


def _chain(x):
    return _psum(x)


def _times(o, e, C):
    kind, n = o["alts"][e][1]
    if kind == "dma":
        return (60.0 if e != "g" else C["issue"]), C["dma"] + n / C["rate"]
    if kind == "pe":
        t = n * C["pe"]
    elif kind == "cyc":
        t = max(n, 64) * C["cyc"]
    else:
        t = (50.0 if e == "v" else 65.0) * C["cyc"] / 0.83 + n * C[kind] * C["cyc"]
    return t, t


def length(ops, order, C):
    free, end = dict((e, 0.0) for e in "vapgs"), [0.0] * len(ops)
    for n in order:
        e = ops[n]["e"]
        st = max([free[e]] + [end[d] + (0.0 if e == "p" == ops[d]["e"] else C["lat"]) for d in ops[n]["deps"]])
        busy, done = _times(ops[n], e, C)
        free[e], end[n] = st + busy, st + done
    return max(end)


def climb(ops, C):
    tags = sorted(set(o["tag"] for o in ops))
    tables = [dict(BIAS), dict(BIAS)]
    best, seed = None, C["seed"]
    for it in range(C["shifts"] + 1):
        seed = (seed * 6364136223846793005 + 1442695040888963407) % 2 ** 64
        new = [dict(x) for x in tables]
        if it:
            x, k = new[(seed >> 50) % 5 < 3], tags[(seed >> 30) % len(tags)]
            x[k] = x.get(k, 0) + [-10, -4, -2, -1, 1, 2, 4, 10][seed >> 20 & 7]
        order = schedule(ops, C, *new)
        c = sum(length(ops, order, dict(C, **f)) / f["gat"] ** 0.5 for f in SPREAD)
        if best is None or c <= best:
            best, tables = c, new
    return schedule(ops, C, *tables)


def schedule(ops, C, first=None, second=None):
    succ = [[] for _ in ops]
    for o in ops:
        for d in o["deps"]:
            succ[d].append(o["n"])
    prio = [0.0] * len(ops)
    for o in reversed(ops):
        e = list(o["alts"])[0]
        prio[o["n"]] = _times(o, e, C)[1] + C["lat"] + max([prio[s] for s in succ[o["n"]]] or [0.0])
    def urgent(prio, table):
        prio = [p + 1000.0 * table.get(o["tag"], 0) for p, o in zip(prio, ops)]
        for o in reversed(ops):
            prio[o["n"]] = max([prio[o["n"]]] + [prio[s] + 1.0 for s in succ[o["n"]]])
        return prio

    forward(ops, C, succ, urgent(prio, first or BIAS))
    return forward(ops, C, succ, urgent(backward(ops, C, succ), second or BIAS))


def backward(ops, C, succ):
    tm = [_times(o, o["e"], C) for o in ops]
    left = [len(s) for s in succ]
    ready = [t[1] - t[0] for t in tm]
    avail = [o["n"] for o in ops if not succ[o["n"]]]
    free = dict((e, 0.0) for e in "vapgs")
    out = [0.0] * len(ops)
    while avail:
        n = min(avail, key=lambda k: (max(free[ops[k]["e"]], ready[k]), -ops[k]["t0"] - tm[k][0]))
        e = ops[n]["e"]
        end = max(free[e], ready[n]) + tm[n][0]
        free[e] = out[n] = end
        avail.remove(n)
        for d in ops[n]["deps"]:
            lag = 0.0 if (e == "p" and ops[d]["e"] == "p") else tm[d][1] - tm[d][0] + C["lat"]
            ready[d] = max(ready[d], end + lag)
            left[d] -= 1
            if left[d] == 0:
                avail.append(d)
    return out


def forward(ops, C, succ, prio):
    left = [len(o["deps"]) for o in ops]
    ready_at = [0.0] * len(ops)
    avail = [o["n"] for o in ops if not o["deps"]]
    free = dict((e, 0.0) for e in "vapgs")
    order = []
    while avail:
        cand = []
        for n in avail:
            alts = list(ops[n]["alts"])
            for j, e in enumerate(alts):
                st = max(free[e], ready_at[n])
                if j == 0 or free[alts[0]] > st + C["alt"]:
                    cand.append((st, j, n, e))
        t0, _, _, e = min(cand)
        st, _, n, _ = max((x for x in cand if x[3] == e and x[0] <= t0 + C["look"]), key=lambda x: (-x[1], prio[x[2]]))
        o = ops[n]
        busy, done = _times(o, e, C)
        o["e"], o["t0"], o["t1"] = e, st, st + done
        free[e] = st + busy
        avail.remove(n)
        order.append(n)
        for s in succ[n]:
            pe_pair = e == "p" and "p" in ops[s]["alts"]
            ready_at[s] = max(ready_at[s], st + (busy if pe_pair else done + C["lat"]))
            left[s] -= 1
            if left[s] == 0:
                avail.append(s)
    return order


def polish(ops, order, C):
    n = len(ops)
    anc, pre, suc = [0] * n, [], [[] for _ in ops]
    for o in ops:
        keep, cov = [], 0
        for d in sorted(o["deps"], reverse=True):
            if not (cov >> d) & 1:
                keep.append(d)
                suc[d].append(o["n"])
            cov |= anc[d] | (1 << d)
        anc[o["n"]] = cov
        pre.append(keep)
    figs = [dict(C, **x) for x in SPREAD]
    names = "vapgs"
    tm = [[dict((names.index(e), _times(o, e, f)) for e in o["alts"]) for o in ops] for f in figs]
    eng = [names.index(o["e"]) for o in ops]
    STEP = 32

    def run(order, eng, j, first, old):
        t, lat = tm[j], figs[j]["lat"]
        k = first // STEP
        end, marks = list(old[0]), old[1][:k + 1]
        free = list(marks[k])
        for a in range(k * STEP, n, STEP):
            if a > k * STEP:
                marks.append(tuple(free))
            for v in order[a:a + STEP]:
                e = eng[v]
                st = free[e]
                if e == 2:
                    for d in pre[v]:
                        x = end[d] if eng[d] == 2 else end[d] + lat
                        if x > st:
                            st = x
                else:
                    st -= lat
                    for d in pre[v]:
                        if end[d] > st:
                            st = end[d]
                    st += lat
                b, dn = t[v][e]
                free[e] = st + b
                end[v] = st + dn
        return end, marks

    def longest(order, eng, j, end):
        t, lat = tm[j], figs[j]["lat"]
        before, last = [-1] * n, [-1] * 5
        for v in order:
            before[v] = last[eng[v]]
            last[eng[v]] = v
        v, way = end.index(max(end)), []
        while v >= 0:
            way.append(v)
            st = end[v] - t[v][eng[v]][1]
            w = [d for d in pre[v] if end[d] + (0.0 if eng[d] == 2 == eng[v] else lat) > st - 0.01]
            v = w[0] if w else before[v]
        return way

    state = [run(order, eng, j, 0, ([0.0] * n, [(0.0,) * 5])) for j in range(len(figs))]
    base = [max(s[0]) for s in state]
    cur = 1.0
    best = (cur, order, eng)
    parts = {}
    for o in ops:
        parts.setdefault((o["tag"], o["q"]), []).append(o["n"])
    kin = [parts[(o["tag"], o["q"])] for o in ops]
    seed = C["seed"]
    way = None
    for it in range(C["tries"]):
        seed = (seed * 6364136223846793005 + 1442695040888963407) % 2 ** 64
        r0, r1, r2, r3 = [(seed >> s & 4095) / 4096.0 for s in (52, 40, 28, 16)]
        if way is None:
            j = it % len(figs)
            way = longest(order, eng, j, state[j][0])
            pos = [0] * n
            for p, v in enumerate(order):
                pos[v] = p
        v = way[int(r0 * len(way))]
        p, e, k = pos[v], eng[v], [1, 1, 1, 2, 3, 5, 8][int(r2 * 7)]
        new, neng, q = order, eng, p
        if r1 > 1.0 - C["whole"]:
            k = [3, 6, 12, 24, 48][int(r2 * 5)]
            new, at = list(order), list(pos)
            mine = sorted(kin[v], key=lambda x: pos[x])
            if seed >> 8 & 1:
                for x in mine:
                    a = at[x]
                    b = max([a - k] + [at[d] + 1 for d in pre[x]] + [0])
                    new[b:a + 1] = [x] + new[b:a]
                    for y in range(b, a + 1):
                        at[new[y]] = y
                    q = min(q, b)
            else:
                for x in reversed(mine):
                    a = at[x]
                    b = min([a + k] + [at[s] - 1 for s in suc[x]] + [n - 1])
                    new[a:b + 1] = new[a + 1:b + 1] + [x]
                    for y in range(a, b + 1):
                        at[new[y]] = y
                q = pos[mine[0]]
        elif r1 < 0.2:
            if len(tm[0][v]) < 2:
                continue
            neng = list(eng)
            neng[v] = sum(tm[0][v]) - e
        elif r1 < 0.65:
            lo = max([pos[d] for d in pre[v]] or [-1]) + 1
            while q > lo and k:
                q -= 1
                k -= eng[order[q]] == e
            if q == p:
                continue
            new = order[:q] + [v] + order[q:p] + order[p + 1:]
        else:
            hi = min([pos[s] for s in suc[v]] or [n]) - 1
            while q < hi and k:
                q += 1
                k -= eng[order[q]] == e
            if q == p:
                continue
            new = order[:p] + order[p + 1:q + 1] + [v] + order[q + 1:]
        trial = [run(new, neng, j, min(p, q), state[j]) for j in range(len(figs))]
        c = sum(max(s[0]) / b for s, b in zip(trial, base)) / len(figs)
        if c <= cur or r3 < math.exp((cur - c) / (C["heat"] * (1.0 - it / C["tries"]) + 1e-5)):
            order, eng, cur, state, way = new, neng, c, trial, None
            if c < best[0]:
                best = (c, order, eng)
    for o in ops:
        o["e"] = names[best[2][o["n"]]]
    return best[1]


def plan():
    ops = build()
    depend(ops)
    order = polish(ops, climb(ops, COST), COST)
    needs = [False] * len(ops)
    for o in ops:
        for d, hard in o["deps"].items():
            same = ops[d]["e"] == o["e"] and ops[d]["kind"] == "c" and o["kind"] == "c"
            if not (same and (o["e"] == "p" or not hard)):
                needs[d] = True
    count = dict((e, 0) for e in "vapg")
    know = dict((e, {}) for e in "vapgs")
    for n in order:
        o = ops[n]
        e = o["e"]
        waits = {}
        for d, hard in o["deps"].items():
            p = ops[d]
            same = p["e"] == e and p["kind"] == "c" and o["kind"] == "c"
            if same and (e == "p" or not hard):
                continue
            s, val = p["sig"]
            if know[e].get(s, 0) < val:
                waits[s] = max(waits.get(s, 0), val)
        keep = {}
        for s, val in waits.items():
            covered = False
            for d in o["deps"]:
                p = ops[d]
                if p["sig"] and p["sig"][0] != s and waits.get(p["sig"][0], 0) >= p["sig"][1] and p["vc"].get(s, 0) >= val:
                    covered = True
            if not covered:
                keep[s] = val
        for d in o["deps"]:
            p = ops[d]
            if p["sig"] and max(know[e].get(p["sig"][0], 0), waits.get(p["sig"][0], 0)) >= p["sig"][1]:
                for s, val in p["vc"].items():
                    know[e][s] = max(know[e].get(s, 0), val)
        for s, val in waits.items():
            know[e][s] = max(know[e].get(s, 0), val)
        o["waits"] = keep
        o["vc"] = dict(know[e]) if o["kind"] != "r" else {}
        if o["kind"] != "c":
            o["sig"] = (o["sem"], 16)
        elif needs[n] or e != "p":
            count[e] += 1
            o["sig"] = (e, count[e])
        else:
            o["sig"] = None
    return ops, order, count


_plan = []


def rank_program(g, core, T, topo):
    rank = T.rank_of(core)
    if rank is None:
        return
    if not _plan:
        _plan.append(plan())
    ops, order, count = _plan[0]
    queue = {"v": g.vector, "a": g.scalar, "p": g.tensor, "g": g, "s": g.sync}
    nrank = len(T.cores)

    def X(x):
        if not isinstance(x, tuple):
            return x
        if x[0] == "*":
            return X(x[1]).indirect(X(x[2]))
        return T[x[0]][x[1]]

    sent = 0
    for n in order:
        o = ops[n]
        q = queue[o["e"]]
        for s, val in o["waits"].items():
            q.wait_ge(T.sem[s], val)
        call = o["alts"][o["e"]][0]
        k = call[0]
        if k == "tt":
            i = q.tensor_tensor(X(call[1]), X(call[2]), X(call[3]), call[4])
        elif k == "ts":
            if call[6] is None:
                i = q.tensor_scalar(X(call[1]), X(call[2]), X(call[3]), None, call[5])
            else:
                i = q.tensor_scalar(X(call[1]), X(call[2]), X(call[3]), X(call[4]), call[5], call[6])
        elif k == "cp":
            i = q.tensor_copy(X(call[1]), X(call[2]))
        elif k == "tp":
            i = q.transpose(X(call[1]), X(call[2]))
        elif k == "ms":
            i = q.memset(X(call[1]), call[2])
        elif k == "act":
            if call[1][0] == "*":
                i = q.activation(X(call[1]), X(call[2]), call[3])
            else:
                i = q.activation(X(call[1]), X(call[2]), call[3], X(call[4]), X(call[5]))
        elif k == "mm":
            for out, l, r, st, sp in call[1]:
                i = q.matmul(X(out), X(l), X(r), st, sp)
        elif k == "iota":
            if SCRATCH[call[1][0]][2] == I32:
                i = q.iota(X(call[1]), call[2], call[3], call[4])
            else:
                i = q.iota(X(call[1]), call[2], call[3], call[4], allow_small_or_imprecise_dtypes=True)
        elif k == "sel":
            i = q.affine_select(X(call[1]), X(call[2]), call[3], call[4], 0.0, call[5], call[6])
        elif k == "dma":
            if len(call) > 3:
                i = q.dma_start(X(call[1]), X(call[2]), accum_op=A.add)
            else:
                i = q.dma_start(X(call[1]), X(call[2]))
        else:
            dst = T.cores[(rank + call[3]) % nrank]
            rid, pid, _ = topo.addr(dst)
            assert len(topo.engines(core, dst)) == o["sig"][1]
            q.remote_dma(X(call[1]), X(call[2]), T.sem[o["sem"]], T.sem.sent, pid, rid, topo.mask(core, dst))
            sent += o["sig"][1]
            continue
        if o["sig"]:
            i.then_inc(T.sem[o["sig"][0]], 16 if o["kind"] == "d" else 1)
    for e in "vapg":
        g.wait_ge(T.sem[e], count[e])
    g.wait_ge(T.sem.sent, sent)
    for o in ops:
        if o["kind"] != "c":
            g.wait_ge(T.sem[o["sem"]], 16)
